import numpy as np
import ml_dtypes


def mxq(x, axis, fmt="e4m3"):
    dtype, down = {"e4m3": (ml_dtypes.float8_e4m3fn, 7), "e5m2": (ml_dtypes.float8_e5m2, 14)}[fmt]
    v = np.moveaxis(np.asarray(x, np.float32).astype(ml_dtypes.bfloat16).astype(np.float64), axis, -1)
    blocks = v.reshape(v.shape[:-1] + (-1, 32))
    amax = np.abs(blocks).max(-1, keepdims=True)
    byte = np.maximum(np.where(amax > 0, np.frexp(amax)[1] - 1 + 127, 0) - down, 1)
    scale = np.exp2(byte - 127.0)
    codes = (blocks / scale).astype(np.float32).astype(dtype).astype(np.float64)
    return np.moveaxis((codes * scale).reshape(v.shape), -1, axis)


WIDE = False


def mx_kscale(k):
    if not WIDE:
        return np.ones(k)
    levels = np.array([10, -10, 5, -5, 0])
    if k % 512:
        return np.exp2(np.random.permutation(np.resize(levels, k // 32))).repeat(32)
    a = np.empty((k // 512, 16))
    for p in range(k // 512):
        a[p, :8] = np.random.permutation(np.resize(levels, 8))
        for g in range(8):
            far = levels[np.abs(levels - a[p, g]) >= 10]
            a[p, g + 8] = far[np.random.randint(len(far))]
    return np.exp2(a.ravel()).repeat(32)


def f64(x):
    return np.asarray(x).astype(np.float64)


def striped(idx):
    return np.tile(idx.reshape(-1, 16).T, (8, 1)).astype(np.uint16)


def unstriped(offs):
    return offs[:16].T.reshape(-1).astype(np.int64)


E2M1 = np.array([0.0, 0.5, 1.0, 1.5, 2.0, 3.0, 4.0, 6.0, -0.0, -0.5, -1.0, -1.5, -2.0, -3.0, -4.0, -6.0])


def pack_weight(w, fmt):
    k, n = w.shape
    w = f64(np.asarray(w, np.float32).astype(ml_dtypes.bfloat16)).reshape(k // 32, 32, n)
    amax = np.abs(w).max(1)
    if fmt == "e4m3":
        byte = np.frexp(amax)[1] - 1 + 127 - 7
    else:
        mant, ex = np.frexp(amax / 6.0)
        byte = np.where(mant > 0.5, ex, ex - 1) + 127
    byte = np.clip(np.where(amax > 0, byte, 1), 1, 254)
    scaled = (w * np.exp2(127.0 - byte)[:, None, :]).reshape(k, n).astype(np.float32)
    by_word = np.ascontiguousarray(scaled.reshape(k // 512, 128, 4, n).transpose(0, 1, 3, 2))
    if fmt == "e4m3":
        words = by_word.astype(ml_dtypes.float8_e4m3fn).view(np.uint8)
    else:
        c = by_word.astype(ml_dtypes.float4_e2m1fn).view(np.uint8) & 0xF
        words = (c[..., 0::2] | (c[..., 1::2] << 4)).reshape(k // 512, 128, 2 * n)
    return np.ascontiguousarray(words), np.ascontiguousarray(byte.astype(np.uint8).reshape(k // 512, 16, n))


def unpack_weight(words, scales, fmt):
    g, _, n = scales.shape
    words = np.ascontiguousarray(words).reshape(g, 128, n, -1)
    if fmt == "e4m3":
        vals = words.view(ml_dtypes.float8_e4m3fn).astype(np.float64)
    else:
        nib = np.empty((g, 128, n, 4), np.uint8)
        nib[..., 0::2] = words & 0xF
        nib[..., 1::2] = words >> 4
        vals = E2M1[nib]
    vals = vals * np.repeat(np.exp2(scales.astype(np.float64) - 127.0), 8, axis=1)[..., None]
    return vals.transpose(0, 1, 3, 2).reshape(g * 512, n)


def sigmoid(v):
    return 1.0 / (1.0 + np.exp(-np.maximum(v, -700.0)))


K, T, E, C, H, N, HOT = 512, 512, 8, 256, 512, 256, 2
TOP = 4


def by_expert(wq, xq):
    return np.concatenate([wq[e].T @ xq[:, e * C:(e + 1) * C] for e in range(E)], axis=1)


def setup_inputs():
    n = np.random.standard_normal
    s = mx_kscale(K)
    u = mx_kscale(H)
    deal = np.repeat(np.arange(E), C).reshape(TOP, T)[:, np.random.permutation(T)]
    deal = np.take_along_axis(deal, np.argsort(np.random.rand(TOP, T), axis=0), axis=0)
    for _ in range(8):
        s_, t_ = np.random.permutation(T).reshape(2, -1); r = np.random.randint(TOP, size=T // 2); x, y = deal[r, s_].copy(), deal[r, t_].copy()
        ok = ~((deal[:, s_] == y).any(0) | (deal[:, t_] == x).any(0)); deal[r[ok], s_[ok]] = y[ok]; deal[r[ok], t_[ok]] = x[ok]
    order = np.lexsort((np.random.rand(TOP * T), deal.reshape(-1)))
    slot_token = order % T; pos = np.empty(TOP * T, np.int64); pos[order] = np.arange(TOP * T); pos = pos.reshape(TOP, T)
    g = np.random.uniform(0.5, 1.5, (TOP, T)); g = g / g.sum(0)
    x = pack_weight(n((K, T)) * s[:, None], "e4m3")
    w1h = [pack_weight(m, "e4m3") for m in n((HOT, K, H)) / np.sqrt(K) / s[None, :, None]]
    w3h = [pack_weight(m, "e4m3") for m in n((HOT, K, H)) / np.sqrt(K) / s[None, :, None] * u]
    w2h = [pack_weight(m, "e4m3") for m in n((HOT, H, N)) / np.sqrt(H) / u[None, :, None]]
    w1c = [pack_weight(m, "e2m1") for m in n((E - HOT, K, H)) / np.sqrt(K) / s[None, :, None]]
    w3c = [pack_weight(m, "e2m1") for m in n((E - HOT, K, H)) / np.sqrt(K) / s[None, :, None] * u]
    w2c = [pack_weight(m, "e2m1") for m in n((E - HOT, H, N)) / np.sqrt(H) / u[None, :, None]]
    return {
        "x_words": x[0],
        "x_scales": x[1],
        "w1h_words": np.stack([m[0] for m in w1h]),
        "w1h_scales": np.stack([m[1] for m in w1h]),
        "w3h_words": np.stack([m[0] for m in w3h]),
        "w3h_scales": np.stack([m[1] for m in w3h]),
        "w2h_words": np.stack([m[0] for m in w2h]),
        "w2h_scales": np.stack([m[1] for m in w2h]),
        "w1c_words": np.stack([m[0] for m in w1c]),
        "w1c_scales": np.stack([m[1] for m in w1c]),
        "w3c_words": np.stack([m[0] for m in w3c]),
        "w3c_scales": np.stack([m[1] for m in w3c]),
        "w2c_words": np.stack([m[0] for m in w2c]),
        "w2c_scales": np.stack([m[1] for m in w2c]),
        "gate": np.stack([np.tile(r, (128, 1)) for r in g]).astype(np.float32),
        "offs": striped(slot_token),
        "pos1": striped(pos[0]),
        "pos2": striped(pos[1]),
        "pos3": striped(pos[2]),
        "pos4": striped(pos[3]),
    }


def reference(x_words, x_scales, w1h_words, w1h_scales, w3h_words, w3h_scales, w2h_words, w2h_scales, w1c_words, w1c_scales, w3c_words, w3c_scales, w2c_words, w2c_scales, gate, offs, pos1, pos2, pos3, pos4):
    w1h = np.stack([unpack_weight(w1h_words[e], w1h_scales[e], "e4m3") for e in range(HOT)])
    w3h = np.stack([unpack_weight(w3h_words[e], w3h_scales[e], "e4m3") for e in range(HOT)])
    w2h = np.stack([unpack_weight(w2h_words[e], w2h_scales[e], "e4m3") for e in range(HOT)])
    w1c = np.stack([unpack_weight(w1c_words[e], w1c_scales[e], "e2m1") for e in range(E - HOT)])
    w3c = np.stack([unpack_weight(w3c_words[e], w3c_scales[e], "e2m1") for e in range(E - HOT)])
    w2c = np.stack([unpack_weight(w2c_words[e], w2c_scales[e], "e2m1") for e in range(E - HOT)])
    idx = unstriped(offs)
    xq = unpack_weight(x_words, x_scales, "e4m3")[:, idx]
    w1 = [*w1h, *w1c]
    w3 = [*w3h, *w3c]
    w2 = [*w2h, *w2c]
    h = sigmoid(by_expert(w1, xq)) * by_expert(w3, xq)
    y = by_expert(w2, mxq(h, 0, "e4m3"))
    out = sum(f64(gate[r, :1]) * y[:, unstriped(p)] for r, p in enumerate((pos1, pos2, pos3, pos4)))
    return out

@@ -1,0 +1,192 @@
+from contextlib import ExitStack
+
+import concourse.mybir as mybir
+from concourse.masks import make_identity
+
+K, T, E, C, H, N, HOT, TOP = 512, 512, 8, 256, 512, 256, 2, 4
+S = E * C
+FLOPS = 2 * S * (2 * K * H + H * N)
+
+F32 = mybir.dt.float32
+BF16 = mybir.dt.bfloat16
+I32 = mybir.dt.int32
+U32 = mybir.dt.uint32
+U16 = mybir.dt.uint16
+U8 = mybir.dt.uint8
+FP8X4 = mybir.dt.float8_e4m3fn_x4
+FP4X4 = mybir.dt.float4_e2m1fn_x4
+MULT = mybir.AluOpType.mult
+ADD = mybir.AluOpType.add
+SIGMOID = mybir.ActivationFunctionType.Sigmoid
+
+P = 128
+
+
+def tile_moe_hot_glu_sigmoid_kernel(
+    tc, x_words, x_scales, w1h_words, w1h_scales, w3h_words, w3h_scales, w2h_words, w2h_scales,
+    w1c_words, w1c_scales, w3c_words, w3c_scales, w2c_words, w2c_scales, gate, offs, pos1, pos2, pos3, pos4, out,
+):
+    nc = tc.nc
+    COLD = E - HOT
+    with ExitStack() as ctx:
+        keep = ctx.enter_context(tc.tile_pool(name="keep", bufs=1))
+        ring = ctx.enter_context(tc.tile_pool(name="ring", bufs=3))
+        psum = ctx.enter_context(tc.psum_pool(name="psum", bufs=1))
+
+        def plane_tile(name, experts, width, engine):
+            plane = keep.tile([P, experts, width], U8, name=name, align_bytes=64)
+            engine.memset(plane[:].bitcast(I32), 0)
+            return plane
+
+        def load_plane(plane, scales):
+            rows = scales.rearrange("f (q r) c -> r q f c", r=4)
+            for r in range(4):
+                nc.sync.dma_start(out=plane[r:P:32, :, :].bitcast(I32), in_=rows[r].bitcast(I32))
+
+        def load_words(name, words):
+            tile = keep.tile(list(words.shape), U8, name=name, align_bytes=64)
+            nc.sync.dma_start(out=tile[:].bitcast(I32), in_=words.bitcast(I32))
+            return tile
+
+        def cold_words(words, a, b):
+            return words[a:b, 0].rearrange("f p c -> p f c")
+
+        def hot_words(words):
+            return words[:, 0].rearrange("f p n t -> p f (n t)")
+
+        xs = keep.tile([P, T], U8, name="xs", align_bytes=64)
+        nc.vector.memset(xs[:].bitcast(I32), 0)
+        s1c = plane_tile("s1c", COLD, H, nc.vector)
+        s3c = plane_tile("s3c", COLD, H, nc.gpsimd)
+        s2c = plane_tile("s2c", COLD, N, nc.vector)
+        s1h = plane_tile("s1h", HOT, H, nc.gpsimd)
+        s3h = plane_tile("s3h", HOT, H, nc.vector)
+        s2h = plane_tile("s2h", HOT, N, nc.gpsimd)
+        ident = keep.tile([P, P], F32, name="ident")
+        make_identity(nc, ident[:])
+
+        offs_t = keep.tile([P, S // 16], U16, name="offs_t")
+        nc.sync.dma_start(offs_t[:], offs)
+        xw = keep.tile([P, T], I32, name="xw", align_bytes=64)
+        nc.sync.dma_start(out=xw[:], in_=x_words[0].rearrange("p t d -> p (t d)").bitcast(I32))
+        x_rows = x_scales[0].rearrange("(q r) c -> r q c", r=4)
+        for r in range(4):
+            nc.sync.dma_start(out=xs[r:P:32, :].bitcast(I32), in_=x_rows[r].bitcast(I32))
+
+        groups = [(0, 1), (1, 3), (3, 6)]
+        w1t, w3t = {}, {}
+
+        def load_cold(g):
+            a, b = groups[g]
+            t1 = load_words(f"w1c{g}", cold_words(w1c_words, a, b))
+            t3 = load_words(f"w3c{g}", cold_words(w3c_words, a, b))
+            for f in range(a, b):
+                w1t[HOT + f] = (t1[:, f - a, :].bitcast(FP4X4), s1c[:, f, :])
+                w3t[HOT + f] = (t3[:, f - a, :].bitcast(FP4X4), s3c[:, f, :])
+
+        load_cold(0)
+        load_plane(s1c, w1c_scales[:, 0])
+        load_plane(s3c, w3c_scales[:, 0])
+        load_cold(1)
+        w2c = load_words("w2c", cold_words(w2c_words, 0, COLD))
+        load_plane(s2c, w2c_scales[:, 0])
+        load_cold(2)
+        load_plane(s1h, w1h_scales[:, 0])
+        load_plane(s3h, w3h_scales[:, 0])
+        load_plane(s2h, w2h_scales[:, 0])
+        w1h = load_words("w1h", hot_words(w1h_words))
+        w3h = load_words("w3h", hot_words(w3h_words))
+        w2h = load_words("w2h", hot_words(w2h_words))
+        for f in range(HOT):
+            w1t[f] = (w1h[:, f, :].bitcast(FP8X4), s1h[:, f, :])
+            w3t[f] = (w3h[:, f, :].bitcast(FP8X4), s3h[:, f, :])
+
+        def w2_block(e, b):
+            if e < HOT:
+                return w2h[:, e, 4 * P * b : 4 * P * (b + 1)].bitcast(FP8X4), s2h[:, e, P * b : P * (b + 1)]
+            return w2c[:, e - HOT, 2 * P * b : 2 * P * (b + 1)].bitcast(FP4X4), s2c[:, e - HOT, P * b : P * (b + 1)]
+
+        pos_t = []
+        for r, pos in enumerate((pos1, pos2, pos3, pos4)):
+            tile = keep.tile([P, T // 16], U16, name=f"pos{r}")
+            nc.sync.dma_start(tile[:], pos)
+            pos_t.append(tile)
+        gate_t = keep.tile([P, TOP, T], F32, name="gate_t")
+        nc.sync.dma_start(out=gate_t[:], in_=gate.rearrange("r p t -> p r t"))
+
+        y = [keep.tile([P, S], F32, name=f"y{b}") for b in range(N // P)]
+
+        def gather(e):
+            lst = offs_t[:, e * C // 16 : (e + 1) * C // 16]
+            gw = ring.tile([P, C], U32, name="gw", align_bytes=64)
+            gs = ring.tile([P, C], U8, name="gs", align_bytes=64)
+            nc.vector.tensor_copy(gw[:], xw[:].bitcast(U32).indirect(lst))
+            nc.vector.tensor_copy(gs[:], xs[:].indirect(lst))
+            return gw, gs
+
+        def first_layer(e, j, gw, gs):
+            cols = slice(j * P, (j + 1) * P)
+            a1 = psum.tile([P, H], F32, name="a1", bufs=3)
+            a3 = psum.tile([P, H], F32, name="a3", bufs=3)
+            for acc, (w, s) in ((a1, w1t[e]), (a3, w3t[e])):
+                nc.tensor.matmul_mx(out=acc[:], lhsT=gw[:, cols].bitcast(FP8X4), lhsT_scale=gs[:, cols], rhs=w, rhs_scale=s, start=True, stop=True)
+            sig = ring.tile([P, H], F32, name="sig")
+            nc.scalar.activation(sig[:].rearrange("s (u q d) -> s u q d", u=2, d=2), a1[:].rearrange("s (q u d) -> s u q d", u=2, d=2), SIGMOID)
+            hb = ring.tile([P, H], BF16, name="hb", bufs=4)
+            nc.vector.tensor_tensor(hb[:].rearrange("s (u q d) -> s u q d", u=2, d=2), a3[:].rearrange("s (q u d) -> s u q d", u=2, d=2),
+                                    sig[:].rearrange("s (u q d) -> s u q d", u=2, d=2), MULT)
+            return hb
+
+        def turn(hbs):
+            bank = psum.tile([P, 2, 2, P], F32, name="turn")
+            for j, hb in enumerate(hbs):
+                words = hb[:].bitcast(F32)
+                for u in range(2):
+                    nc.tensor.transpose(bank[:, j, u, :], words[:, u * P : (u + 1) * P], ident[:])
+            ht = ring.tile([P, 4 * C], BF16, name="ht", align_bytes=64)
+            nc.scalar.copy(ht[:].bitcast(F32).rearrange("q (j s u) -> q j s u", j=2, u=2), bank[:].rearrange("q j u s -> q j s u"))
+            return ht
+
+        def quantise(ht):
+            hq = ring.tile([P, C], U32, name="hq", align_bytes=64)
+            hs = ring.tile([P, C], U8, name="hs", align_bytes=64)
+            nc.vector.quantize_mx(out=hq[:].bitcast(FP8X4), scales=hs[:], in_=ht[:])
+            return hq, hs
+
+        def second_layer(e, hq, hs):
+            bank = psum.tile([P, 2, C], F32, name="ybank")
+            for b in range(N // P):
+                w, s = w2_block(e, b)
+                nc.tensor.matmul_mx(out=bank[:, b, :], lhsT=w, lhsT_scale=s, rhs=hq[:].bitcast(FP8X4), rhs_scale=hs[:], start=True, stop=True)
+            for b in range(N // P):
+                nc.scalar.copy(y[b][:, e * C : (e + 1) * C], bank[:, b, :])
+
+        order = list(range(HOT, E)) + list(range(HOT))
+        tokens, hidden, turned = {}, {}, {}
+        tokens[0] = gather(order[0])
+        tokens[1] = gather(order[1])
+        for i in range(E + 2):
+            if i >= 2:
+                codes = quantise(turned[i - 2])
+            if i < E:
+                hidden[i] = [first_layer(order[i], j, *tokens[i]) for j in range(2)]
+            if i + 2 < E:
+                tokens[i + 2] = gather(order[i + 2])
+            if 1 <= i <= E:
+                turned[i - 1] = turn(hidden[i - 1])
+            if i >= 2:
+                second_layer(order[i - 2], *codes)
+
+        for b in range(N // P):
+            parts = []
+            for r in range(TOP):
+                part = keep.tile([P, T], F32, name=f"part{b}{r}")
+                nc.vector.tensor_tensor(part[:], y[b][:].indirect(pos_t[r][:]), gate_t[:, r, :], MULT)
+                parts.append(part)
+            s01 = keep.tile([P, T], F32, name=f"s01{b}")
+            s23 = keep.tile([P, T], F32, name=f"s23{b}")
+            res = keep.tile([P, T], F32, name=f"res{b}")
+            nc.vector.tensor_tensor(s01[:], parts[0][:], parts[1][:], ADD)
+            nc.vector.tensor_tensor(s23[:], parts[2][:], parts[3][:], ADD)
+            nc.vector.tensor_tensor(res[:], s01[:], s23[:], ADD)
+            nc.sync.dma_start(out=out[b * P : (b + 1) * P, :], in_=res[:])

@@ -20,6 +20,8 @@ ADD = mybir.AluOpType.add
 SIGMOID = mybir.ActivationFunctionType.Sigmoid
 
 P = 128
+EARLY = 0
+WINDOW = 704
 
 
 def tile_moe_hot_glu_sigmoid_kernel(
@@ -54,52 +56,52 @@ def tile_moe_hot_glu_sigmoid_kernel(
         def hot_words(words):
             return words[:, 0].rearrange("f p n t -> p f (n t)")
 
-        xs = keep.tile([P, T], U8, name="xs", align_bytes=64)
-        nc.vector.memset(xs[:].bitcast(I32), 0)
+        xs = keep.tile([P, WINDOW], U8, name="xs", align_bytes=64)
+        nc.gpsimd.memset(xs[:].bitcast(I32), 0)
+        s1h = plane_tile("s1h", HOT, H, nc.vector)
+        s3h = plane_tile("s3h", HOT, H, nc.gpsimd)
         s1c = plane_tile("s1c", COLD, H, nc.vector)
         s3c = plane_tile("s3c", COLD, H, nc.gpsimd)
+        s2h = plane_tile("s2h", HOT, N, nc.vector)
         s2c = plane_tile("s2c", COLD, N, nc.vector)
-        s1h = plane_tile("s1h", HOT, H, nc.gpsimd)
-        s3h = plane_tile("s3h", HOT, H, nc.vector)
-        s2h = plane_tile("s2h", HOT, N, nc.gpsimd)
         ident = keep.tile([P, P], F32, name="ident")
         make_identity(nc, ident[:])
 
         offs_t = keep.tile([P, S // 16], U16, name="offs_t")
         nc.sync.dma_start(offs_t[:], offs)
-        xw = keep.tile([P, T], I32, name="xw", align_bytes=64)
-        nc.sync.dma_start(out=xw[:], in_=x_words[0].rearrange("p t d -> p (t d)").bitcast(I32))
-        x_rows = x_scales[0].rearrange("(q r) c -> r q c", r=4)
-        for r in range(4):
-            nc.sync.dma_start(out=xs[r:P:32, :].bitcast(I32), in_=x_rows[r].bitcast(I32))
-
-        groups = [(0, 1), (1, 3), (3, 6)]
+        xw = keep.tile([P, WINDOW], I32, name="xw", align_bytes=64)
+        nc.vector.memset(xw[:, T:WINDOW], 0)
+        nc.sync.dma_start(out=xw[:, 0:T], in_=x_words[0].rearrange("p t d -> p (t d)").bitcast(I32))
         w1t, w3t = {}, {}
 
-        def load_cold(g):
-            a, b = groups[g]
-            t1 = load_words(f"w1c{g}", cold_words(w1c_words, a, b))
-            t3 = load_words(f"w3c{g}", cold_words(w3c_words, a, b))
+        def load_hot(f):
+            t1 = load_words(f"w1h{f}", hot_words(w1h_words)[:, f, :])
+            t3 = load_words(f"w3h{f}", hot_words(w3h_words)[:, f, :])
+            w1t[f] = (t1[:].bitcast(FP8X4), s1h[:, f, :])
+            w3t[f] = (t3[:].bitcast(FP8X4), s3h[:, f, :])
+
+        def load_cold(a, b):
+            t1 = load_words(f"w1c{a}", cold_words(w1c_words, a, b))
+            t3 = load_words(f"w3c{a}", cold_words(w3c_words, a, b))
             for f in range(a, b):
                 w1t[HOT + f] = (t1[:, f - a, :].bitcast(FP4X4), s1c[:, f, :])
                 w3t[HOT + f] = (t3[:, f - a, :].bitcast(FP4X4), s3c[:, f, :])
 
-        load_cold(0)
-        load_plane(s1c, w1c_scales[:, 0])
-        load_plane(s3c, w3c_scales[:, 0])
-        load_cold(1)
-        w2c = load_words("w2c", cold_words(w2c_words, 0, COLD))
-        load_plane(s2c, w2c_scales[:, 0])
-        load_cold(2)
+        load_hot(0)
+        x_rows = x_scales[0].rearrange("(q r) c -> r q c", r=4)
+        for r in range(4):
+            nc.sync.dma_start(out=xs[r:P:32, 0:T].bitcast(I32), in_=x_rows[r].bitcast(I32))
         load_plane(s1h, w1h_scales[:, 0])
         load_plane(s3h, w3h_scales[:, 0])
+        load_hot(1)
+        load_cold(0, 2)
+        load_plane(s1c, w1c_scales[:, 0])
+        load_plane(s3c, w3c_scales[:, 0])
         load_plane(s2h, w2h_scales[:, 0])
-        w1h = load_words("w1h", hot_words(w1h_words))
-        w3h = load_words("w3h", hot_words(w3h_words))
         w2h = load_words("w2h", hot_words(w2h_words))
-        for f in range(HOT):
-            w1t[f] = (w1h[:, f, :].bitcast(FP8X4), s1h[:, f, :])
-            w3t[f] = (w3h[:, f, :].bitcast(FP8X4), s3h[:, f, :])
+        load_cold(2, COLD)
+        w2c = load_words("w2c", cold_words(w2c_words, 0, COLD))
+        load_plane(s2c, w2c_scales[:, 0])
 
         def w2_block(e, b):
             if e < HOT:
@@ -116,77 +118,134 @@ def tile_moe_hot_glu_sigmoid_kernel(
 
         y = [keep.tile([P, S], F32, name=f"y{b}") for b in range(N // P)]
 
-        def gather(e):
-            lst = offs_t[:, e * C // 16 : (e + 1) * C // 16]
-            gw = ring.tile([P, C], U32, name="gw", align_bytes=64)
-            gs = ring.tile([P, C], U8, name="gs", align_bytes=64)
+        def gather(pair):
+            lst = offs_t[:, pair * 2 * C // 16 : (pair + 1) * 2 * C // 16]
+            gw = ring.tile([P, 2 * C], U32, name="gw", bufs=2, align_bytes=64)
+            gs = ring.tile([P, 2 * C], U8, name="gs", bufs=2, align_bytes=64)
             nc.vector.tensor_copy(gw[:], xw[:].bitcast(U32).indirect(lst))
             nc.vector.tensor_copy(gs[:], xs[:].indirect(lst))
             return gw, gs
 
         def first_layer(e, j, gw, gs):
-            cols = slice(j * P, (j + 1) * P)
-            a1 = psum.tile([P, H], F32, name="a1", bufs=3)
-            a3 = psum.tile([P, H], F32, name="a3", bufs=3)
+            cols = slice((e % 2) * C + j * P, (e % 2) * C + (j + 1) * P)
+            a1 = psum.tile([P, H], F32, name="a1", bufs=2)
+            a3 = psum.tile([P, H], F32, name="a3", bufs=2)
             for acc, (w, s) in ((a1, w1t[e]), (a3, w3t[e])):
                 nc.tensor.matmul_mx(out=acc[:], lhsT=gw[:, cols].bitcast(FP8X4), lhsT_scale=gs[:, cols], rhs=w, rhs_scale=s, start=True, stop=True)
             sig = ring.tile([P, H], F32, name="sig")
             nc.scalar.activation(sig[:].rearrange("s (u q d) -> s u q d", u=2, d=2), a1[:].rearrange("s (q u d) -> s u q d", u=2, d=2), SIGMOID)
-            hb = ring.tile([P, H], BF16, name="hb", bufs=4)
+            hb = ring.tile([P, H], BF16, name="hb", bufs=6)
             nc.vector.tensor_tensor(hb[:].rearrange("s (u q d) -> s u q d", u=2, d=2), a3[:].rearrange("s (q u d) -> s u q d", u=2, d=2),
                                     sig[:].rearrange("s (u q d) -> s u q d", u=2, d=2), MULT)
             return hb
 
         def turn(hbs):
-            bank = psum.tile([P, 2, 2, P], F32, name="turn")
-            for j, hb in enumerate(hbs):
-                words = hb[:].bitcast(F32)
+            n = len(hbs)
+            bank = psum.tile([P, n, 2, P], F32, name="turn", bufs=2)
+            for j in reversed(range(n)):
+                words = hbs[j][:].bitcast(F32)
                 for u in range(2):
                     nc.tensor.transpose(bank[:, j, u, :], words[:, u * P : (u + 1) * P], ident[:])
-            ht = ring.tile([P, 4 * C], BF16, name="ht", align_bytes=64)
-            nc.scalar.copy(ht[:].bitcast(F32).rearrange("q (j s u) -> q j s u", j=2, u=2), bank[:].rearrange("q j u s -> q j s u"))
+            ht = ring.tile([P, 4 * P * n], BF16, name="ht", align_bytes=64)
+            nc.scalar.copy(ht[:].bitcast(F32).rearrange("q (j s u) -> q j s u", j=n, u=2), bank[:].rearrange("q j u s -> q j s u"))
             return ht
 
         def quantise(ht):
-            hq = ring.tile([P, C], U32, name="hq", align_bytes=64)
-            hs = ring.tile([P, C], U8, name="hs", align_bytes=64)
+            width = ht.shape[1] // 4
+            hq = ring.tile([P, width], U32, name="hq", bufs=9, align_bytes=64)
+            hs = ring.tile([P, width], U8, name="hs", bufs=9, align_bytes=64)
             nc.vector.quantize_mx(out=hq[:].bitcast(FP8X4), scales=hs[:], in_=ht[:])
             return hq, hs
 
-        def second_layer(e, hq, hs):
-            bank = psum.tile([P, 2, C], F32, name="ybank")
-            for b in range(N // P):
-                w, s = w2_block(e, b)
-                nc.tensor.matmul_mx(out=bank[:, b, :], lhsT=w, lhsT_scale=s, rhs=hq[:].bitcast(FP8X4), rhs_scale=hs[:], start=True, stop=True)
-            for b in range(N // P):
+        def second_layer(acc, e, b, hq, hs):
+            w, s = w2_block(e, b)
+            nc.tensor.matmul_mx(out=acc, lhsT=w, lhsT_scale=s, rhs=hq[:].bitcast(FP8X4), rhs_scale=hs[:], start=True, stop=True)
+
+        chunks = T // P
+
+        def finish(e, blocks, hq, hs):
+            bank = psum.tile([P, 2, C], F32, name="ybank", bufs=2)
+            for b in range(blocks):
+                second_layer(bank[:, b, :], e, b, hq, hs)
+            for b in range(blocks):
                 nc.scalar.copy(y[b][:, e * C : (e + 1) * C], bank[:, b, :])
 
-        order = list(range(HOT, E)) + list(range(HOT))
-        tokens, hidden, turned = {}, {}, {}
-        tokens[0] = gather(order[0])
-        tokens[1] = gather(order[1])
-        for i in range(E + 2):
+        tokens, hidden, turned, codes = {}, {}, {}, {}
+        tokens[0] = gather(0)
+        for i in range(E + 1):
             if i >= 2:
-                codes = quantise(turned[i - 2])
+                codes[i - 2] = quantise(turned[i - 2])
             if i < E:
-                hidden[i] = [first_layer(order[i], j, *tokens[i]) for j in range(2)]
-            if i + 2 < E:
-                tokens[i + 2] = gather(order[i + 2])
-            if 1 <= i <= E:
+                hidden[i] = [first_layer(i, j, *tokens[i // 2]) for j in range(2)]
+            if i % 2 == 0 and i + 2 < E:
+                tokens[i // 2 + 1] = gather(i // 2 + 1)
+            if 1 <= i < E:
                 turned[i - 1] = turn(hidden[i - 1])
+            if i == E:
+                last = [turn([hb]) for hb in hidden[E - 1]]
             if i >= 2:
-                second_layer(order[i - 2], *codes)
+                finish(i - 2, 2 if i - 2 < EARLY else 1, *codes[i - 2])
+        last_codes, last_banks = [], []
+        for j in range(2):
+            last_codes.append(quantise(last[j]))
+            bank = psum.tile([P, 2 * C], F32, name="a3", bufs=2)
+            second_layer(bank[:, 0:P], E - 1, 0, *last_codes[j])
+            nc.scalar.copy(y[0][:, (E - 1) * C + j * P : (E - 1) * C + (j + 1) * P], bank[:, 0:P])
+            last_banks.append(bank)
+        for pair, first in enumerate(range(EARLY, E, 2)):
+            bank = last_banks[pair % 2]
+            second_layer(bank[:, 0:C], first, 1, *codes[first])
+            if first + 1 < E - 1:
+                second_layer(bank[:, C : 2 * C], first + 1, 1, *codes[first + 1])
+            else:
+                for j in range(2):
+                    second_layer(bank[:, C + j * P : C + (j + 1) * P], E - 1, 1, *last_codes[j])
+            nc.scalar.copy(y[1][:, first * C : (first + 2) * C], bank[:])
 
-        for b in range(N // P):
-            parts = []
-            for r in range(TOP):
-                part = keep.tile([P, T], F32, name=f"part{b}{r}")
-                nc.vector.tensor_tensor(part[:], y[b][:].indirect(pos_t[r][:]), gate_t[:, r, :], MULT)
-                parts.append(part)
-            s01 = keep.tile([P, T], F32, name=f"s01{b}")
-            s23 = keep.tile([P, T], F32, name=f"s23{b}")
-            res = keep.tile([P, T], F32, name=f"res{b}")
-            nc.vector.tensor_tensor(s01[:], parts[0][:], parts[1][:], ADD)
-            nc.vector.tensor_tensor(s23[:], parts[2][:], parts[3][:], ADD)
-            nc.vector.tensor_tensor(res[:], s01[:], s23[:], ADD)
-            nc.sync.dma_start(out=out[b * P : (b + 1) * P, :], in_=res[:])
+        half = T // 2
+
+        def product(b, r, across):
+            picked = keep.tile([P, T], F32, name=f"picked{b}{r}")
+            nc.vector.tensor_tensor(picked[:], y[b][:].indirect(pos_t[r][:]), gate_t[:, r, :], MULT)
+            for c in range(chunks):
+                nc.tensor.matmul(across[c][:], picked[:, c * P : (c + 1) * P], ident[:], start=(r == 0), stop=(r == TOP - 2), is_transpose=True)
+
+        def turn_back(b, across):
+            acc = psum.tile([P, T], F32, name="ybank", bufs=2)
+            for c in range(chunks):
+                summed = keep.tile([P, P], F32, name=f"summed{b}{c}")
+                nc.scalar.copy(summed[:], across[c][:])
+                nc.tensor.transpose(acc[:, c * P : (c + 1) * P], summed[:], ident[:])
+            return acc
+
+        part = keep.tile([P, T], F32, name="part")
+
+        def last_product(b, pieces):
+            width = T // pieces
+            for k in range(pieces):
+                cols = slice(k * width, (k + 1) * width)
+                nc.vector.tensor_tensor(part[:, cols], y[b][:].indirect(pos_t[TOP - 1][:, k * width // 16 : (k + 1) * width // 16]), gate_t[:, TOP - 1, cols], MULT)
+
+        def add_and_store(b, acc):
+            for k in range(2):
+                cols = slice(k * half, (k + 1) * half)
+                res = keep.tile([P, half], F32, name=f"res{b}{k}")
+                nc.vector.tensor_tensor(res[:], acc[:, cols], part[:, cols], ADD)
+                nc.sync.dma_start(out=out[b * P : (b + 1) * P, cols], in_=res[:])
+
+        def chunk_banks():
+            return [psum.tile([P, P], F32, name=("a1", "turn")[c % 2], bufs=2) for c in range(chunks)]
+
+        across = chunk_banks()
+        for r in range(TOP - 1):
+            product(0, r, across)
+        acc0 = turn_back(0, across)
+        across = chunk_banks()
+        for r in range(TOP - 2):
+            product(1, r, across)
+        last_product(0, 1)
+        product(1, TOP - 2, across)
+        add_and_store(0, acc0)
+        acc1 = turn_back(1, across)
+        last_product(1, 2)
+        add_and_store(1, acc1)

@@ -57,7 +57,7 @@ def tile_moe_hot_glu_sigmoid_kernel(
             return words[:, 0].rearrange("f p n t -> p f (n t)")
 
         xs = keep.tile([P, WINDOW], U8, name="xs", align_bytes=64)
-        nc.gpsimd.memset(xs[:].bitcast(I32), 0)
+        nc.gpsimd.memset(xs[:, T:WINDOW].bitcast(I32), 0)
         s1h = plane_tile("s1h", HOT, H, nc.vector)
         s3h = plane_tile("s3h", HOT, H, nc.gpsimd)
         s1c = plane_tile("s1c", COLD, H, nc.vector)
@@ -72,6 +72,9 @@ def tile_moe_hot_glu_sigmoid_kernel(
         xw = keep.tile([P, WINDOW], I32, name="xw", align_bytes=64)
         nc.vector.memset(xw[:, T:WINDOW], 0)
         nc.sync.dma_start(out=xw[:, 0:T], in_=x_words[0].rearrange("p t d -> p (t d)").bitcast(I32))
+        x_rows = x_scales[0].rearrange("(q r) c -> r q c", r=4)
+        for r in range(4):
+            nc.sync.dma_start(out=xs[r:P:4, 0:T].bitcast(I32), in_=x_rows[r].bitcast(I32).unsqueeze(1).to_broadcast([4, 8, T // 4]))
         w1t, w3t = {}, {}
 
         def load_hot(f):
@@ -88,9 +91,6 @@ def tile_moe_hot_glu_sigmoid_kernel(
                 w3t[HOT + f] = (t3[:, f - a, :].bitcast(FP4X4), s3c[:, f, :])
 
         load_hot(0)
-        x_rows = x_scales[0].rearrange("(q r) c -> r q c", r=4)
-        for r in range(4):
-            nc.sync.dma_start(out=xs[r:P:32, 0:T].bitcast(I32), in_=x_rows[r].bitcast(I32))
         load_plane(s1h, w1h_scales[:, 0])
         load_plane(s3h, w3h_scales[:, 0])
         load_hot(1)
@@ -122,8 +122,8 @@ def tile_moe_hot_glu_sigmoid_kernel(
             lst = offs_t[:, pair * 2 * C // 16 : (pair + 1) * 2 * C // 16]
             gw = ring.tile([P, 2 * C], U32, name="gw", bufs=2, align_bytes=64)
             gs = ring.tile([P, 2 * C], U8, name="gs", bufs=2, align_bytes=64)
-            nc.vector.tensor_copy(gw[:], xw[:].bitcast(U32).indirect(lst))
             nc.vector.tensor_copy(gs[:], xs[:].indirect(lst))
+            nc.vector.tensor_copy(gw[:], xw[:].bitcast(U32).indirect(lst))
             return gw, gs
 
         def first_layer(e, j, gw, gs):
@@ -204,48 +204,37 @@ def tile_moe_hot_glu_sigmoid_kernel(
 
         half = T // 2
 
-        def product(b, r, across):
-            picked = keep.tile([P, T], F32, name=f"picked{b}{r}")
-            nc.vector.tensor_tensor(picked[:], y[b][:].indirect(pos_t[r][:]), gate_t[:, r, :], MULT)
-            for c in range(chunks):
-                nc.tensor.matmul(across[c][:], picked[:, c * P : (c + 1) * P], ident[:], start=(r == 0), stop=(r == TOP - 2), is_transpose=True)
+        def product(dst, b, r, cols):
+            lst = pos_t[r][:, cols.start // 16 : cols.stop // 16]
+            nc.vector.tensor_tensor(dst[:, cols], y[b][:].indirect(lst), gate_t[:, r, cols], MULT)
 
-        def turn_back(b, across):
-            acc = psum.tile([P, T], F32, name="ybank", bufs=2)
+        def turned_sum(b, lists):
+            across = [psum.tile([P, P], F32, name=("a1", "turn")[c % 2], bufs=2) for c in range(chunks)]
+            for r in range(lists):
+                picked = keep.tile([P, T], F32, name=f"picked{b}{r}")
+                pieces = 2 if (b, r) == (1, lists - 1) else 1
+                for k in range(pieces):
+                    product(picked, b, r, slice(k * T // pieces, (k + 1) * T // pieces))
+                for c in range(chunks):
+                    nc.tensor.matmul(across[c][:], picked[:, c * P : (c + 1) * P], ident[:], start=(r == 0), stop=(r == lists - 1), is_transpose=True)
+            halves = [psum.tile([P, half], F32, name="ybank", bufs=2) for k in range(2)]
             for c in range(chunks):
                 summed = keep.tile([P, P], F32, name=f"summed{b}{c}")
                 nc.scalar.copy(summed[:], across[c][:])
-                nc.tensor.transpose(acc[:, c * P : (c + 1) * P], summed[:], ident[:])
-            return acc
+                nc.tensor.transpose(halves[c // 2][:, (c % 2) * P : (c % 2 + 1) * P], summed[:], ident[:])
+            return halves
 
+        acc0 = turned_sum(0, TOP)
+        res0 = keep.tile([P, T], F32, name="res0")
+        for k in range(2):
+            nc.scalar.copy(res0[:, k * half : (k + 1) * half], acc0[k][:])
+        nc.sync.dma_start(out=out[0:P, :], in_=res0[:])
+        acc1 = turned_sum(1, TOP - 1)
         part = keep.tile([P, T], F32, name="part")
-
-        def last_product(b, pieces):
-            width = T // pieces
-            for k in range(pieces):
-                cols = slice(k * width, (k + 1) * width)
-                nc.vector.tensor_tensor(part[:, cols], y[b][:].indirect(pos_t[TOP - 1][:, k * width // 16 : (k + 1) * width // 16]), gate_t[:, TOP - 1, cols], MULT)
-
-        def add_and_store(b, acc):
-            for k in range(2):
-                cols = slice(k * half, (k + 1) * half)
-                res = keep.tile([P, half], F32, name=f"res{b}{k}")
-                nc.vector.tensor_tensor(res[:], acc[:, cols], part[:, cols], ADD)
-                nc.sync.dma_start(out=out[b * P : (b + 1) * P, cols], in_=res[:])
-
-        def chunk_banks():
-            return [psum.tile([P, P], F32, name=("a1", "turn")[c % 2], bufs=2) for c in range(chunks)]
-
-        across = chunk_banks()
-        for r in range(TOP - 1):
-            product(0, r, across)
-        acc0 = turn_back(0, across)
-        across = chunk_banks()
-        for r in range(TOP - 2):
-            product(1, r, across)
-        last_product(0, 1)
-        product(1, TOP - 2, across)
-        add_and_store(0, acc0)
-        acc1 = turn_back(1, across)
-        last_product(1, 2)
-        add_and_store(1, acc1)
+        for k in range(2):
+            product(part, 1, TOP - 1, slice(k * half, (k + 1) * half))
+        for k in range(2):
+            cols = slice(k * half, (k + 1) * half)
+            res = keep.tile([P, half], F32, name=f"res1{k}")
+            nc.vector.tensor_tensor(res[:], acc1[k][:], part[:, cols], ADD)
+            nc.sync.dma_start(out=out[P : 2 * P, cols], in_=res[:])

@@ -20,7 +20,6 @@ ADD = mybir.AluOpType.add
 SIGMOID = mybir.ActivationFunctionType.Sigmoid
 
 P = 128
-EARLY = 0
 WINDOW = 704
 
 
@@ -32,7 +31,6 @@ def tile_moe_hot_glu_sigmoid_kernel(
     COLD = E - HOT
     with ExitStack() as ctx:
         keep = ctx.enter_context(tc.tile_pool(name="keep", bufs=1))
-        ring = ctx.enter_context(tc.tile_pool(name="ring", bufs=3))
         psum = ctx.enter_context(tc.psum_pool(name="psum", bufs=1))
 
         def plane_tile(name, experts, width, engine):
@@ -58,6 +56,8 @@ def tile_moe_hot_glu_sigmoid_kernel(
 
         xs = keep.tile([P, WINDOW], U8, name="xs", align_bytes=64)
         nc.gpsimd.memset(xs[:, T:WINDOW].bitcast(I32), 0)
+        xw = keep.tile([P, WINDOW], I32, name="xw", align_bytes=64)
+        nc.gpsimd.memset(xw[:, T:WINDOW], 0)
         s1h = plane_tile("s1h", HOT, H, nc.vector)
         s3h = plane_tile("s3h", HOT, H, nc.gpsimd)
         s1c = plane_tile("s1c", COLD, H, nc.vector)
@@ -68,40 +68,37 @@ def tile_moe_hot_glu_sigmoid_kernel(
         make_identity(nc, ident[:])
 
         offs_t = keep.tile([P, S // 16], U16, name="offs_t")
-        nc.sync.dma_start(offs_t[:], offs)
-        xw = keep.tile([P, WINDOW], I32, name="xw", align_bytes=64)
-        nc.vector.memset(xw[:, T:WINDOW], 0)
         nc.sync.dma_start(out=xw[:, 0:T], in_=x_words[0].rearrange("p t d -> p (t d)").bitcast(I32))
         x_rows = x_scales[0].rearrange("(q r) c -> r q c", r=4)
         for r in range(4):
             nc.sync.dma_start(out=xs[r:P:4, 0:T].bitcast(I32), in_=x_rows[r].bitcast(I32).unsqueeze(1).to_broadcast([4, 8, T // 4]))
+        nc.sync.dma_start(offs_t[:], offs)
         w1t, w3t = {}, {}
 
-        def load_hot(f):
-            t1 = load_words(f"w1h{f}", hot_words(w1h_words)[:, f, :])
-            t3 = load_words(f"w3h{f}", hot_words(w3h_words)[:, f, :])
-            w1t[f] = (t1[:].bitcast(FP8X4), s1h[:, f, :])
-            w3t[f] = (t3[:].bitcast(FP8X4), s3h[:, f, :])
+        def load_hot(table, name, words, plane):
+            tile = load_words(name, hot_words(words))
+            for f in range(HOT):
+                table[f] = (tile[:, f, :].bitcast(FP8X4), plane[:, f, :])
 
-        def load_cold(a, b):
-            t1 = load_words(f"w1c{a}", cold_words(w1c_words, a, b))
-            t3 = load_words(f"w3c{a}", cold_words(w3c_words, a, b))
+        def load_cold(table, name, words, plane, a, b):
+            tile = load_words(f"{name}{a}", cold_words(words, a, b))
             for f in range(a, b):
-                w1t[HOT + f] = (t1[:, f - a, :].bitcast(FP4X4), s1c[:, f, :])
-                w3t[HOT + f] = (t3[:, f - a, :].bitcast(FP4X4), s3c[:, f, :])
+                table[HOT + f] = (tile[:, f - a, :].bitcast(FP4X4), plane[:, f, :])
 
-        load_hot(0)
-        load_plane(s1h, w1h_scales[:, 0])
-        load_plane(s3h, w3h_scales[:, 0])
-        load_hot(1)
-        load_cold(0, 2)
+        load_cold(w1t, "w1c", w1c_words, s1c, 0, 2)
         load_plane(s1c, w1c_scales[:, 0])
+        load_cold(w1t, "w1c", w1c_words, s1c, 2, COLD)
         load_plane(s3c, w3c_scales[:, 0])
-        load_plane(s2h, w2h_scales[:, 0])
-        w2h = load_words("w2h", hot_words(w2h_words))
-        load_cold(2, COLD)
-        w2c = load_words("w2c", cold_words(w2c_words, 0, COLD))
+        load_cold(w3t, "w3c", w3c_words, s3c, 4, COLD)
+        load_plane(s1h, w1h_scales[:, 0])
+        load_hot(w1t, "w1h", w1h_words, s1h)
+        load_cold(w3t, "w3c", w3c_words, s3c, 0, 4)
+        load_plane(s3h, w3h_scales[:, 0])
+        load_hot(w3t, "w3h", w3h_words, s3h)
         load_plane(s2c, w2c_scales[:, 0])
+        load_plane(s2h, w2h_scales[:, 0])
+        w2c = load_words("w2c", cold_words(w2c_words, 0, COLD))
+        w2h = load_words("w2h", hot_words(w2h_words))
 
         def w2_block(e, b):
             if e < HOT:
@@ -118,89 +115,95 @@ def tile_moe_hot_glu_sigmoid_kernel(
 
         y = [keep.tile([P, S], F32, name=f"y{b}") for b in range(N // P)]
 
-        def gather(pair):
-            lst = offs_t[:, pair * 2 * C // 16 : (pair + 1) * 2 * C // 16]
-            gw = ring.tile([P, 2 * C], U32, name="gw", bufs=2, align_bytes=64)
-            gs = ring.tile([P, 2 * C], U8, name="gs", bufs=2, align_bytes=64)
-            nc.vector.tensor_copy(gs[:], xs[:].indirect(lst))
+        banks = [psum.tile([P, H], F32, name=f"bank{k}") for k in range(8)]
+        experts = list(range(HOT, E)) + list(range(HOT))
+        tiles = [(e, j) for e in experts for j in range(2)]
+
+        tokens = {}
+        pieces = [tiles[k : k + 4] for k in range(0, 2 * E, 4)]
+        for n, piece in enumerate(pieces):
+            first = piece[0][0] * C + piece[0][1] * P
+            lst = offs_t[:, first // 16 : (first + len(piece) * P) // 16]
+            gw = keep.tile([P, len(piece) * P], U32, name=f"gw{n}", align_bytes=64)
+            gs = keep.tile([P, len(piece) * P], U8, name=f"gs{n}", align_bytes=64)
             nc.vector.tensor_copy(gw[:], xw[:].bitcast(U32).indirect(lst))
-            return gw, gs
+            nc.vector.tensor_copy(gs[:], xs[:].indirect(lst))
+            for k, tile in enumerate(piece):
+                tokens[tile] = (gw[:, k * P : (k + 1) * P].bitcast(FP8X4), gs[:, k * P : (k + 1) * P])
 
-        def first_layer(e, j, gw, gs):
-            cols = slice((e % 2) * C + j * P, (e % 2) * C + (j + 1) * P)
-            a1 = psum.tile([P, H], F32, name="a1", bufs=2)
-            a3 = psum.tile([P, H], F32, name="a3", bufs=2)
-            for acc, (w, s) in ((a1, w1t[e]), (a3, w3t[e])):
-                nc.tensor.matmul_mx(out=acc[:], lhsT=gw[:, cols].bitcast(FP8X4), lhsT_scale=gs[:, cols], rhs=w, rhs_scale=s, start=True, stop=True)
-            sig = ring.tile([P, H], F32, name="sig")
-            nc.scalar.activation(sig[:].rearrange("s (u q d) -> s u q d", u=2, d=2), a1[:].rearrange("s (q u d) -> s u q d", u=2, d=2), SIGMOID)
-            hb = ring.tile([P, H], BF16, name="hb", bufs=6)
-            nc.vector.tensor_tensor(hb[:].rearrange("s (u q d) -> s u q d", u=2, d=2), a3[:].rearrange("s (q u d) -> s u q d", u=2, d=2),
-                                    sig[:].rearrange("s (u q d) -> s u q d", u=2, d=2), MULT)
-            return hb
+        def first_layer(bank, tile, table):
+            (words, scales), (w, s) = tokens[tile], table[tile[0]]
+            nc.tensor.matmul_mx(out=bank[:], lhsT=words, lhsT_scale=scales, rhs=w, rhs_scale=s, start=True, stop=True)
+            return bank[:].rearrange("s (q u d) -> s u q d", u=2, d=2)
 
-        def turn(hbs):
-            n = len(hbs)
-            bank = psum.tile([P, n, 2, P], F32, name="turn", bufs=2)
+        sigs = {}
+        for i, tile in enumerate(tiles):
+            a1 = first_layer(banks[4 + i % 4 if i // 4 == 1 else i % 4], tile, w1t)
+            sig = keep.tile([P, H], F32, name=f"sig{i}")
+            nc.scalar.activation(sig[:].rearrange("s (u q d) -> s u q d", u=2, d=2), a1, SIGMOID)
+            sigs[tile] = sig
+
+        order = experts[4:6] + experts[0:4] + experts[6:8]
+        hidden = {}
+        turned = keep.tile([P, 2 * E * H], BF16, name="turned", align_bytes=64)
+
+        def products(i):
+            for j in range(2):
+                tile = (order[i], j)
+                a3 = first_layer(banks[4 + (2 * i + j) % 4], tile, w3t)
+                hb = keep.tile([P, H], BF16, name=f"hb{2 * i + j}")
+                nc.vector.tensor_tensor(hb[:].rearrange("s (u q d) -> s u q d", u=2, d=2), a3, sigs[tile][:].rearrange("s (u q d) -> s u q d", u=2, d=2), MULT)
+                hidden[2 * i + j] = hb
+
+        def turn(bank, first, last):
+            n = last - first
+            across = bank[:, 0 : n * C].rearrange("q (j u s) -> q j u s", j=n, u=2)
             for j in reversed(range(n)):
-                words = hbs[j][:].bitcast(F32)
+                words = hidden[first + j][:].bitcast(F32)
                 for u in range(2):
-                    nc.tensor.transpose(bank[:, j, u, :], words[:, u * P : (u + 1) * P], ident[:])
-            ht = ring.tile([P, 4 * P * n], BF16, name="ht", align_bytes=64)
-            nc.scalar.copy(ht[:].bitcast(F32).rearrange("q (j s u) -> q j s u", j=n, u=2), bank[:].rearrange("q j u s -> q j s u"))
-            return ht
+                    nc.tensor.transpose(across[:, j, u, :], words[:, u * P : (u + 1) * P], ident[:])
+            dst = turned[:, first * H : last * H].bitcast(F32).rearrange("q (j s u) -> q j s u", j=n, u=2)
+            nc.scalar.copy(dst, across.rearrange("q j u s -> q j s u"))
 
-        def quantise(ht):
-            width = ht.shape[1] // 4
-            hq = ring.tile([P, width], U32, name="hq", bufs=9, align_bytes=64)
-            hs = ring.tile([P, width], U8, name="hs", bufs=9, align_bytes=64)
-            nc.vector.quantize_mx(out=hq[:].bitcast(FP8X4), scales=hs[:], in_=ht[:])
-            return hq, hs
+        codes = {}
 
-        def second_layer(acc, e, b, hq, hs):
-            w, s = w2_block(e, b)
-            nc.tensor.matmul_mx(out=acc, lhsT=w, lhsT_scale=s, rhs=hq[:].bitcast(FP8X4), rhs_scale=hs[:], start=True, stop=True)
+        def quantise(first, last):
+            hq = keep.tile([P, (last - first) * P], U32, name=f"hq{first}", align_bytes=64)
+            hs = keep.tile([P, (last - first) * P], U8, name=f"hs{first}", align_bytes=64)
+            nc.vector.quantize_mx(out=hq[:].bitcast(FP8X4), scales=hs[:], in_=turned[:, first * H : last * H])
+            step = min(2, last - first)
+            for i in range(first, last, step):
+                cols = slice((i - first) * P, (i - first + step) * P)
+                codes[i] = (hq[:, cols].bitcast(FP8X4), hs[:, cols], step)
+
+        def second_layer(bank, b, first, last, copy):
+            i = first
+            while i < last:
+                hq, hs, step = codes[i]
+                w, s = w2_block(order[i // 2], b)
+                nc.tensor.matmul_mx(out=bank[:, (i - first) * P : (i - first + step) * P], lhsT=w, lhsT_scale=s, rhs=hq, rhs_scale=hs, start=True, stop=True)
+                i = i + step
+            slot = order[first // 2] * C + first % 2 * P
+            copy(y[b][:, slot : slot + (last - first) * P], bank[:, 0 : (last - first) * P])
 
         chunks = T // P
-
-        def finish(e, blocks, hq, hs):
-            bank = psum.tile([P, 2, C], F32, name="ybank", bufs=2)
-            for b in range(blocks):
-                second_layer(bank[:, b, :], e, b, hq, hs)
-            for b in range(blocks):
-                nc.scalar.copy(y[b][:, e * C : (e + 1) * C], bank[:, b, :])
-
-        tokens, hidden, turned, codes = {}, {}, {}, {}
-        tokens[0] = gather(0)
-        for i in range(E + 1):
-            if i >= 2:
-                codes[i - 2] = quantise(turned[i - 2])
-            if i < E:
-                hidden[i] = [first_layer(i, j, *tokens[i // 2]) for j in range(2)]
-            if i % 2 == 0 and i + 2 < E:
-                tokens[i // 2 + 1] = gather(i // 2 + 1)
-            if 1 <= i < E:
-                turned[i - 1] = turn(hidden[i - 1])
-            if i == E:
-                last = [turn([hb]) for hb in hidden[E - 1]]
-            if i >= 2:
-                finish(i - 2, 2 if i - 2 < EARLY else 1, *codes[i - 2])
-        last_codes, last_banks = [], []
-        for j in range(2):
-            last_codes.append(quantise(last[j]))
-            bank = psum.tile([P, 2 * C], F32, name="a3", bufs=2)
-            second_layer(bank[:, 0:P], E - 1, 0, *last_codes[j])
-            nc.scalar.copy(y[0][:, (E - 1) * C + j * P : (E - 1) * C + (j + 1) * P], bank[:, 0:P])
-            last_banks.append(bank)
-        for pair, first in enumerate(range(EARLY, E, 2)):
-            bank = last_banks[pair % 2]
-            second_layer(bank[:, 0:C], first, 1, *codes[first])
-            if first + 1 < E - 1:
-                second_layer(bank[:, C : 2 * C], first + 1, 1, *codes[first + 1])
-            else:
-                for j in range(2):
-                    second_layer(bank[:, C + j * P : C + (j + 1) * P], E - 1, 1, *last_codes[j])
-            nc.scalar.copy(y[1][:, first * C : (first + 2) * C], bank[:])
+        for i in range(E):
+            products(i)
+            if i < E - 1:
+                turn(banks[i % 3], 2 * i, 2 * i + 2)
+            if i == 3:
+                quantise(0, 4)
+                second_layer(banks[3], 0, 0, 4, nc.scalar.copy)
+        turn(banks[1], 14, 15)
+        turn(banks[2], 15, 16)
+        for first, last in ((4, 8), (8, 12), (12, 14), (14, 15), (15, 16)):
+            quantise(first, last)
+        second_layer(banks[4], 0, 4, 8, nc.scalar.copy)
+        second_layer(banks[5], 0, 8, 12, nc.vector.tensor_copy)
+        second_layer(banks[6], 0, 12, 14, nc.scalar.copy)
+        second_layer(banks[7], 0, 14, 16, nc.scalar.copy)
+        for pair in range(4):
+            second_layer(banks[4 + pair], 1, 4 * pair, 4 * pair + 4, nc.scalar.copy)
 
         half = T // 2
 
@@ -208,33 +211,44 @@ def tile_moe_hot_glu_sigmoid_kernel(
             lst = pos_t[r][:, cols.start // 16 : cols.stop // 16]
             nc.vector.tensor_tensor(dst[:, cols], y[b][:].indirect(lst), gate_t[:, r, cols], MULT)
 
-        def turned_sum(b, lists):
-            across = [psum.tile([P, P], F32, name=("a1", "turn")[c % 2], bufs=2) for c in range(chunks)]
-            for r in range(lists):
-                picked = keep.tile([P, T], F32, name=f"picked{b}{r}")
-                pieces = 2 if (b, r) == (1, lists - 1) else 1
-                for k in range(pieces):
-                    product(picked, b, r, slice(k * T // pieces, (k + 1) * T // pieces))
-                for c in range(chunks):
-                    nc.tensor.matmul(across[c][:], picked[:, c * P : (c + 1) * P], ident[:], start=(r == 0), stop=(r == lists - 1), is_transpose=True)
-            halves = [psum.tile([P, half], F32, name="ybank", bufs=2) for k in range(2)]
-            for c in range(chunks):
+        def turned_sum(b, whole_halves):
+            picked = [keep.tile([P, T], F32, name=f"picked{b}{r}") for r in range(TOP)]
+            for r in range(TOP):
+                width = T if r < TOP - 1 else whole_halves * half
+                if width:
+                    product(picked[r], b, r, slice(0, width))
+                for c in range(width // P):
+                    last = TOP - 1 if c * P < whole_halves * half else TOP - 2
+                    nc.tensor.matmul(banks[c][:, 0:P], picked[r][:, c * P : (c + 1) * P], ident[:], start=(r == 0), stop=(r == last), is_transpose=True)
+            halves = [banks[4 + 2 * b + k][:, 0:half] for k in range(2)]
+            for c in reversed(range(chunks)) if whole_halves else range(chunks):
                 summed = keep.tile([P, P], F32, name=f"summed{b}{c}")
-                nc.scalar.copy(summed[:], across[c][:])
+                nc.scalar.copy(summed[:], banks[c][:, 0:P])
                 nc.tensor.transpose(halves[c // 2][:, (c % 2) * P : (c % 2 + 1) * P], summed[:], ident[:])
-            return halves
+            return halves, picked
 
-        acc0 = turned_sum(0, TOP)
-        res0 = keep.tile([P, T], F32, name="res0")
-        for k in range(2):
-            nc.scalar.copy(res0[:, k * half : (k + 1) * half], acc0[k][:])
-        nc.sync.dma_start(out=out[0:P, :], in_=res0[:])
-        acc1 = turned_sum(1, TOP - 1)
-        part = keep.tile([P, T], F32, name="part")
-        for k in range(2):
-            product(part, 1, TOP - 1, slice(k * half, (k + 1) * half))
-        for k in range(2):
-            cols = slice(k * half, (k + 1) * half)
-            res = keep.tile([P, half], F32, name=f"res1{k}")
-            nc.vector.tensor_tensor(res[:], acc1[k][:], part[:, cols], ADD)
-            nc.sync.dma_start(out=out[P : 2 * P, cols], in_=res[:])
+        def store(b, k, res):
+            nc.sync.dma_start(out=out[b * P : (b + 1) * P, k * half : (k + 1) * half], in_=res[:])
+
+        sums = {0: turned_sum(0, 1)}
+        res = keep.tile([P, half], F32, name="res00")
+        nc.scalar.copy(res[:], sums[0][0][0])
+        store(0, 0, res)
+        sums[1] = turned_sum(1, 0)
+
+        parts = {(0, 1): sums[1][1][0], (1, 0): sums[1][1][TOP - 1], (1, 1): sums[1][1][TOP - 1]}
+
+        def last_list(b, k):
+            product(parts[b, k], b, TOP - 1, slice(k * half, (k + 1) * half))
+
+        def add(b, k):
+            res = keep.tile([P, half], F32, name=f"res{b}{k}")
+            nc.vector.tensor_tensor(res[:], sums[b][0][k], parts[b, k][:, k * half : (k + 1) * half], ADD)
+            store(b, k, res)
+
+        last_list(1, 0)
+        last_list(1, 1)
+        last_list(0, 1)
+        add(1, 0)
+        add(1, 1)
+        add(0, 1)

@@ -20,6 +20,8 @@ ADD = mybir.AluOpType.add
 SIGMOID = mybir.ActivationFunctionType.Sigmoid
 
 P = 128
+ASIDE = 3
+AHEAD = 0
 WINDOW = 704
 
 
@@ -120,7 +122,8 @@ def tile_moe_hot_glu_sigmoid_kernel(
         tiles = [(e, j) for e in experts for j in range(2)]
 
         tokens = {}
-        pieces = [tiles[k : k + 4] for k in range(0, 2 * E, 4)]
+        cuts = (0, 2, 6, 10, 12, 14, 16)
+        pieces = [tiles[a:z] for a, z in zip(cuts, cuts[1:])]
         for n, piece in enumerate(pieces):
             first = piece[0][0] * C + piece[0][1] * P
             lst = offs_t[:, first // 16 : (first + len(piece) * P) // 16]
@@ -136,39 +139,72 @@ def tile_moe_hot_glu_sigmoid_kernel(
             nc.tensor.matmul_mx(out=bank[:], lhsT=words, lhsT_scale=scales, rhs=w, rhs_scale=s, start=True, stop=True)
             return bank[:].rearrange("s (q u d) -> s u q d", u=2, d=2)
 
-        sigs = {}
-        for i, tile in enumerate(tiles):
-            a1 = first_layer(banks[4 + i % 4 if i // 4 == 1 else i % 4], tile, w1t)
-            sig = keep.tile([P, H], F32, name=f"sig{i}")
-            nc.scalar.activation(sig[:].rearrange("s (u q d) -> s u q d", u=2, d=2), a1, SIGMOID)
-            sigs[tile] = sig
+        def in_order(tile):
+            return tile[:].rearrange("s (u q d) -> s u q d", u=2, d=2)
 
-        order = experts[4:6] + experts[0:4] + experts[6:8]
+        sigs = {}
+
+        def sigmoid(i, bank):
+            a1 = first_layer(bank, tiles[i], w1t)
+            sig = keep.tile([P, H], F32, name=f"sig{i}", align_bytes=64)
+            nc.scalar.activation(in_order(sig), a1, SIGMOID)
+            sigs[tiles[i]] = sig
+
+        order = experts[4:6] + experts[0:2] + experts[6:8] + experts[2:4]
         hidden = {}
         turned = keep.tile([P, 2 * E * H], BF16, name="turned", align_bytes=64)
+
+        rounds = []
+
+        def low_bank():
+            rounds.append(None)
+            return banks[(len(rounds) - 1) % 4]
+
+        aside = tiles[8 - ASIDE : 8]
+
+        def product_aside(i):
+            a3 = first_layer(low_bank(), aside[i], w3t)
+            plain = keep.tile([P, H], F32, name=f"plain{i}")
+            nc.scalar.copy(in_order(plain), a3)
+            hb = keep.tile([P, H], BF16, name=f"aside{i}")
+            nc.gpsimd.tensor_tensor(hb[:], plain[:], sigs[aside[i]][:], MULT)
+            hidden[2 * order.index(aside[i][0]) + aside[i][1]] = hb
+
+        for i in range(14):
+            sigmoid(i, banks[i] if i // 4 == 1 else low_bank())
+        for i in range(AHEAD):
+            product_aside(i)
+        for i in range(14, 16):
+            sigmoid(i, low_bank())
+        for i in range(AHEAD, ASIDE):
+            product_aside(i)
+        made = []
 
         def products(i):
             for j in range(2):
                 tile = (order[i], j)
-                a3 = first_layer(banks[4 + (2 * i + j) % 4], tile, w3t)
-                hb = keep.tile([P, H], BF16, name=f"hb{2 * i + j}")
-                nc.vector.tensor_tensor(hb[:].rearrange("s (u q d) -> s u q d", u=2, d=2), a3, sigs[tile][:].rearrange("s (u q d) -> s u q d", u=2, d=2), MULT)
-                hidden[2 * i + j] = hb
+                if tile not in aside:
+                    a3 = first_layer(banks[4 + len(made) % 4], tile, w3t)
+                    hb = keep.tile([P, H], BF16, name=f"hb{2 * i + j}")
+                    nc.vector.tensor_tensor(in_order(hb), a3, in_order(sigs[tile]), MULT)
+                    hidden[2 * i + j] = hb
+                    made.append(tile)
 
-        def turn(bank, first, last):
-            n = last - first
-            across = bank[:, 0 : n * C].rearrange("q (j u s) -> q j u s", j=n, u=2)
-            for j in reversed(range(n)):
-                words = hidden[first + j][:].bitcast(F32)
+        def turn(first, last, *into):
+            n = (last - first) // len(into)
+            across = [bank[:, 0 : n * C].rearrange("q (j u s) -> q j u s", j=n, u=2) for bank in into]
+            for i in reversed(range(first, last)):
+                words = hidden[i][:].bitcast(F32)
                 for u in range(2):
-                    nc.tensor.transpose(across[:, j, u, :], words[:, u * P : (u + 1) * P], ident[:])
-            dst = turned[:, first * H : last * H].bitcast(F32).rearrange("q (j s u) -> q j s u", j=n, u=2)
-            nc.scalar.copy(dst, across.rearrange("q j u s -> q j s u"))
+                    nc.tensor.transpose(across[(i - first) // n][:, (i - first) % n, u, :], words[:, u * P : (u + 1) * P], ident[:])
+            for k in reversed(range(len(into))):
+                dst = turned[:, (first + k * n) * H : (first + (k + 1) * n) * H].bitcast(F32).rearrange("q (j s u) -> q j s u", j=n, u=2)
+                nc.scalar.copy(dst, across[k].rearrange("q j u s -> q j s u"))
 
         codes = {}
 
-        def quantise(first, last):
-            hq = keep.tile([P, (last - first) * P], U32, name=f"hq{first}", align_bytes=64)
+        def quantise(first, last, name):
+            hq = keep.tile([P, (last - first) * P], U32, name=name, align_bytes=64)
             hs = keep.tile([P, (last - first) * P], U8, name=f"hs{first}", align_bytes=64)
             nc.vector.quantize_mx(out=hq[:].bitcast(FP8X4), scales=hs[:], in_=turned[:, first * H : last * H])
             step = min(2, last - first)
@@ -189,21 +225,21 @@ def tile_moe_hot_glu_sigmoid_kernel(
         chunks = T // P
         for i in range(E):
             products(i)
-            if i < E - 1:
-                turn(banks[i % 3], 2 * i, 2 * i + 2)
-            if i == 3:
-                quantise(0, 4)
-                second_layer(banks[3], 0, 0, 4, nc.scalar.copy)
-        turn(banks[1], 14, 15)
-        turn(banks[2], 15, 16)
-        for first, last in ((4, 8), (8, 12), (12, 14), (14, 15), (15, 16)):
-            quantise(first, last)
-        second_layer(banks[4], 0, 4, 8, nc.scalar.copy)
-        second_layer(banks[5], 0, 8, 12, nc.vector.tensor_copy)
-        second_layer(banks[6], 0, 12, 14, nc.scalar.copy)
-        second_layer(banks[7], 0, 14, 16, nc.scalar.copy)
+            if i < E - 2:
+                turn(2 * i, 2 * i + 2, low_bank())
+        turn(14, 16, low_bank())
+        turn(13, 14, low_bank())
+        turn(12, 13, low_bank())
+        for first, last, name in ((0, 4, "sig15"), (4, 8, "sig4"), (8, 12, "sig14"), (14, 16, "hq14"), (13, 14, "hq13"), (12, 13, "hq12")):
+            quantise(first, last, name)
+        second_layer(banks[5], 0, 0, 4, nc.scalar.copy)
+        second_layer(banks[6], 0, 4, 8, nc.scalar.copy)
+        second_layer(banks[7], 0, 8, 12, nc.vector.tensor_copy)
+        second_layer(banks[4], 0, 14, 16, nc.vector.tensor_copy)
+        last = low_bank()
+        second_layer(last, 0, 12, 14, nc.scalar.copy)
         for pair in range(4):
-            second_layer(banks[4 + pair], 1, 4 * pair, 4 * pair + 4, nc.scalar.copy)
+            second_layer((last, banks[4])[pair % 2], 1, 4 * pair, 4 * pair + 4, nc.scalar.copy)
 
         half = T // 2
 
@@ -211,44 +247,33 @@ def tile_moe_hot_glu_sigmoid_kernel(
             lst = pos_t[r][:, cols.start // 16 : cols.stop // 16]
             nc.vector.tensor_tensor(dst[:, cols], y[b][:].indirect(lst), gate_t[:, r, cols], MULT)
 
-        def turned_sum(b, whole_halves):
-            picked = [keep.tile([P, T], F32, name=f"picked{b}{r}") for r in range(TOP)]
-            for r in range(TOP):
-                width = T if r < TOP - 1 else whole_halves * half
-                if width:
-                    product(picked[r], b, r, slice(0, width))
-                for c in range(width // P):
-                    last = TOP - 1 if c * P < whole_halves * half else TOP - 2
-                    nc.tensor.matmul(banks[c][:, 0:P], picked[r][:, c * P : (c + 1) * P], ident[:], start=(r == 0), stop=(r == last), is_transpose=True)
+        def turned_sum(b, lists):
+            across = [banks[c][:, 0:P] for c in range(chunks)]
+            for r in range(lists):
+                picked = keep.tile([P, T], F32, name=f"picked{b}{r}")
+                pieces = 2 if (b, r) == (1, lists - 1) else 1
+                for k in range(pieces):
+                    product(picked, b, r, slice(k * T // pieces, (k + 1) * T // pieces))
+                for c in range(chunks):
+                    nc.tensor.matmul(across[c][:], picked[:, c * P : (c + 1) * P], ident[:], start=(r == 0), stop=(r == lists - 1), is_transpose=True)
             halves = [banks[4 + 2 * b + k][:, 0:half] for k in range(2)]
-            for c in reversed(range(chunks)) if whole_halves else range(chunks):
+            for c in range(chunks):
                 summed = keep.tile([P, P], F32, name=f"summed{b}{c}")
-                nc.scalar.copy(summed[:], banks[c][:, 0:P])
+                nc.scalar.copy(summed[:], across[c][:])
                 nc.tensor.transpose(halves[c // 2][:, (c % 2) * P : (c % 2 + 1) * P], summed[:], ident[:])
-            return halves, picked
+            return halves
 
-        def store(b, k, res):
-            nc.sync.dma_start(out=out[b * P : (b + 1) * P, k * half : (k + 1) * half], in_=res[:])
-
-        sums = {0: turned_sum(0, 1)}
-        res = keep.tile([P, half], F32, name="res00")
-        nc.scalar.copy(res[:], sums[0][0][0])
-        store(0, 0, res)
-        sums[1] = turned_sum(1, 0)
-
-        parts = {(0, 1): sums[1][1][0], (1, 0): sums[1][1][TOP - 1], (1, 1): sums[1][1][TOP - 1]}
-
-        def last_list(b, k):
-            product(parts[b, k], b, TOP - 1, slice(k * half, (k + 1) * half))
-
-        def add(b, k):
-            res = keep.tile([P, half], F32, name=f"res{b}{k}")
-            nc.vector.tensor_tensor(res[:], sums[b][0][k], parts[b, k][:, k * half : (k + 1) * half], ADD)
-            store(b, k, res)
-
-        last_list(1, 0)
-        last_list(1, 1)
-        last_list(0, 1)
-        add(1, 0)
-        add(1, 1)
-        add(0, 1)
+        acc0 = turned_sum(0, TOP)
+        res0 = keep.tile([P, T], F32, name="res0")
+        for k in range(2):
+            nc.scalar.copy(res0[:, k * half : (k + 1) * half], acc0[k][:])
+        nc.sync.dma_start(out=out[0:P, :], in_=res0[:])
+        acc1 = turned_sum(1, TOP - 1)
+        part = keep.tile([P, T], F32, name="part")
+        for k in range(2):
+            product(part, 1, TOP - 1, slice(k * half, (k + 1) * half))
+        for k in range(2):
+            cols = slice(k * half, (k + 1) * half)
+            res = keep.tile([P, half], F32, name=f"res1{k}")
+            nc.vector.tensor_tensor(res[:], acc1[k][:], part[:, cols], ADD)
+            nc.sync.dma_start(out=out[P : 2 * P, cols], in_=res[:])

@@ -22,7 +22,6 @@ SIGMOID = mybir.ActivationFunctionType.Sigmoid
 P = 128
 ASIDE = 3
 AHEAD = 0
-WINDOW = 704
 
 
 def tile_moe_hot_glu_sigmoid_kernel(
@@ -56,10 +55,8 @@ def tile_moe_hot_glu_sigmoid_kernel(
         def hot_words(words):
             return words[:, 0].rearrange("f p n t -> p f (n t)")
 
-        xs = keep.tile([P, WINDOW], U8, name="xs", align_bytes=64)
-        nc.gpsimd.memset(xs[:, T:WINDOW].bitcast(I32), 0)
-        xw = keep.tile([P, WINDOW], I32, name="xw", align_bytes=64)
-        nc.gpsimd.memset(xw[:, T:WINDOW], 0)
+        xs = keep.tile([P, T], U8, name="xs", align_bytes=64)
+        xw = keep.tile([P, T], I32, name="xw", align_bytes=64)
         s1h = plane_tile("s1h", HOT, H, nc.vector)
         s3h = plane_tile("s3h", HOT, H, nc.gpsimd)
         s1c = plane_tile("s1c", COLD, H, nc.vector)
@@ -89,13 +86,15 @@ def tile_moe_hot_glu_sigmoid_kernel(
 
         load_cold(w1t, "w1c", w1c_words, s1c, 0, 2)
         load_plane(s1c, w1c_scales[:, 0])
-        load_cold(w1t, "w1c", w1c_words, s1c, 2, COLD)
-        load_plane(s3c, w3c_scales[:, 0])
-        load_cold(w3t, "w3c", w3c_words, s3c, 4, COLD)
         load_plane(s1h, w1h_scales[:, 0])
-        load_hot(w1t, "w1h", w1h_words, s1h)
-        load_cold(w3t, "w3c", w3c_words, s3c, 0, 4)
+        load_cold(w1t, "w1c", w1c_words, s1c, 2, 4)
+        load_cold(w1t, "w1c", w1c_words, s1c, 4, COLD)
+        load_plane(s3c, w3c_scales[:, 0])
         load_plane(s3h, w3h_scales[:, 0])
+        load_cold(w3t, "w3c", w3c_words, s3c, 4, COLD)
+        load_hot(w1t, "w1h", w1h_words, s1h)
+        load_cold(w3t, "w3c", w3c_words, s3c, 0, 2)
+        load_cold(w3t, "w3c", w3c_words, s3c, 2, 4)
         load_hot(w3t, "w3h", w3h_words, s3h)
         load_plane(s2c, w2c_scales[:, 0])
         load_plane(s2h, w2h_scales[:, 0])
@@ -122,7 +121,7 @@ def tile_moe_hot_glu_sigmoid_kernel(
         tiles = [(e, j) for e in experts for j in range(2)]
 
         tokens = {}
-        cuts = (0, 2, 6, 10, 12, 14, 16)
+        cuts = (0, 3, 6, 9, 12, 14, 16)
         pieces = [tiles[a:z] for a, z in zip(cuts, cuts[1:])]
         for n, piece in enumerate(pieces):
             first = piece[0][0] * C + piece[0][1] * P

@@ -4,6 +4,7 @@ import concourse.mybir as mybir
 from concourse.masks import make_identity
 
 K, T, E, C, H, N, HOT, TOP = 512, 512, 8, 256, 512, 256, 2, 4
+COLD = E - HOT
 S = E * C
 FLOPS = 2 * S * (2 * K * H + H * N)
 
@@ -20,8 +21,9 @@ ADD = mybir.AluOpType.add
 SIGMOID = mybir.ActivationFunctionType.Sigmoid
 
 P = 128
-ASIDE = 3
-AHEAD = 0
+HALF = T // 2
+COLD_PIECE = 3
+HOT_PIECE = 2
 
 
 def tile_moe_hot_glu_sigmoid_kernel(
@@ -29,18 +31,18 @@ def tile_moe_hot_glu_sigmoid_kernel(
     w1c_words, w1c_scales, w3c_words, w3c_scales, w2c_words, w2c_scales, gate, offs, pos1, pos2, pos3, pos4, out,
 ):
     nc = tc.nc
-    COLD = E - HOT
     with ExitStack() as ctx:
         keep = ctx.enter_context(tc.tile_pool(name="keep", bufs=1))
         psum = ctx.enter_context(tc.psum_pool(name="psum", bufs=1))
 
-        def plane_tile(name, experts, width, engine):
+
+        def zeroed_plane(name, experts, width, engine):
             plane = keep.tile([P, experts, width], U8, name=name, align_bytes=64)
             engine.memset(plane[:].bitcast(I32), 0)
             return plane
 
         def load_plane(plane, scales):
-            rows = scales.rearrange("f (q r) c -> r q f c", r=4)
+            rows = scales[:, 0].rearrange("f (q r) c -> r q f c", r=4)
             for r in range(4):
                 nc.sync.dma_start(out=plane[r:P:32, :, :].bitcast(I32), in_=rows[r].bitcast(I32))
 
@@ -49,55 +51,56 @@ def tile_moe_hot_glu_sigmoid_kernel(
             nc.sync.dma_start(out=tile[:].bitcast(I32), in_=words.bitcast(I32))
             return tile
 
-        def cold_words(words, a, b):
-            return words[a:b, 0].rearrange("f p c -> p f c")
+        def cold_words(words, first, last):
+            return words[first:last, 0].rearrange("f p c -> p f c")
 
         def hot_words(words):
             return words[:, 0].rearrange("f p n t -> p f (n t)")
 
         xs = keep.tile([P, T], U8, name="xs", align_bytes=64)
         xw = keep.tile([P, T], I32, name="xw", align_bytes=64)
-        s1h = plane_tile("s1h", HOT, H, nc.vector)
-        s3h = plane_tile("s3h", HOT, H, nc.gpsimd)
-        s1c = plane_tile("s1c", COLD, H, nc.vector)
-        s3c = plane_tile("s3c", COLD, H, nc.gpsimd)
-        s2h = plane_tile("s2h", HOT, N, nc.vector)
-        s2c = plane_tile("s2c", COLD, N, nc.vector)
+        s1h = zeroed_plane("s1h", HOT, H, nc.vector)
+        s3h = zeroed_plane("s3h", HOT, H, nc.gpsimd)
+        s1c = zeroed_plane("s1c", COLD, H, nc.vector)
+        s3c = zeroed_plane("s3c", COLD, H, nc.gpsimd)
+        s2h = zeroed_plane("s2h", HOT, N, nc.vector)
+        s2c = zeroed_plane("s2c", COLD, N, nc.vector)
         ident = keep.tile([P, P], F32, name="ident")
         make_identity(nc, ident[:])
 
         offs_t = keep.tile([P, S // 16], U16, name="offs_t")
-        nc.sync.dma_start(out=xw[:, 0:T], in_=x_words[0].rearrange("p t d -> p (t d)").bitcast(I32))
+        nc.sync.dma_start(out=xw[:], in_=x_words[0].rearrange("p t d -> p (t d)").bitcast(I32))
         x_rows = x_scales[0].rearrange("(q r) c -> r q c", r=4)
         for r in range(4):
-            nc.sync.dma_start(out=xs[r:P:4, 0:T].bitcast(I32), in_=x_rows[r].bitcast(I32).unsqueeze(1).to_broadcast([4, 8, T // 4]))
+            nc.sync.dma_start(out=xs[r:P:4, :].bitcast(I32), in_=x_rows[r].bitcast(I32).unsqueeze(1).to_broadcast([4, 8, T // 4]))
         nc.sync.dma_start(offs_t[:], offs)
-        w1t, w3t = {}, {}
+
+        w1, w3 = {}, {}
 
         def load_hot(table, name, words, plane):
             tile = load_words(name, hot_words(words))
             for f in range(HOT):
                 table[f] = (tile[:, f, :].bitcast(FP8X4), plane[:, f, :])
 
-        def load_cold(table, name, words, plane, a, b):
-            tile = load_words(f"{name}{a}", cold_words(words, a, b))
-            for f in range(a, b):
-                table[HOT + f] = (tile[:, f - a, :].bitcast(FP4X4), plane[:, f, :])
+        def load_cold_pair(table, name, words, plane, first):
+            tile = load_words(f"{name}{first}", cold_words(words, first, first + 2))
+            for f in range(2):
+                table[HOT + first + f] = (tile[:, f, :].bitcast(FP4X4), plane[:, first + f, :])
 
-        load_cold(w1t, "w1c", w1c_words, s1c, 0, 2)
-        load_plane(s1c, w1c_scales[:, 0])
-        load_plane(s1h, w1h_scales[:, 0])
-        load_cold(w1t, "w1c", w1c_words, s1c, 2, 4)
-        load_cold(w1t, "w1c", w1c_words, s1c, 4, COLD)
-        load_plane(s3c, w3c_scales[:, 0])
-        load_plane(s3h, w3h_scales[:, 0])
-        load_cold(w3t, "w3c", w3c_words, s3c, 4, COLD)
-        load_hot(w1t, "w1h", w1h_words, s1h)
-        load_cold(w3t, "w3c", w3c_words, s3c, 0, 2)
-        load_cold(w3t, "w3c", w3c_words, s3c, 2, 4)
-        load_hot(w3t, "w3h", w3h_words, s3h)
-        load_plane(s2c, w2c_scales[:, 0])
-        load_plane(s2h, w2h_scales[:, 0])
+        load_cold_pair(w1, "w1c", w1c_words, s1c, 0)
+        load_plane(s1c, w1c_scales)
+        load_plane(s1h, w1h_scales)
+        load_cold_pair(w1, "w1c", w1c_words, s1c, 2)
+        load_cold_pair(w1, "w1c", w1c_words, s1c, 4)
+        load_plane(s3c, w3c_scales)
+        load_plane(s3h, w3h_scales)
+        load_cold_pair(w3, "w3c", w3c_words, s3c, 4)
+        load_cold_pair(w3, "w3c", w3c_words, s3c, 2)
+        load_cold_pair(w3, "w3c", w3c_words, s3c, 0)
+        load_hot(w1, "w1h", w1h_words, s1h)
+        load_hot(w3, "w3h", w3h_words, s3h)
+        load_plane(s2c, w2c_scales)
+        load_plane(s2h, w2h_scales)
         w2c = load_words("w2c", cold_words(w2c_words, 0, COLD))
         w2h = load_words("w2h", hot_words(w2h_words))
 
@@ -117,88 +120,101 @@ def tile_moe_hot_glu_sigmoid_kernel(
         y = [keep.tile([P, S], F32, name=f"y{b}") for b in range(N // P)]
 
         banks = [psum.tile([P, H], F32, name=f"bank{k}") for k in range(8)]
-        experts = list(range(HOT, E)) + list(range(HOT))
-        tiles = [(e, j) for e in experts for j in range(2)]
+        low, high = banks[:4], banks[4:]
+        low_uses = []
+
+        def next_low():
+            low_uses.append(low[len(low_uses) % 4])
+            return low_uses[-1]
+
+        def slot_tiles(experts):
+            return [(e, j) for e in experts for j in range(2)]
+
+        pair_a, pair_b, pair_c = [[HOT + f, HOT + f + 1] for f in range(0, COLD, 2)]
+        pair_hot = list(range(HOT))
+        cold_tiles, hot_tiles = slot_tiles(pair_a + pair_b + pair_c), slot_tiles(pair_hot)
+
 
         tokens = {}
-        cuts = (0, 3, 6, 9, 12, 14, 16)
-        pieces = [tiles[a:z] for a, z in zip(cuts, cuts[1:])]
+        pieces = [cold_tiles[k : k + COLD_PIECE] for k in range(0, len(cold_tiles), COLD_PIECE)]
+        pieces = pieces + [hot_tiles[k : k + HOT_PIECE] for k in range(0, len(hot_tiles), HOT_PIECE)]
         for n, piece in enumerate(pieces):
-            first = piece[0][0] * C + piece[0][1] * P
-            lst = offs_t[:, first // 16 : (first + len(piece) * P) // 16]
+            slot = piece[0][0] * C + piece[0][1] * P
+            entries = offs_t[:, slot // 16 : (slot + len(piece) * P) // 16]
             gw = keep.tile([P, len(piece) * P], U32, name=f"gw{n}", align_bytes=64)
             gs = keep.tile([P, len(piece) * P], U8, name=f"gs{n}", align_bytes=64)
-            nc.vector.tensor_copy(gw[:], xw[:].bitcast(U32).indirect(lst))
-            nc.vector.tensor_copy(gs[:], xs[:].indirect(lst))
+            nc.vector.tensor_copy(gw[:], xw[:].bitcast(U32).indirect(entries))
+            nc.vector.tensor_copy(gs[:], xs[:].indirect(entries))
             for k, tile in enumerate(piece):
                 tokens[tile] = (gw[:, k * P : (k + 1) * P].bitcast(FP8X4), gs[:, k * P : (k + 1) * P])
 
         def first_layer(bank, tile, table):
-            (words, scales), (w, s) = tokens[tile], table[tile[0]]
-            nc.tensor.matmul_mx(out=bank[:], lhsT=words, lhsT_scale=scales, rhs=w, rhs_scale=s, start=True, stop=True)
+            (words, scales), (w, plane) = tokens[tile], table[tile[0]]
+            nc.tensor.matmul_mx(out=bank[:], lhsT=words, lhsT_scale=scales, rhs=w, rhs_scale=plane, start=True, stop=True)
             return bank[:].rearrange("s (q u d) -> s u q d", u=2, d=2)
 
-        def in_order(tile):
+        def uqd(tile):
             return tile[:].rearrange("s (u q d) -> s u q d", u=2, d=2)
+
+        def sig_name(tile):
+            return f"sig{tile[0]}{tile[1]}"
 
         sigs = {}
 
-        def sigmoid(i, bank):
-            a1 = first_layer(bank, tiles[i], w1t)
-            sig = keep.tile([P, H], F32, name=f"sig{i}", align_bytes=64)
-            nc.scalar.activation(in_order(sig), a1, SIGMOID)
-            sigs[tiles[i]] = sig
+        def sigmoid(tile, bank):
+            a1 = first_layer(bank, tile, w1)
+            sig = keep.tile([P, H], F32, name=sig_name(tile), align_bytes=64)
+            nc.scalar.activation(uqd(sig), a1, SIGMOID)
+            sigs[tile] = sig
 
-        order = experts[4:6] + experts[0:2] + experts[6:8] + experts[2:4]
+        places = slot_tiles(pair_c + pair_a + pair_hot + pair_b)
+        on_vector = len(places) - len(slot_tiles(pair_b))
         hidden = {}
-        turned = keep.tile([P, 2 * E * H], BF16, name="turned", align_bytes=64)
+        turned = keep.tile([P, len(places) * H], BF16, name="turned", align_bytes=64)
 
-        rounds = []
+        for tile in cold_tiles:
+            sigmoid(tile, high[slot_tiles(pair_b).index(tile)] if tile[0] in pair_b else next_low())
 
-        def low_bank():
-            rounds.append(None)
-            return banks[(len(rounds) - 1) % 4]
 
-        aside = tiles[8 - ASIDE : 8]
+        for place in range(on_vector, len(places)):
+            a3 = first_layer(next_low(), places[place], w3)
+            plain = keep.tile([P, H], F32, name=f"plain{place}")
+            nc.scalar.copy(uqd(plain), a3)
+            hb = keep.tile([P, H], BF16, name=f"hb{place}")
+            nc.gpsimd.tensor_tensor(hb[:], plain[:], sigs[places[place]][:], MULT)
+            hidden[place] = hb
+        for tile in hot_tiles:
+            sigmoid(tile, next_low())
 
-        def product_aside(i):
-            a3 = first_layer(low_bank(), aside[i], w3t)
-            plain = keep.tile([P, H], F32, name=f"plain{i}")
-            nc.scalar.copy(in_order(plain), a3)
-            hb = keep.tile([P, H], BF16, name=f"aside{i}")
-            nc.gpsimd.tensor_tensor(hb[:], plain[:], sigs[aside[i]][:], MULT)
-            hidden[2 * order.index(aside[i][0]) + aside[i][1]] = hb
+        def product(place):
+            a3 = first_layer(high[place % 4], places[place], w3)
+            hb = keep.tile([P, H], BF16, name=f"hb{place}")
+            nc.vector.tensor_tensor(uqd(hb), a3, uqd(sigs[places[place]]), MULT)
+            hidden[place] = hb
 
-        for i in range(14):
-            sigmoid(i, banks[i] if i // 4 == 1 else low_bank())
-        for i in range(AHEAD):
-            product_aside(i)
-        for i in range(14, 16):
-            sigmoid(i, low_bank())
-        for i in range(AHEAD, ASIDE):
-            product_aside(i)
-        made = []
-
-        def products(i):
-            for j in range(2):
-                tile = (order[i], j)
-                if tile not in aside:
-                    a3 = first_layer(banks[4 + len(made) % 4], tile, w3t)
-                    hb = keep.tile([P, H], BF16, name=f"hb{2 * i + j}")
-                    nc.vector.tensor_tensor(in_order(hb), a3, in_order(sigs[tile]), MULT)
-                    hidden[2 * i + j] = hb
-                    made.append(tile)
-
-        def turn(first, last, *into):
-            n = (last - first) // len(into)
-            across = [bank[:, 0 : n * C].rearrange("q (j u s) -> q j u s", j=n, u=2) for bank in into]
-            for i in reversed(range(first, last)):
-                words = hidden[i][:].bitcast(F32)
+        def turn(first, last):
+            n = last - first
+            across = next_low()[:, 0 : n * 2 * P].rearrange("q (j u s) -> q j u s", j=n, u=2)
+            for place in reversed(range(first, last)):
+                pairs = hidden[place][:].bitcast(F32)
                 for u in range(2):
-                    nc.tensor.transpose(across[(i - first) // n][:, (i - first) % n, u, :], words[:, u * P : (u + 1) * P], ident[:])
-            for k in reversed(range(len(into))):
-                dst = turned[:, (first + k * n) * H : (first + (k + 1) * n) * H].bitcast(F32).rearrange("q (j s u) -> q j s u", j=n, u=2)
-                nc.scalar.copy(dst, across[k].rearrange("q j u s -> q j s u"))
+                    nc.tensor.transpose(across[:, place - first, u, :], pairs[:, u * P : (u + 1) * P], ident[:])
+            dst = turned[:, first * H : last * H].bitcast(F32).rearrange("q (j s u) -> q j s u", j=n, u=2)
+            nc.scalar.copy(dst, across.rearrange("q j u s -> q j s u"))
+
+        span_c, span_a, span_b = (0, 4), (4, 8), (12, 16)
+        hot_first, hot_second = (8, 10), (10, 12)
+        for place in range(0, on_vector, 2):
+            product(place)
+            product(place + 1)
+            if place < hot_first[0]:
+                turn(place, place + 2)
+        for place in range(*span_b, 2):
+            turn(place, place + 2)
+        turn(*hot_first)
+        for place in range(*hot_second):
+            turn(place, place + 1)
+
 
         codes = {}
 
@@ -207,72 +223,70 @@ def tile_moe_hot_glu_sigmoid_kernel(
             hs = keep.tile([P, (last - first) * P], U8, name=f"hs{first}", align_bytes=64)
             nc.vector.quantize_mx(out=hq[:].bitcast(FP8X4), scales=hs[:], in_=turned[:, first * H : last * H])
             step = min(2, last - first)
-            for i in range(first, last, step):
-                cols = slice((i - first) * P, (i - first + step) * P)
-                codes[i] = (hq[:, cols].bitcast(FP8X4), hs[:, cols], step)
+            for place in range(first, last, step):
+                cols = slice((place - first) * P, (place - first + step) * P)
+                codes[place] = (hq[:, cols].bitcast(FP8X4), hs[:, cols], step)
 
         def second_layer(bank, b, first, last, copy):
-            i = first
-            while i < last:
-                hq, hs, step = codes[i]
-                w, s = w2_block(order[i // 2], b)
-                nc.tensor.matmul_mx(out=bank[:, (i - first) * P : (i - first + step) * P], lhsT=w, lhsT_scale=s, rhs=hq, rhs_scale=hs, start=True, stop=True)
-                i = i + step
-            slot = order[first // 2] * C + first % 2 * P
+            for place in range(first, last):
+                if place in codes:
+                    hq, hs, step = codes[place]
+                    w, plane = w2_block(places[place][0], b)
+                    acc = bank[:, (place - first) * P : (place - first + step) * P]
+                    nc.tensor.matmul_mx(out=acc, lhsT=w, lhsT_scale=plane, rhs=hq, rhs_scale=hs, start=True, stop=True)
+            slot = places[first][0] * C + places[first][1] * P
             copy(y[b][:, slot : slot + (last - first) * P], bank[:, 0 : (last - first) * P])
 
+        quantise(*span_c, sig_name(places[on_vector - 2]))
+        quantise(*span_a, sig_name(places[on_vector - 1]))
+        quantise(*span_b, sig_name(places[on_vector - 3]))
+        quantise(*hot_first, "hq_hot_first")
+        for place in range(*hot_second):
+            quantise(place, place + 1, f"hq{place}")
+        second_layer(high[0], 0, *span_c, nc.scalar.copy)
+        second_layer(high[1], 0, *span_a, nc.scalar.copy)
+        second_layer(high[2], 0, *span_b, nc.vector.tensor_copy)
+        second_layer(high[3], 0, *hot_first, nc.vector.tensor_copy)
+        last_bank = next_low()
+        second_layer(last_bank, 0, *hot_second, nc.scalar.copy)
+
+
+        for k, first in enumerate(range(0, len(places), 4)):
+            second_layer((last_bank, high[3])[k % 2], 1, first, first + 4, nc.scalar.copy)
+
         chunks = T // P
-        for i in range(E):
-            products(i)
-            if i < E - 2:
-                turn(2 * i, 2 * i + 2, low_bank())
-        turn(14, 16, low_bank())
-        turn(13, 14, low_bank())
-        turn(12, 13, low_bank())
-        for first, last, name in ((0, 4, "sig15"), (4, 8, "sig4"), (8, 12, "sig14"), (14, 16, "hq14"), (13, 14, "hq13"), (12, 13, "hq12")):
-            quantise(first, last, name)
-        second_layer(banks[5], 0, 0, 4, nc.scalar.copy)
-        second_layer(banks[6], 0, 4, 8, nc.scalar.copy)
-        second_layer(banks[7], 0, 8, 12, nc.vector.tensor_copy)
-        second_layer(banks[4], 0, 14, 16, nc.vector.tensor_copy)
-        last = low_bank()
-        second_layer(last, 0, 12, 14, nc.scalar.copy)
-        for pair in range(4):
-            second_layer((last, banks[4])[pair % 2], 1, 4 * pair, 4 * pair + 4, nc.scalar.copy)
 
-        half = T // 2
+        def pick(dst, b, r, cols):
+            entries = pos_t[r][:, cols.start // 16 : cols.stop // 16]
+            nc.vector.tensor_tensor(dst[:, cols], y[b][:].indirect(entries), gate_t[:, r, cols], MULT)
 
-        def product(dst, b, r, cols):
-            lst = pos_t[r][:, cols.start // 16 : cols.stop // 16]
-            nc.vector.tensor_tensor(dst[:, cols], y[b][:].indirect(lst), gate_t[:, r, cols], MULT)
-
-        def turned_sum(b, lists):
-            across = [banks[c][:, 0:P] for c in range(chunks)]
+        def turned_sum(b, lists, last_parts):
             for r in range(lists):
                 picked = keep.tile([P, T], F32, name=f"picked{b}{r}")
-                pieces = 2 if (b, r) == (1, lists - 1) else 1
-                for k in range(pieces):
-                    product(picked, b, r, slice(k * T // pieces, (k + 1) * T // pieces))
+                parts = last_parts if r == lists - 1 else 1
+                for k in range(parts):
+                    pick(picked, b, r, slice(k * T // parts, (k + 1) * T // parts))
                 for c in range(chunks):
-                    nc.tensor.matmul(across[c][:], picked[:, c * P : (c + 1) * P], ident[:], start=(r == 0), stop=(r == lists - 1), is_transpose=True)
-            halves = [banks[4 + 2 * b + k][:, 0:half] for k in range(2)]
+                    nc.tensor.matmul(low[c][:, 0:P], picked[:, c * P : (c + 1) * P], ident[:], start=(r == 0), stop=(r == lists - 1), is_transpose=True)
+            halves = [high[2 * b + k][:, 0:HALF] for k in range(2)]
             for c in range(chunks):
                 summed = keep.tile([P, P], F32, name=f"summed{b}{c}")
-                nc.scalar.copy(summed[:], across[c][:])
+                nc.scalar.copy(summed[:], low[c][:, 0:P])
                 nc.tensor.transpose(halves[c // 2][:, (c % 2) * P : (c % 2 + 1) * P], summed[:], ident[:])
             return halves
 
-        acc0 = turned_sum(0, TOP)
+        sums = turned_sum(0, TOP, 1)
         res0 = keep.tile([P, T], F32, name="res0")
         for k in range(2):
-            nc.scalar.copy(res0[:, k * half : (k + 1) * half], acc0[k][:])
+            nc.scalar.copy(res0[:, k * HALF : (k + 1) * HALF], sums[k])
         nc.sync.dma_start(out=out[0:P, :], in_=res0[:])
-        acc1 = turned_sum(1, TOP - 1)
-        part = keep.tile([P, T], F32, name="part")
+
+        sums = turned_sum(1, TOP - 1, 2)
+        fourth = keep.tile([P, T], F32, name="fourth")
         for k in range(2):
-            product(part, 1, TOP - 1, slice(k * half, (k + 1) * half))
+            pick(fourth, 1, TOP - 1, slice(k * HALF, (k + 1) * HALF))
         for k in range(2):
-            cols = slice(k * half, (k + 1) * half)
-            res = keep.tile([P, half], F32, name=f"res1{k}")
-            nc.vector.tensor_tensor(res[:], acc1[k][:], part[:, cols], ADD)
-            nc.sync.dma_start(out=out[P : 2 * P, cols], in_=res[:])
+            cols = slice(k * HALF, (k + 1) * HALF)
+            res1 = keep.tile([P, HALF], F32, name=f"res1{k}")
+            nc.vector.tensor_tensor(res1[:], sums[k], fourth[:, cols], ADD)
+            nc.sync.dma_start(out=out[P : 2 * P, cols], in_=res1[:])

@@ -70,9 +70,9 @@ def tile_moe_hot_glu_sigmoid_kernel(
 
         offs_t = keep.tile([P, S // 16], U16, name="offs_t")
         nc.sync.dma_start(out=xw[:], in_=x_words[0].rearrange("p t d -> p (t d)").bitcast(I32))
-        x_rows = x_scales[0].rearrange("(q r) c -> r q c", r=4)
-        for r in range(4):
-            nc.sync.dma_start(out=xs[r:P:4, :].bitcast(I32), in_=x_rows[r].bitcast(I32).unsqueeze(1).to_broadcast([4, 8, T // 4]))
+        for q in range(4):
+            rows = x_scales[0, 4 * q : 4 * q + 4].bitcast(I32)
+            nc.sync.dma_start(out=xs[32 * q : 32 * q + 32, :].bitcast(I32), in_=rows.unsqueeze(0).to_broadcast([8, 4, T // 4]))
         nc.sync.dma_start(offs_t[:], offs)
 
         w1, w3 = {}, {}
@@ -246,13 +246,12 @@ def tile_moe_hot_glu_sigmoid_kernel(
         second_layer(high[0], 0, *span_c, nc.scalar.copy)
         second_layer(high[1], 0, *span_a, nc.scalar.copy)
         second_layer(high[2], 0, *span_b, nc.vector.tensor_copy)
-        second_layer(high[3], 0, *hot_first, nc.vector.tensor_copy)
-        last_bank = next_low()
-        second_layer(last_bank, 0, *hot_second, nc.scalar.copy)
+        second_layer(high[3], 0, *hot_first, nc.scalar.copy)
+        second_layer(next_low(), 0, *hot_second, nc.scalar.copy)
 
 
-        for k, first in enumerate(range(0, len(places), 4)):
-            second_layer((last_bank, high[3])[k % 2], 1, first, first + 4, nc.scalar.copy)
+        for bank, first in zip(high, range(0, len(places), 4)):
+            second_layer(bank, 1, first, first + 4, nc.scalar.copy)
 
         chunks = T // P
 

@@ -41,9 +41,9 @@ def tile_moe_hot_glu_sigmoid_kernel(
             engine.memset(plane[:].bitcast(I32), 0)
             return plane
 
-        def load_plane(plane, scales):
+        def load_plane(plane, scales, which=range(4)):
             rows = scales[:, 0].rearrange("f (q r) c -> r q f c", r=4)
-            for r in range(4):
+            for r in which:
                 nc.sync.dma_start(out=plane[r:P:32, :, :].bitcast(I32), in_=rows[r].bitcast(I32))
 
         def load_words(name, words):
@@ -59,12 +59,12 @@ def tile_moe_hot_glu_sigmoid_kernel(
 
         xs = keep.tile([P, T], U8, name="xs", align_bytes=64)
         xw = keep.tile([P, T], I32, name="xw", align_bytes=64)
-        s1h = zeroed_plane("s1h", HOT, H, nc.vector)
-        s3h = zeroed_plane("s3h", HOT, H, nc.gpsimd)
         s1c = zeroed_plane("s1c", COLD, H, nc.vector)
         s3c = zeroed_plane("s3c", COLD, H, nc.gpsimd)
-        s2h = zeroed_plane("s2h", HOT, N, nc.vector)
+        s1h = zeroed_plane("s1h", HOT, H, nc.vector)
+        s3h = zeroed_plane("s3h", HOT, H, nc.gpsimd)
         s2c = zeroed_plane("s2c", COLD, N, nc.vector)
+        s2h = zeroed_plane("s2h", HOT, N, nc.vector)
         ident = keep.tile([P, P], F32, name="ident")
         make_identity(nc, ident[:])
 
@@ -89,17 +89,29 @@ def tile_moe_hot_glu_sigmoid_kernel(
 
         load_cold_pair(w1, "w1c", w1c_words, s1c, 0)
         load_plane(s1c, w1c_scales)
-        load_plane(s1h, w1h_scales)
-        load_cold_pair(w1, "w1c", w1c_words, s1c, 2)
-        load_cold_pair(w1, "w1c", w1c_words, s1c, 4)
         load_plane(s3c, w3c_scales)
-        load_plane(s3h, w3h_scales)
-        load_cold_pair(w3, "w3c", w3c_words, s3c, 4)
+        load_cold_pair(w1, "w1c", w1c_words, s1c, 2)
         load_cold_pair(w3, "w3c", w3c_words, s3c, 2)
         load_cold_pair(w3, "w3c", w3c_words, s3c, 0)
-        load_hot(w1, "w1h", w1h_words, s1h)
-        load_hot(w3, "w3h", w3h_words, s3h)
-        load_plane(s2c, w2c_scales)
+
+        def load_cold(table, name, words, plane, f):
+            tile = load_words(f"{name}{f}", cold_words(words, f, f + 1))
+            table[HOT + f] = (tile[:, 0, :].bitcast(FP4X4), plane[:, f, :])
+
+        def load_one_hot(table, name, words, plane, f):
+            tile = load_words(f"{name}{f}", hot_words(words)[:, f : f + 1, :])
+            table[f] = (tile[:, 0, :].bitcast(FP8X4), plane[:, f, :])
+
+        load_cold_pair(w1, "w1c", w1c_words, s1c, 4)
+        load_cold_pair(w3, "w3c", w3c_words, s3c, 4)
+        load_plane(s1h, w1h_scales)
+        load_plane(s3h, w3h_scales)
+        load_one_hot(w1, "w1h", w1h_words, s1h, 0)
+        load_one_hot(w3, "w3h", w3h_words, s3h, 0)
+        load_one_hot(w1, "w1h", w1h_words, s1h, 1)
+        load_plane(s2c, w2c_scales, range(1))
+        load_one_hot(w3, "w3h", w3h_words, s3h, 1)
+        load_plane(s2c, w2c_scales, range(1, 4))
         load_plane(s2h, w2h_scales)
         w2c = load_words("w2c", cold_words(w2c_words, 0, COLD))
         w2h = load_words("w2h", hot_words(w2h_words))
@@ -138,15 +150,19 @@ def tile_moe_hot_glu_sigmoid_kernel(
         tokens = {}
         pieces = [cold_tiles[k : k + COLD_PIECE] for k in range(0, len(cold_tiles), COLD_PIECE)]
         pieces = pieces + [hot_tiles[k : k + HOT_PIECE] for k in range(0, len(hot_tiles), HOT_PIECE)]
-        for n, piece in enumerate(pieces):
+
+        def gather(piece, words_name, scales_name):
             slot = piece[0][0] * C + piece[0][1] * P
             entries = offs_t[:, slot // 16 : (slot + len(piece) * P) // 16]
-            gw = keep.tile([P, len(piece) * P], U32, name=f"gw{n}", align_bytes=64)
-            gs = keep.tile([P, len(piece) * P], U8, name=f"gs{n}", align_bytes=64)
+            gw = keep.tile([P, len(piece) * P], U32, name=words_name, align_bytes=64)
+            gs = keep.tile([P, len(piece) * P], U8, name=scales_name, align_bytes=64)
             nc.vector.tensor_copy(gw[:], xw[:].bitcast(U32).indirect(entries))
             nc.vector.tensor_copy(gs[:], xs[:].indirect(entries))
             for k, tile in enumerate(piece):
                 tokens[tile] = (gw[:, k * P : (k + 1) * P].bitcast(FP8X4), gs[:, k * P : (k + 1) * P])
+
+        for n, piece in enumerate(pieces[:4]):
+            gather(piece, f"gw{n}", f"gs{n}")
 
         def first_layer(bank, tile, table):
             (words, scales), (w, plane) = tokens[tile], table[tile[0]]
@@ -167,24 +183,22 @@ def tile_moe_hot_glu_sigmoid_kernel(
             nc.scalar.activation(uqd(sig), a1, SIGMOID)
             sigs[tile] = sig
 
-        places = slot_tiles(pair_c + pair_a + pair_hot + pair_b)
+        places = slot_tiles(pair_a + pair_c + pair_hot + pair_b)
         on_vector = len(places) - len(slot_tiles(pair_b))
         hidden = {}
         turned = keep.tile([P, len(places) * H], BF16, name="turned", align_bytes=64)
 
-        for tile in cold_tiles:
-            sigmoid(tile, high[slot_tiles(pair_b).index(tile)] if tile[0] in pair_b else next_low())
-
-
-        for place in range(on_vector, len(places)):
-            a3 = first_layer(next_low(), places[place], w3)
-            plain = keep.tile([P, H], F32, name=f"plain{place}")
-            nc.scalar.copy(uqd(plain), a3)
-            hb = keep.tile([P, H], BF16, name=f"hb{place}")
-            nc.gpsimd.tensor_tensor(hb[:], plain[:], sigs[places[place]][:], MULT)
-            hidden[place] = hb
-        for tile in hot_tiles:
+        for tile in cold_tiles[:6]:
             sigmoid(tile, next_low())
+
+
+        plains = {}
+
+        def lend(place):
+            a3 = first_layer(next_low(), places[place], w3)
+            plain = keep.tile([P, H], F32, name=f"plain{place}", align_bytes=64)
+            nc.scalar.copy(uqd(plain), a3)
+            plains[place] = plain
 
         def product(place):
             a3 = first_layer(high[place % 4], places[place], w3)
@@ -192,28 +206,58 @@ def tile_moe_hot_glu_sigmoid_kernel(
             nc.vector.tensor_tensor(uqd(hb), a3, uqd(sigs[places[place]]), MULT)
             hidden[place] = hb
 
-        def turn(first, last):
+        def turn(first, last, bank, copy=nc.scalar.copy):
             n = last - first
-            across = next_low()[:, 0 : n * 2 * P].rearrange("q (j u s) -> q j u s", j=n, u=2)
-            for place in reversed(range(first, last)):
+            across = bank[:, 0 : n * 2 * P].rearrange("q (j u s) -> q j u s", j=n, u=2)
+            for place in range(first, last) if first == on_vector else reversed(range(first, last)):
                 pairs = hidden[place][:].bitcast(F32)
                 for u in range(2):
                     nc.tensor.transpose(across[:, place - first, u, :], pairs[:, u * P : (u + 1) * P], ident[:])
             dst = turned[:, first * H : last * H].bitcast(F32).rearrange("q (j s u) -> q j s u", j=n, u=2)
-            nc.scalar.copy(dst, across.rearrange("q j u s -> q j s u"))
+            copy(dst, across.rearrange("q j u s -> q j s u"))
 
         span_c, span_a, span_b = (0, 4), (4, 8), (12, 16)
         hot_first, hot_second = (8, 10), (10, 12)
-        for place in range(0, on_vector, 2):
+        lend(12)
+        lend(13)
+        sigmoid(cold_tiles[6], next_low())
+        sigmoid(cold_tiles[7], next_low())
+        lend(14)
+        lend(15)
+
+        def lent_product(place, name):
+            hidden[place] = keep.tile([P, H], BF16, name=name, align_bytes=64)
+            nc.gpsimd.tensor_tensor(hidden[place][:], plains[place][:], sigs[places[place]][:], MULT)
+
+        lent_product(13, "hb13")
+        for place in range(4):
             product(place)
-            product(place + 1)
-            if place < hot_first[0]:
-                turn(place, place + 2)
-        for place in range(*span_b, 2):
-            turn(place, place + 2)
-        turn(*hot_first)
+        gather(pieces[4], sig_name(places[0]), sig_name(places[1]))
+        gather(pieces[5], sig_name(places[2]), sig_name(places[3]))
+        sigmoid(cold_tiles[8], next_low())
+        sigmoid(cold_tiles[9], next_low())
+        turn(0, 2, next_low())
+        sigmoid(cold_tiles[10], next_low())
+        sigmoid(cold_tiles[11], next_low())
+        lent_product(12, "w1c4")
+        lent_product(14, "plain12")
+        lent_product(15, sig_name(places[12]))
+        turn(2, 4, next_low(), nc.vector.tensor_copy)
+        sigmoid(hot_tiles[0], next_low())
+        sigmoid(hot_tiles[1], next_low())
+        sigmoid(hot_tiles[2], next_low())
+        sigmoid(hot_tiles[3], next_low())
+        for place in range(4, hot_second[0]):
+            product(place)
+        turn(4, 6, low[2])
+        turn(12, 14, low[3])
         for place in range(*hot_second):
-            turn(place, place + 1)
+            product(place)
+        turn(6, 8, low[0])
+        turn(14, 16, low[1])
+        turn(8, 10, high[0])
+        turn(10, 11, high[1])
+        turn(11, 12, high[2])
 
 
         codes = {}
@@ -241,16 +285,16 @@ def tile_moe_hot_glu_sigmoid_kernel(
         quantise(*span_a, sig_name(places[on_vector - 1]))
         quantise(*span_b, sig_name(places[on_vector - 3]))
         quantise(*hot_first, "hq_hot_first")
-        for place in range(*hot_second):
-            quantise(place, place + 1, f"hq{place}")
-        second_layer(high[0], 0, *span_c, nc.scalar.copy)
-        second_layer(high[1], 0, *span_a, nc.scalar.copy)
-        second_layer(high[2], 0, *span_b, nc.vector.tensor_copy)
-        second_layer(high[3], 0, *hot_first, nc.scalar.copy)
-        second_layer(next_low(), 0, *hot_second, nc.scalar.copy)
+        quantise(10, 11, "hq10")
+        quantise(11, 12, "hq11")
+        second_layer(low[1], 0, *span_c, nc.scalar.copy)
+        second_layer(high[3], 0, *span_a, nc.scalar.copy)
+        second_layer(low[2], 0, *span_b, nc.vector.tensor_copy)
+        second_layer(low[3], 0, *hot_first, nc.scalar.copy)
+        second_layer(low[0], 0, *hot_second, nc.scalar.copy)
 
 
-        for bank, first in zip(high, range(0, len(places), 4)):
+        for bank, first in zip((high[1], high[0], high[2], high[3]), (8, 12, 0, 4)):
             second_layer(bank, 1, first, first + 4, nc.scalar.copy)
 
         chunks = T // P

@@ -61,8 +61,7 @@ def tile_moe_hot_glu_sigmoid_kernel(
         xw = keep.tile([P, T], I32, name="xw", align_bytes=64)
         s1c = zeroed_plane("s1c", COLD, H, nc.vector)
         s3c = zeroed_plane("s3c", COLD, H, nc.gpsimd)
-        s1h = zeroed_plane("s1h", HOT, H, nc.vector)
-        s3h = zeroed_plane("s3h", HOT, H, nc.gpsimd)
+        sh_raw = zeroed_plane("sh_raw", 1, H, nc.vector)
         s2c = zeroed_plane("s2c", COLD, N, nc.vector)
         s2h = zeroed_plane("s2h", HOT, N, nc.vector)
         ident = keep.tile([P, P], F32, name="ident")
@@ -77,11 +76,6 @@ def tile_moe_hot_glu_sigmoid_kernel(
 
         w1, w3 = {}, {}
 
-        def load_hot(table, name, words, plane):
-            tile = load_words(name, hot_words(words))
-            for f in range(HOT):
-                table[f] = (tile[:, f, :].bitcast(FP8X4), plane[:, f, :])
-
         def load_cold_pair(table, name, words, plane, first):
             tile = load_words(f"{name}{first}", cold_words(words, first, first + 2))
             for f in range(2):
@@ -90,31 +84,38 @@ def tile_moe_hot_glu_sigmoid_kernel(
         load_cold_pair(w1, "w1c", w1c_words, s1c, 0)
         load_plane(s1c, w1c_scales)
         load_plane(s3c, w3c_scales)
+
+        sh = keep.tile([P, H], U8, name="sh", align_bytes=64)
+
+        def load_one_hot(table, name, words, f, row):
+            raw = load_words(f"{name}{f}", hot_words(words)[:, f, :])
+            tile = keep.tile([P, H], I32, name=f"{name}{f}_by_t", align_bytes=64)
+            nc.gpsimd.tensor_copy(tile[:].rearrange("p (t q) -> p t q", t=4), raw[:].bitcast(I32).rearrange("p (q t) -> p t q", t=4))
+            table[f] = (tile, row)
+
+        def load_hot_rows(first, scales):
+            for q in range(4):
+                nc.sync.dma_start(
+                    out=sh_raw[32 * q + first : 32 * q + first + 8, 0, :].bitcast(I32),
+                    in_=scales[:, 0, 4 * q : 4 * q + 4, :].bitcast(I32),
+                )
+
+        load_one_hot(w1, "w1h", w1h_words, 0, 0)
+        load_one_hot(w3, "w3h", w3h_words, 0, 8)
         load_cold_pair(w1, "w1c", w1c_words, s1c, 2)
         load_cold_pair(w3, "w3c", w3c_words, s3c, 2)
         load_cold_pair(w3, "w3c", w3c_words, s3c, 0)
-
-        def load_cold(table, name, words, plane, f):
-            tile = load_words(f"{name}{f}", cold_words(words, f, f + 1))
-            table[HOT + f] = (tile[:, 0, :].bitcast(FP4X4), plane[:, f, :])
-
-        def load_one_hot(table, name, words, plane, f):
-            tile = load_words(f"{name}{f}", hot_words(words)[:, f : f + 1, :])
-            table[f] = (tile[:, 0, :].bitcast(FP8X4), plane[:, f, :])
-
         load_cold_pair(w1, "w1c", w1c_words, s1c, 4)
         load_cold_pair(w3, "w3c", w3c_words, s3c, 4)
-        load_plane(s1h, w1h_scales)
-        load_plane(s3h, w3h_scales)
-        load_one_hot(w1, "w1h", w1h_words, s1h, 0)
-        load_one_hot(w3, "w3h", w3h_words, s3h, 0)
-        load_one_hot(w1, "w1h", w1h_words, s1h, 1)
-        load_plane(s2c, w2c_scales, range(1))
-        load_one_hot(w3, "w3h", w3h_words, s3h, 1)
-        load_plane(s2c, w2c_scales, range(1, 4))
+        load_hot_rows(0, w1h_scales)
+        load_hot_rows(8, w3h_scales)
+        nc.gpsimd.tensor_copy(sh[:].rearrange("p (t q) -> p t q", t=4), sh_raw[:, 0, :].rearrange("p (q t) -> p t q", t=4))
+        load_one_hot(w1, "w1h", w1h_words, 1, 4)
+        load_one_hot(w3, "w3h", w3h_words, 1, 12)
+        load_plane(s2c, w2c_scales)
         load_plane(s2h, w2h_scales)
-        w2c = load_words("w2c", cold_words(w2c_words, 0, COLD))
         w2h = load_words("w2h", hot_words(w2h_words))
+        w2c = load_words("w2c", cold_words(w2c_words, 0, COLD))
 
         def w2_block(e, b):
             if e < HOT:
@@ -166,11 +167,20 @@ def tile_moe_hot_glu_sigmoid_kernel(
 
         def first_layer(bank, tile, table):
             (words, scales), (w, plane) = tokens[tile], table[tile[0]]
+            if tile[0] < HOT:
+                for t in range(4):
+                    cols = slice(t * P, (t + 1) * P)
+                    nc.tensor.matmul_mx(out=bank[:, cols], lhsT=w[:, cols].bitcast(FP8X4), lhsT_scale=sh[plane:P, cols],
+                                        rhs=words, rhs_scale=scales, start=True, stop=True)
+                return bank[:].rearrange("q (t s) -> q s t", t=4)
             nc.tensor.matmul_mx(out=bank[:], lhsT=words, lhsT_scale=scales, rhs=w, rhs_scale=plane, start=True, stop=True)
             return bank[:].rearrange("s (q u d) -> s u q d", u=2, d=2)
 
-        def uqd(tile):
-            return tile[:].rearrange("s (u q d) -> s u q d", u=2, d=2)
+        def uqd(ap):
+            return ap.rearrange("s (u q d) -> s u q d", u=2, d=2)
+
+        def like_sums(ap, tile):
+            return ap.rearrange("q (s t) -> q s t", t=4) if tile[0] < HOT else uqd(ap)
 
         def sig_name(tile):
             return f"sig{tile[0]}{tile[1]}"
@@ -180,13 +190,15 @@ def tile_moe_hot_glu_sigmoid_kernel(
         def sigmoid(tile, bank):
             a1 = first_layer(bank, tile, w1)
             sig = keep.tile([P, H], F32, name=sig_name(tile), align_bytes=64)
-            nc.scalar.activation(uqd(sig), a1, SIGMOID)
+            nc.scalar.activation(like_sums(sig[:], tile), a1, SIGMOID)
             sigs[tile] = sig
 
         places = slot_tiles(pair_a + pair_c + pair_hot + pair_b)
         on_vector = len(places) - len(slot_tiles(pair_b))
         hidden = {}
         turned = keep.tile([P, len(places) * H], BF16, name="turned", align_bytes=64)
+
+        hot_h = keep.tile([P, 4 * H], BF16, name="hot_h", align_bytes=64)
 
         for tile in cold_tiles[:6]:
             sigmoid(tile, next_low())
@@ -197,14 +209,18 @@ def tile_moe_hot_glu_sigmoid_kernel(
         def lend(place):
             a3 = first_layer(next_low(), places[place], w3)
             plain = keep.tile([P, H], F32, name=f"plain{place}", align_bytes=64)
-            nc.scalar.copy(uqd(plain), a3)
+            nc.scalar.copy(uqd(plain[:]), a3)
             plains[place] = plain
 
         def product(place):
-            a3 = first_layer(high[place % 4], places[place], w3)
-            hb = keep.tile([P, H], BF16, name=f"hb{place}")
-            nc.vector.tensor_tensor(uqd(hb), a3, uqd(sigs[places[place]]), MULT)
-            hidden[place] = hb
+            tile = places[place]
+            a3 = first_layer(high[place % 4], tile, w3)
+            if tile[0] < HOT:
+                hb = hot_h[:, (place - 8) * H : (place - 7) * H]
+            else:
+                hidden[place] = keep.tile([P, H], BF16, name=f"hb{place}")
+                hb = hidden[place][:]
+            nc.vector.tensor_tensor(like_sums(hb, tile), a3, like_sums(sigs[tile][:], tile), MULT)
 
         def turn(first, last, bank, copy=nc.scalar.copy):
             n = last - first
@@ -229,7 +245,6 @@ def tile_moe_hot_glu_sigmoid_kernel(
             hidden[place] = keep.tile([P, H], BF16, name=name, align_bytes=64)
             nc.gpsimd.tensor_tensor(hidden[place][:], plains[place][:], sigs[places[place]][:], MULT)
 
-        lent_product(13, "hb13")
         for place in range(4):
             product(place)
         gather(pieces[4], sig_name(places[0]), sig_name(places[1]))
@@ -239,10 +254,11 @@ def tile_moe_hot_glu_sigmoid_kernel(
         turn(0, 2, next_low())
         sigmoid(cold_tiles[10], next_low())
         sigmoid(cold_tiles[11], next_low())
-        lent_product(12, "w1c4")
-        lent_product(14, "plain12")
-        lent_product(15, sig_name(places[12]))
-        turn(2, 4, next_low(), nc.vector.tensor_copy)
+        lent_product(12, "hb12")
+        lent_product(13, "hb13")
+        lent_product(14, "w3h1")
+        lent_product(15, "w1h1")
+        turn(2, 4, next_low())
         sigmoid(hot_tiles[0], next_low())
         sigmoid(hot_tiles[1], next_low())
         sigmoid(hot_tiles[2], next_low())
@@ -250,14 +266,11 @@ def tile_moe_hot_glu_sigmoid_kernel(
         for place in range(4, hot_second[0]):
             product(place)
         turn(4, 6, low[2])
-        turn(12, 14, low[3])
         for place in range(*hot_second):
             product(place)
+        turn(12, 14, low[3])
         turn(6, 8, low[0])
         turn(14, 16, low[1])
-        turn(8, 10, high[0])
-        turn(10, 11, high[1])
-        turn(11, 12, high[2])
 
 
         codes = {}
@@ -265,7 +278,8 @@ def tile_moe_hot_glu_sigmoid_kernel(
         def quantise(first, last, name):
             hq = keep.tile([P, (last - first) * P], U32, name=name, align_bytes=64)
             hs = keep.tile([P, (last - first) * P], U8, name=f"hs{first}", align_bytes=64)
-            nc.vector.quantize_mx(out=hq[:].bitcast(FP8X4), scales=hs[:], in_=turned[:, first * H : last * H])
+            source = hot_h[:, (first - 8) * H : (last - 8) * H] if 8 <= first < 12 else turned[:, first * H : last * H]
+            nc.vector.quantize_mx(out=hq[:].bitcast(FP8X4), scales=hs[:], in_=source)
             step = min(2, last - first)
             for place in range(first, last, step):
                 cols = slice((place - first) * P, (place - first + step) * P)
@@ -281,20 +295,20 @@ def tile_moe_hot_glu_sigmoid_kernel(
             slot = places[first][0] * C + places[first][1] * P
             copy(y[b][:, slot : slot + (last - first) * P], bank[:, 0 : (last - first) * P])
 
-        quantise(*span_c, sig_name(places[on_vector - 2]))
-        quantise(*span_a, sig_name(places[on_vector - 1]))
-        quantise(*span_b, sig_name(places[on_vector - 3]))
-        quantise(*hot_first, "hq_hot_first")
-        quantise(10, 11, "hq10")
-        quantise(11, 12, "hq11")
-        second_layer(low[1], 0, *span_c, nc.scalar.copy)
-        second_layer(high[3], 0, *span_a, nc.scalar.copy)
-        second_layer(low[2], 0, *span_b, nc.vector.tensor_copy)
-        second_layer(low[3], 0, *hot_first, nc.scalar.copy)
-        second_layer(low[0], 0, *hot_second, nc.scalar.copy)
+        quantise(*hot_first, sig_name(places[on_vector - 2]))
+        quantise(*hot_second, "hq_hot_second")
+        quantise(*span_c, sig_name(places[on_vector - 1]))
+        quantise(*span_a, "hq_a")
+        quantise(12, 14, "hq12")
+        quantise(14, 16, "hq14")
+        second_layer(high[0], 0, 8, 12, nc.scalar.copy)
+        second_layer(high[1], 0, *span_c, nc.scalar.copy)
+        second_layer(high[2], 0, *span_a, nc.vector.tensor_copy)
+        second_layer(high[3], 0, 12, 14, nc.scalar.copy)
+        second_layer(low[2], 0, 14, 16, nc.scalar.copy)
 
 
-        for bank, first in zip((high[1], high[0], high[2], high[3]), (8, 12, 0, 4)):
+        for bank, first in zip((high[3], high[2], high[3], high[2]), (8, 0, 4, 12)):
             second_layer(bank, 1, first, first + 4, nc.scalar.copy)
 
         chunks = T // P

@@ -100,18 +100,18 @@ def tile_moe_hot_glu_sigmoid_kernel(
                     in_=scales[:, 0, 4 * q : 4 * q + 4, :].bitcast(I32),
                 )
 
+        load_cold_pair(w1, "w1c", w1c_words, s1c, 2)
         load_one_hot(w1, "w1h", w1h_words, 0, 0)
         load_one_hot(w3, "w3h", w3h_words, 0, 8)
-        load_cold_pair(w1, "w1c", w1c_words, s1c, 2)
-        load_cold_pair(w3, "w3c", w3c_words, s3c, 2)
         load_cold_pair(w3, "w3c", w3c_words, s3c, 0)
+        load_cold_pair(w3, "w3c", w3c_words, s3c, 2)
         load_cold_pair(w1, "w1c", w1c_words, s1c, 4)
+        load_one_hot(w1, "w1h", w1h_words, 1, 4)
         load_cold_pair(w3, "w3c", w3c_words, s3c, 4)
+        load_one_hot(w3, "w3h", w3h_words, 1, 12)
         load_hot_rows(0, w1h_scales)
         load_hot_rows(8, w3h_scales)
         nc.gpsimd.tensor_copy(sh[:].rearrange("p (t q) -> p t q", t=4), sh_raw[:, 0, :].rearrange("p (q t) -> p t q", t=4))
-        load_one_hot(w1, "w1h", w1h_words, 1, 4)
-        load_one_hot(w3, "w3h", w3h_words, 1, 12)
         load_plane(s2c, w2c_scales)
         load_plane(s2h, w2h_scales)
         w2h = load_words("w2h", hot_words(w2h_words))
@@ -200,7 +200,7 @@ def tile_moe_hot_glu_sigmoid_kernel(
 
         hot_h = keep.tile([P, 4 * H], BF16, name="hot_h", align_bytes=64)
 
-        for tile in cold_tiles[:6]:
+        for tile in cold_tiles[:8]:
             sigmoid(tile, next_low())
 
 
@@ -234,12 +234,8 @@ def tile_moe_hot_glu_sigmoid_kernel(
 
         span_c, span_a, span_b = (0, 4), (4, 8), (12, 16)
         hot_first, hot_second = (8, 10), (10, 12)
-        lend(12)
-        lend(13)
-        sigmoid(cold_tiles[6], next_low())
-        sigmoid(cold_tiles[7], next_low())
-        lend(14)
-        lend(15)
+        for place in range(*span_b):
+            lend(place)
 
         def lent_product(place, name):
             hidden[place] = keep.tile([P, H], BF16, name=name, align_bytes=64)
@@ -254,10 +250,10 @@ def tile_moe_hot_glu_sigmoid_kernel(
         turn(0, 2, next_low())
         sigmoid(cold_tiles[10], next_low())
         sigmoid(cold_tiles[11], next_low())
-        lent_product(12, "hb12")
-        lent_product(13, "hb13")
-        lent_product(14, "w3h1")
-        lent_product(15, "w1h1")
+        lent_product(12, "w3h1")
+        lent_product(13, "sh_raw")
+        lent_product(14, "plain13")
+        lent_product(15, sig_name(places[13]))
         turn(2, 4, next_low())
         sigmoid(hot_tiles[0], next_low())
         sigmoid(hot_tiles[1], next_low())

@@ -74,7 +74,7 @@ def tile_moe_hot_glu_sigmoid_kernel(
             nc.sync.dma_start(out=xs[32 * q : 32 * q + 32, :].bitcast(I32), in_=rows.unsqueeze(0).to_broadcast([8, 4, T // 4]))
         nc.sync.dma_start(offs_t[:], offs)
 
-        w1, w3 = {}, {}
+        w1, w3, w2c = {}, {}, {}
 
         def load_cold_pair(table, name, words, plane, first):
             tile = load_words(f"{name}{first}", cold_words(words, first, first + 2))
@@ -105,22 +105,28 @@ def tile_moe_hot_glu_sigmoid_kernel(
         load_one_hot(w3, "w3h", w3h_words, 0, 8)
         load_cold_pair(w3, "w3c", w3c_words, s3c, 0)
         load_cold_pair(w3, "w3c", w3c_words, s3c, 2)
-        load_cold_pair(w1, "w1c", w1c_words, s1c, 4)
         load_one_hot(w1, "w1h", w1h_words, 1, 4)
+        load_cold_pair(w1, "w1c", w1c_words, s1c, 4)
         load_cold_pair(w3, "w3c", w3c_words, s3c, 4)
-        load_one_hot(w3, "w3h", w3h_words, 1, 12)
         load_hot_rows(0, w1h_scales)
         load_hot_rows(8, w3h_scales)
         nc.gpsimd.tensor_copy(sh[:].rearrange("p (t q) -> p t q", t=4), sh_raw[:, 0, :].rearrange("p (q t) -> p t q", t=4))
+        load_one_hot(w3, "w3h", w3h_words, 1, 12)
         load_plane(s2c, w2c_scales)
         load_plane(s2h, w2h_scales)
+
+        def load_w2c(first):
+            w2c.setdefault(first, load_words(f"w2c{first}", cold_words(w2c_words, first, first + 2)))
+
+        load_w2c(0)
         w2h = load_words("w2h", hot_words(w2h_words))
-        w2c = load_words("w2c", cold_words(w2c_words, 0, COLD))
+        load_w2c(4)
+        load_w2c(2)
 
         def w2_block(e, b):
             if e < HOT:
                 return w2h[:, e, 4 * P * b : 4 * P * (b + 1)].bitcast(FP8X4), s2h[:, e, P * b : P * (b + 1)]
-            return w2c[:, e - HOT, 2 * P * b : 2 * P * (b + 1)].bitcast(FP4X4), s2c[:, e - HOT, P * b : P * (b + 1)]
+            return w2c[e - HOT - e % 2][:, e % 2, 2 * P * b : 2 * P * (b + 1)].bitcast(FP4X4), s2c[:, e - HOT, P * b : P * (b + 1)]
 
         pos_t = []
         for r, pos in enumerate((pos1, pos2, pos3, pos4)):
@@ -212,9 +218,16 @@ def tile_moe_hot_glu_sigmoid_kernel(
             nc.scalar.copy(uqd(plain[:]), a3)
             plains[place] = plain
 
+        gated = {}
+
+        def other_half(place):
+            gated[place] = first_layer(high[place % 4], places[place], w3)
+
         def product(place):
             tile = places[place]
-            a3 = first_layer(high[place % 4], tile, w3)
+            if place not in gated:
+                other_half(place)
+            a3 = gated[place]
             if tile[0] < HOT:
                 hb = hot_h[:, (place - 8) * H : (place - 7) * H]
             else:
@@ -250,22 +263,26 @@ def tile_moe_hot_glu_sigmoid_kernel(
         turn(0, 2, next_low())
         sigmoid(cold_tiles[10], next_low())
         sigmoid(cold_tiles[11], next_low())
-        lent_product(12, "w3h1")
-        lent_product(13, "sh_raw")
-        lent_product(14, "plain13")
-        lent_product(15, sig_name(places[13]))
+        lent_product(12, "hb12")
+        lent_product(13, "hb13")
+        lent_product(14, "w3h1")
+        lent_product(15, "sh_raw")
         turn(2, 4, next_low())
+        for place in range(4, 8):
+            product(place)
         sigmoid(hot_tiles[0], next_low())
         sigmoid(hot_tiles[1], next_low())
+        other_half(8)
         sigmoid(hot_tiles[2], next_low())
+        other_half(9)
         sigmoid(hot_tiles[3], next_low())
-        for place in range(4, hot_second[0]):
-            product(place)
+        other_half(10)
+        other_half(11)
         turn(4, 6, low[2])
-        for place in range(*hot_second):
+        for place in range(8, 12):
             product(place)
-        turn(12, 14, low[3])
-        turn(6, 8, low[0])
+        turn(6, 8, low[3])
+        turn(12, 14, low[0])
         turn(14, 16, low[1])
 
 
@@ -291,20 +308,19 @@ def tile_moe_hot_glu_sigmoid_kernel(
             slot = places[first][0] * C + places[first][1] * P
             copy(y[b][:, slot : slot + (last - first) * P], bank[:, 0 : (last - first) * P])
 
-        quantise(*hot_first, sig_name(places[on_vector - 2]))
-        quantise(*hot_second, "hq_hot_second")
-        quantise(*span_c, sig_name(places[on_vector - 1]))
+        quantise(*span_c, sig_name(places[on_vector - 2]))
+        quantise(8, 12, "hq_hot")
         quantise(*span_a, "hq_a")
         quantise(12, 14, "hq12")
         quantise(14, 16, "hq14")
-        second_layer(high[0], 0, 8, 12, nc.scalar.copy)
-        second_layer(high[1], 0, *span_c, nc.scalar.copy)
+        second_layer(high[0], 0, *span_c, nc.scalar.copy)
+        second_layer(high[1], 0, 8, 12, nc.scalar.copy)
         second_layer(high[2], 0, *span_a, nc.vector.tensor_copy)
         second_layer(high[3], 0, 12, 14, nc.scalar.copy)
         second_layer(low[2], 0, 14, 16, nc.scalar.copy)
 
 
-        for bank, first in zip((high[3], high[2], high[3], high[2]), (8, 0, 4, 12)):
+        for bank, first in zip((high[3], high[2], high[3], high[2]), (0, 8, 4, 12)):
             second_layer(bank, 1, first, first + 4, nc.scalar.copy)
 
         chunks = T // P

@@ -90,7 +90,10 @@ def tile_moe_hot_glu_sigmoid_kernel(
         def load_one_hot(table, name, words, f, row):
             raw = load_words(f"{name}{f}", hot_words(words)[:, f, :])
             tile = keep.tile([P, H], I32, name=f"{name}{f}_by_t", align_bytes=64)
-            nc.gpsimd.tensor_copy(tile[:].rearrange("p (t q) -> p t q", t=4), raw[:].bitcast(I32).rearrange("p (q t) -> p t q", t=4))
+            nc.gpsimd.tensor_copy(
+                tile[:].rearrange("p (t c i) -> p c t i", t=4, i=4),
+                raw[:].bitcast(I32).rearrange("p (c i t) -> p c t i", t=4, i=4),
+            )
             table[f] = (tile, row)
 
         def load_hot_rows(first, scales):

@@ -71,7 +71,8 @@ def tile_moe_hot_glu_sigmoid_kernel(
         nc.sync.dma_start(out=xw[:], in_=x_words[0].rearrange("p t d -> p (t d)").bitcast(I32))
         for q in range(4):
             rows = x_scales[0, 4 * q : 4 * q + 4].bitcast(I32)
-            nc.sync.dma_start(out=xs[32 * q : 32 * q + 32, :].bitcast(I32), in_=rows.unsqueeze(0).to_broadcast([8, 4, T // 4]))
+            queue = nc.scalar if q < 2 else nc.sync
+            queue.dma_start(out=xs[32 * q : 32 * q + 32, :].bitcast(I32), in_=rows.unsqueeze(0).to_broadcast([8, 4, T // 4]))
         nc.sync.dma_start(offs_t[:], offs)
 
         w1, w3, w2c = {}, {}, {}
@@ -104,10 +105,10 @@ def tile_moe_hot_glu_sigmoid_kernel(
                 )
 
         load_cold_pair(w1, "w1c", w1c_words, s1c, 2)
-        load_one_hot(w1, "w1h", w1h_words, 0, 0)
-        load_one_hot(w3, "w3h", w3h_words, 0, 8)
         load_cold_pair(w3, "w3c", w3c_words, s3c, 0)
+        load_one_hot(w1, "w1h", w1h_words, 0, 0)
         load_cold_pair(w3, "w3c", w3c_words, s3c, 2)
+        load_one_hot(w3, "w3h", w3h_words, 0, 8)
         load_one_hot(w1, "w1h", w1h_words, 1, 4)
         load_cold_pair(w1, "w1c", w1c_words, s1c, 4)
         load_cold_pair(w3, "w3c", w3c_words, s3c, 4)

@@ -19,9 +19,11 @@ FP4X4 = mybir.dt.float4_e2m1fn_x4
 MULT = mybir.AluOpType.mult
 ADD = mybir.AluOpType.add
 SIGMOID = mybir.ActivationFunctionType.Sigmoid
+COPY = mybir.ActivationFunctionType.Copy
 
 P = 128
 HALF = T // 2
+CHUNKS = T // P
 COLD_PIECE = 3
 HOT_PIECE = 2
 
@@ -35,331 +37,319 @@ def tile_moe_hot_glu_sigmoid_kernel(
         keep = ctx.enter_context(tc.tile_pool(name="keep", bufs=1))
         psum = ctx.enter_context(tc.psum_pool(name="psum", bufs=1))
 
+        def sbuf(shape, dtype, name):
+            return keep.tile(shape, dtype, name=name, align_bytes=64)
 
         def zeroed_plane(name, experts, width, engine):
-            plane = keep.tile([P, experts, width], U8, name=name, align_bytes=64)
+            plane = sbuf([P, experts, width], U8, name)
             engine.memset(plane[:].bitcast(I32), 0)
             return plane
 
-        def load_plane(plane, scales, which=range(4)):
+        def load_plane(plane, scales):
             rows = scales[:, 0].rearrange("f (q r) c -> r q f c", r=4)
-            for r in which:
+            for r in range(4):
                 nc.sync.dma_start(out=plane[r:P:32, :, :].bitcast(I32), in_=rows[r].bitcast(I32))
 
         def load_words(name, words):
-            tile = keep.tile(list(words.shape), U8, name=name, align_bytes=64)
+            tile = sbuf(list(words.shape), U8, name)
             nc.sync.dma_start(out=tile[:].bitcast(I32), in_=words.bitcast(I32))
             return tile
 
-        def cold_words(words, first, last):
-            return words[first:last, 0].rearrange("f p c -> p f c")
+        def load_cold_pair(name, words, pair):
+            return load_words(f"{name}{pair}", words[2 * pair : 2 * pair + 2, 0].rearrange("f p c -> p f c"))
 
-        def hot_words(words):
-            return words[:, 0].rearrange("f p n t -> p f (n t)")
+        def load_hot(name, words, f):
+            return load_words(f"{name}{f}", words[f, 0].rearrange("p n t -> p (n t)"))
 
-        xs = keep.tile([P, T], U8, name="xs", align_bytes=64)
-        xw = keep.tile([P, T], I32, name="xw", align_bytes=64)
+        def load_list(name, entries):
+            tile = keep.tile(list(entries.shape), U16, name=name)
+            nc.sync.dma_start(tile[:], entries)
+            return tile
+
+        def load_gate(r):
+            tile = sbuf([P, T], F32, f"gate{r}")
+            nc.sync.dma_start(out=tile[:], in_=gate[r])
+            return tile
+
         s1c = zeroed_plane("s1c", COLD, H, nc.vector)
         s3c = zeroed_plane("s3c", COLD, H, nc.gpsimd)
-        sh_raw = zeroed_plane("sh_raw", 1, H, nc.vector)
+        hot_rows = zeroed_plane("hot_rows", 1, H, nc.vector)
         s2c = zeroed_plane("s2c", COLD, N, nc.vector)
         s2h = zeroed_plane("s2h", HOT, N, nc.vector)
-        ident = keep.tile([P, P], F32, name="ident")
+        ident = sbuf([P, P], F32, "ident")
         make_identity(nc, ident[:])
 
-        offs_t = keep.tile([P, S // 16], U16, name="offs_t")
+        xw = sbuf([P, T], I32, "xw")
+        xs = sbuf([P, T], U8, "xs")
         nc.sync.dma_start(out=xw[:], in_=x_words[0].rearrange("p t d -> p (t d)").bitcast(I32))
         for q in range(4):
             rows = x_scales[0, 4 * q : 4 * q + 4].bitcast(I32)
             queue = nc.scalar if q < 2 else nc.sync
             queue.dma_start(out=xs[32 * q : 32 * q + 32, :].bitcast(I32), in_=rows.unsqueeze(0).to_broadcast([8, 4, T // 4]))
-        nc.sync.dma_start(offs_t[:], offs)
+        offs_t = load_list("offs_t", offs)
 
-        w1, w3, w2c = {}, {}, {}
-
-        def load_cold_pair(table, name, words, plane, first):
-            tile = load_words(f"{name}{first}", cold_words(words, first, first + 2))
-            for f in range(2):
-                table[HOT + first + f] = (tile[:, f, :].bitcast(FP4X4), plane[:, first + f, :])
-
-        load_cold_pair(w1, "w1c", w1c_words, s1c, 0)
+        w1c, w3c, w2c, raw = {}, {}, {}, {}
+        w1c[0] = load_cold_pair("w1c", w1c_words, 0)
         load_plane(s1c, w1c_scales)
+        w3c[0] = load_cold_pair("w3c", w3c_words, 0)
         load_plane(s3c, w3c_scales)
-
-        sh = keep.tile([P, H], U8, name="sh", align_bytes=64)
-
-        def load_one_hot(table, name, words, f, row):
-            raw = load_words(f"{name}{f}", hot_words(words)[:, f, :])
-            tile = keep.tile([P, H], I32, name=f"{name}{f}_by_t", align_bytes=64)
-            nc.gpsimd.tensor_copy(
-                tile[:].rearrange("p (t c i) -> p c t i", t=4, i=4),
-                raw[:].bitcast(I32).rearrange("p (c i t) -> p c t i", t=4, i=4),
-            )
-            table[f] = (tile, row)
-
-        def load_hot_rows(first, scales):
+        raw[1, 0] = load_hot("w1h", w1h_words, 0)
+        w1c[1] = load_cold_pair("w1c", w1c_words, 1)
+        w3c[1] = load_cold_pair("w3c", w3c_words, 1)
+        for first, scales in ((0, w1h_scales), (8, w3h_scales)):
             for q in range(4):
                 nc.sync.dma_start(
-                    out=sh_raw[32 * q + first : 32 * q + first + 8, 0, :].bitcast(I32),
+                    out=hot_rows[32 * q + first : 32 * q + first + 8, 0, :].bitcast(I32),
                     in_=scales[:, 0, 4 * q : 4 * q + 4, :].bitcast(I32),
                 )
-
-        load_cold_pair(w1, "w1c", w1c_words, s1c, 2)
-        load_cold_pair(w3, "w3c", w3c_words, s3c, 0)
-        load_one_hot(w1, "w1h", w1h_words, 0, 0)
-        load_cold_pair(w3, "w3c", w3c_words, s3c, 2)
-        load_one_hot(w3, "w3h", w3h_words, 0, 8)
-        load_one_hot(w1, "w1h", w1h_words, 1, 4)
-        load_cold_pair(w1, "w1c", w1c_words, s1c, 4)
-        load_cold_pair(w3, "w3c", w3c_words, s3c, 4)
-        load_hot_rows(0, w1h_scales)
-        load_hot_rows(8, w3h_scales)
-        nc.gpsimd.tensor_copy(sh[:].rearrange("p (t q) -> p t q", t=4), sh_raw[:, 0, :].rearrange("p (q t) -> p t q", t=4))
-        load_one_hot(w3, "w3h", w3h_words, 1, 12)
+        raw[3, 0] = load_hot("w3h", w3h_words, 0)
+        raw[1, 1] = load_hot("w1h", w1h_words, 1)
+        raw[3, 1] = load_hot("w3h", w3h_words, 1)
+        w1c[2] = load_cold_pair("w1c", w1c_words, 2)
+        w3c[2] = load_cold_pair("w3c", w3c_words, 2)
         load_plane(s2c, w2c_scales)
         load_plane(s2h, w2h_scales)
-
-        def load_w2c(first):
-            w2c.setdefault(first, load_words(f"w2c{first}", cold_words(w2c_words, first, first + 2)))
-
-        load_w2c(0)
-        w2h = load_words("w2h", hot_words(w2h_words))
-        load_w2c(4)
-        load_w2c(2)
-
-        def w2_block(e, b):
-            if e < HOT:
-                return w2h[:, e, 4 * P * b : 4 * P * (b + 1)].bitcast(FP8X4), s2h[:, e, P * b : P * (b + 1)]
-            return w2c[e - HOT - e % 2][:, e % 2, 2 * P * b : 2 * P * (b + 1)].bitcast(FP4X4), s2c[:, e - HOT, P * b : P * (b + 1)]
-
-        pos_t = []
-        for r, pos in enumerate((pos1, pos2, pos3, pos4)):
-            tile = keep.tile([P, T // 16], U16, name=f"pos{r}")
-            nc.sync.dma_start(tile[:], pos)
-            pos_t.append(tile)
-        gate_t = keep.tile([P, TOP, T], F32, name="gate_t")
-        nc.sync.dma_start(out=gate_t[:], in_=gate.rearrange("r p t -> p r t"))
-
-        y = [keep.tile([P, S], F32, name=f"y{b}") for b in range(N // P)]
+        w2c[0] = load_cold_pair("w2c", w2c_words, 0)
+        w2h = load_words("w2h", w2h_words[:, 0].rearrange("f p n t -> p f (n t)"))
+        w2c[1] = load_cold_pair("w2c", w2c_words, 1)
+        w2c[2] = load_cold_pair("w2c", w2c_words, 2)
+        pos_t, gate_t = {}, {}
+        for r in range(2):
+            pos_t[r] = load_list(f"pos{r}", (pos1, pos2)[r])
+            gate_t[r] = load_gate(r)
+        pos_t[3] = load_list("pos3", pos4)
+        gate_col = sbuf([P, CHUNKS], F32, "gate_col")
+        with nc.allow_non_contiguous_dma(reason="one gate value a partition"):
+            nc.sync.dma_start(out=gate_col[:], in_=gate[3, 0].rearrange("(c p) -> p c", p=P))
+        pos_t[2] = load_list("pos2", pos3)
+        gate_t[2] = load_gate(2)
 
         banks = [psum.tile([P, H], F32, name=f"bank{k}") for k in range(8)]
         low, high = banks[:4], banks[4:]
-        low_uses = []
 
-        def next_low():
-            low_uses.append(low[len(low_uses) % 4])
-            return low_uses[-1]
-
-        def slot_tiles(experts):
-            return [(e, j) for e in experts for j in range(2)]
-
-        pair_a, pair_b, pair_c = [[HOT + f, HOT + f + 1] for f in range(0, COLD, 2)]
-        pair_hot = list(range(HOT))
-        cold_tiles, hot_tiles = slot_tiles(pair_a + pair_b + pair_c), slot_tiles(pair_hot)
-
+        first_slot = {"h": 0, "a": 2 * C, "b": 4 * C, "c": 6 * C}
+        pair_of = {"a": 0, "b": 1, "c": 2}
 
         tokens = {}
-        pieces = [cold_tiles[k : k + COLD_PIECE] for k in range(0, len(cold_tiles), COLD_PIECE)]
-        pieces = pieces + [hot_tiles[k : k + HOT_PIECE] for k in range(0, len(hot_tiles), HOT_PIECE)]
-
-        def gather(piece, words_name, scales_name):
-            slot = piece[0][0] * C + piece[0][1] * P
+        cold_tiles = [(g, k) for g in "abc" for k in range(4)]
+        hot_tiles = [("h", k) for k in range(4)]
+        pieces = [cold_tiles[k : k + COLD_PIECE] for k in range(0, 12, COLD_PIECE)]
+        pieces = pieces + [hot_tiles[k : k + HOT_PIECE] for k in range(0, 4, HOT_PIECE)]
+        for n, piece in enumerate(pieces):
+            slot = first_slot[piece[0][0]] + piece[0][1] * P
             entries = offs_t[:, slot // 16 : (slot + len(piece) * P) // 16]
-            gw = keep.tile([P, len(piece) * P], U32, name=words_name, align_bytes=64)
-            gs = keep.tile([P, len(piece) * P], U8, name=scales_name, align_bytes=64)
+            gw = sbuf([P, len(piece) * P], U32, f"gw{n}")
+            gs = sbuf([P, len(piece) * P], U8, f"gs{n}")
             nc.vector.tensor_copy(gw[:], xw[:].bitcast(U32).indirect(entries))
             nc.vector.tensor_copy(gs[:], xs[:].indirect(entries))
             for k, tile in enumerate(piece):
                 tokens[tile] = (gw[:, k * P : (k + 1) * P].bitcast(FP8X4), gs[:, k * P : (k + 1) * P])
 
-        for n, piece in enumerate(pieces[:4]):
-            gather(piece, f"gw{n}", f"gs{n}")
+        by_t = {}
+        hot_plane = sbuf([P, H], U8, "hot_plane")
 
-        def first_layer(bank, tile, table):
-            (words, scales), (w, plane) = tokens[tile], table[tile[0]]
-            if tile[0] < HOT:
-                for t in range(4):
-                    cols = slice(t * P, (t + 1) * P)
-                    nc.tensor.matmul_mx(out=bank[:, cols], lhsT=w[:, cols].bitcast(FP8X4), lhsT_scale=sh[plane:P, cols],
-                                        rhs=words, rhs_scale=scales, start=True, stop=True)
-                return bank[:].rearrange("q (t s) -> q s t", t=4)
-            nc.tensor.matmul_mx(out=bank[:], lhsT=words, lhsT_scale=scales, rhs=w, rhs_scale=plane, start=True, stop=True)
-            return bank[:].rearrange("s (q u d) -> s u q d", u=2, d=2)
+        def permute(which, f):
+            tile = sbuf([P, H], I32, f"w{which}h{f}_by_t")
+            nc.gpsimd.tensor_copy(
+                tile[:].rearrange("p (t c i) -> p c t i", t=4, i=4),
+                raw[which, f][:].bitcast(I32).rearrange("p (c i t) -> p c t i", t=4, i=4),
+            )
+            by_t[which, f] = tile
 
         def uqd(ap):
             return ap.rearrange("s (u q d) -> s u q d", u=2, d=2)
 
+        def first_layer(bank, tile, which):
+            words, scales = tokens[tile]
+            g, f = tile[0], tile[1] // 2
+            if g == "h":
+                row = 4 * f + (8 if which == 3 else 0)
+                for t in range(4):
+                    cols = slice(t * P, (t + 1) * P)
+                    nc.tensor.matmul_mx(out=bank[:, cols], lhsT=by_t[which, f][:, cols].bitcast(FP8X4), lhsT_scale=hot_plane[row:P, cols],
+                                        rhs=words, rhs_scale=scales, start=True, stop=True)
+                return bank[:].rearrange("q (t s) -> q s t", t=4)
+            w = (w1c if which == 1 else w3c)[pair_of[g]][:, f, :].bitcast(FP4X4)
+            plane = (s1c if which == 1 else s3c)[:, 2 * pair_of[g] + f, :]
+            nc.tensor.matmul_mx(out=bank[:], lhsT=words, lhsT_scale=scales, rhs=w, rhs_scale=plane, start=True, stop=True)
+            return bank[:].rearrange("s (q u d) -> s u q d", u=2, d=2)
+
         def like_sums(ap, tile):
-            return ap.rearrange("q (s t) -> q s t", t=4) if tile[0] < HOT else uqd(ap)
+            return ap.rearrange("q (s t) -> q s t", t=4) if tile[0] == "h" else uqd(ap)
 
-        def sig_name(tile):
-            return f"sig{tile[0]}{tile[1]}"
-
-        sigs = {}
+        sigs, plains, a3, hidden = {}, {}, {}, {}
+        ready = {g: sbuf([P, 4 * H], BF16, f"ready_{g}") for g in "abch"}
 
         def sigmoid(tile, bank):
-            a1 = first_layer(bank, tile, w1)
-            sig = keep.tile([P, H], F32, name=sig_name(tile), align_bytes=64)
-            nc.scalar.activation(like_sums(sig[:], tile), a1, SIGMOID)
-            sigs[tile] = sig
+            a1 = first_layer(bank, tile, 1)
+            sigs[tile] = sbuf([P, H], F32, f"sig_{tile[0]}{tile[1]}")
+            nc.scalar.activation(like_sums(sigs[tile][:], tile), a1, SIGMOID)
 
-        places = slot_tiles(pair_a + pair_c + pair_hot + pair_b)
-        on_vector = len(places) - len(slot_tiles(pair_b))
-        hidden = {}
-        turned = keep.tile([P, len(places) * H], BF16, name="turned", align_bytes=64)
+        def lend(tile, bank):
+            sums = first_layer(bank, tile, 3)
+            plains[tile] = sbuf([P, H], F32, f"plain{tile[1]}")
+            nc.scalar.copy(uqd(plains[tile][:]), sums)
 
-        hot_h = keep.tile([P, 4 * H], BF16, name="hot_h", align_bytes=64)
+        def lent_product(tile):
+            hidden[tile] = sbuf([P, H], BF16, f"hb_{tile[0]}{tile[1]}")
+            nc.gpsimd.tensor_tensor(hidden[tile][:], plains[tile][:], sigs[tile][:], MULT)
 
-        for tile in cold_tiles[:8]:
-            sigmoid(tile, next_low())
+        def other_half(tile):
+            a3[tile] = first_layer(high[tile[1]], tile, 3)
 
-
-        plains = {}
-
-        def lend(place):
-            a3 = first_layer(next_low(), places[place], w3)
-            plain = keep.tile([P, H], F32, name=f"plain{place}", align_bytes=64)
-            nc.scalar.copy(uqd(plain[:]), a3)
-            plains[place] = plain
-
-        gated = {}
-
-        def other_half(place):
-            gated[place] = first_layer(high[place % 4], places[place], w3)
-
-        def product(place):
-            tile = places[place]
-            if place not in gated:
-                other_half(place)
-            a3 = gated[place]
-            if tile[0] < HOT:
-                hb = hot_h[:, (place - 8) * H : (place - 7) * H]
+        def product(tile):
+            if tile[0] == "h":
+                hb = ready["h"][:, tile[1] * H : (tile[1] + 1) * H]
             else:
-                hidden[place] = keep.tile([P, H], BF16, name=f"hb{place}")
-                hb = hidden[place][:]
-            nc.vector.tensor_tensor(like_sums(hb, tile), a3, like_sums(sigs[tile][:], tile), MULT)
+                hidden[tile] = sbuf([P, H], BF16, f"hb_{tile[0]}{tile[1]}")
+                hb = hidden[tile][:]
+            nc.vector.tensor_tensor(like_sums(hb, tile), a3[tile], like_sums(sigs[tile][:], tile), MULT)
 
-        def turn(first, last, bank, copy=nc.scalar.copy):
-            n = last - first
-            across = bank[:, 0 : n * 2 * P].rearrange("q (j u s) -> q j u s", j=n, u=2)
-            for place in range(first, last) if first == on_vector else reversed(range(first, last)):
-                pairs = hidden[place][:].bitcast(F32)
+        def turn(g, f, bank):
+            across = bank[:].rearrange("q (j u s) -> q j u s", j=2, u=2)
+            for j in (1, 0):
+                pairs = hidden[g, 2 * f + j][:].bitcast(F32)
                 for u in range(2):
-                    nc.tensor.transpose(across[:, place - first, u, :], pairs[:, u * P : (u + 1) * P], ident[:])
-            dst = turned[:, first * H : last * H].bitcast(F32).rearrange("q (j s u) -> q j s u", j=n, u=2)
-            copy(dst, across.rearrange("q j u s -> q j s u"))
+                    nc.tensor.transpose(across[:, j, u, :], pairs[:, u * P : (u + 1) * P], ident[:])
+            dst = ready[g][:, 2 * f * H : (2 * f + 2) * H].bitcast(F32).rearrange("q (j s u) -> q j s u", j=2, u=2)
+            nc.scalar.copy(dst, across.rearrange("q j u s -> q j s u"))
 
-        span_c, span_a, span_b = (0, 4), (4, 8), (12, 16)
-        hot_first, hot_second = (8, 10), (10, 12)
-        for place in range(*span_b):
-            lend(place)
-
-        def lent_product(place, name):
-            hidden[place] = keep.tile([P, H], BF16, name=name, align_bytes=64)
-            nc.gpsimd.tensor_tensor(hidden[place][:], plains[place][:], sigs[places[place]][:], MULT)
-
-        for place in range(4):
-            product(place)
-        gather(pieces[4], sig_name(places[0]), sig_name(places[1]))
-        gather(pieces[5], sig_name(places[2]), sig_name(places[3]))
-        sigmoid(cold_tiles[8], next_low())
-        sigmoid(cold_tiles[9], next_low())
-        turn(0, 2, next_low())
-        sigmoid(cold_tiles[10], next_low())
-        sigmoid(cold_tiles[11], next_low())
-        lent_product(12, "hb12")
-        lent_product(13, "hb13")
-        lent_product(14, "w3h1")
-        lent_product(15, "sh_raw")
-        turn(2, 4, next_low())
-        for place in range(4, 8):
-            product(place)
-        sigmoid(hot_tiles[0], next_low())
-        sigmoid(hot_tiles[1], next_low())
-        other_half(8)
-        sigmoid(hot_tiles[2], next_low())
-        other_half(9)
-        sigmoid(hot_tiles[3], next_low())
-        other_half(10)
-        other_half(11)
-        turn(4, 6, low[2])
-        for place in range(8, 12):
-            product(place)
-        turn(6, 8, low[3])
-        turn(12, 14, low[0])
-        turn(14, 16, low[1])
-
+        permute(1, 0)
+        sigmoid(("a", 0), low[0])
+        sigmoid(("a", 1), low[1])
+        lend(("a", 0), low[2])
+        lend(("a", 1), low[3])
+        sigmoid(("a", 2), low[2])
+        sigmoid(("a", 3), low[3])
+        lend(("a", 2), low[0])
+        lend(("a", 3), low[1])
+        for k in range(4):
+            lent_product(("a", k))
+        nc.gpsimd.tensor_copy(hot_plane[:].rearrange("p (t q) -> p t q", t=4), hot_rows[:, 0, :].rearrange("p (q t) -> p t q", t=4))
+        permute(3, 0)
+        permute(1, 1)
+        permute(3, 1)
+        for k in range(4):
+            sigmoid(("b", k), low[(k + 2) % 4])
+        for k in range(4):
+            other_half(("b", k))
+            product(("b", k))
+        for k in range(4):
+            sigmoid(("c", k), low[(k + 2) % 4])
+        turn("a", 0, low[2])
+        turn("a", 1, low[3])
+        for k in range(4):
+            other_half(("c", k))
+            product(("c", k))
+        sigmoid(("h", 0), low[0])
+        sigmoid(("h", 1), low[1])
+        other_half(("h", 0))
+        sigmoid(("h", 2), low[2])
+        other_half(("h", 1))
+        sigmoid(("h", 3), low[3])
+        other_half(("h", 2))
+        other_half(("h", 3))
+        for k in range(4):
+            product(("h", k))
+        turn("b", 0, low[0])
+        turn("b", 1, low[1])
+        turn("c", 0, low[2])
+        turn("c", 1, low[3])
 
         codes = {}
 
-        def quantise(first, last, name):
-            hq = keep.tile([P, (last - first) * P], U32, name=name, align_bytes=64)
-            hs = keep.tile([P, (last - first) * P], U8, name=f"hs{first}", align_bytes=64)
-            source = hot_h[:, (first - 8) * H : (last - 8) * H] if 8 <= first < 12 else turned[:, first * H : last * H]
-            nc.vector.quantize_mx(out=hq[:].bitcast(FP8X4), scales=hs[:], in_=source)
-            step = min(2, last - first)
-            for place in range(first, last, step):
-                cols = slice((place - first) * P, (place - first + step) * P)
-                codes[place] = (hq[:, cols].bitcast(FP8X4), hs[:, cols], step)
+        def quantise(g, experts, name):
+            first, n = experts[0], len(experts)
+            hq = sbuf([P, n * C], U32, name)
+            hs = sbuf([P, n * C], U8, f"hs_{g}{first}")
+            nc.vector.quantize_mx(out=hq[:].bitcast(FP8X4), scales=hs[:], in_=ready[g][:, 2 * first * H : 2 * (first + n) * H])
+            for f in experts:
+                cols = slice((f - first) * C, (f - first + 1) * C)
+                codes[g, f] = (hq[:, cols].bitcast(FP8X4), hs[:, cols])
 
-        def second_layer(bank, b, first, last, copy):
-            for place in range(first, last):
-                if place in codes:
-                    hq, hs, step = codes[place]
-                    w, plane = w2_block(places[place][0], b)
-                    acc = bank[:, (place - first) * P : (place - first + step) * P]
-                    nc.tensor.matmul_mx(out=acc, lhsT=w, lhsT_scale=plane, rhs=hq, rhs_scale=hs, start=True, stop=True)
-            slot = places[first][0] * C + places[first][1] * P
-            copy(y[b][:, slot : slot + (last - first) * P], bank[:, 0 : (last - first) * P])
+        y = [sbuf([P, S], F32, f"y{b}") for b in range(2)]
 
-        quantise(*span_c, sig_name(places[on_vector - 2]))
-        quantise(8, 12, "hq_hot")
-        quantise(*span_a, "hq_a")
-        quantise(12, 14, "hq12")
-        quantise(14, 16, "hq14")
-        second_layer(high[0], 0, *span_c, nc.scalar.copy)
-        second_layer(high[1], 0, 8, 12, nc.scalar.copy)
-        second_layer(high[2], 0, *span_a, nc.vector.tensor_copy)
-        second_layer(high[3], 0, 12, 14, nc.scalar.copy)
-        second_layer(low[2], 0, 14, 16, nc.scalar.copy)
+        def second_layer(bank, b, g, experts, copy):
+            for k, f in enumerate(experts):
+                if g == "h":
+                    w, plane = w2h[:, f, 4 * P * b : 4 * P * (b + 1)].bitcast(FP8X4), s2h[:, f, P * b : P * (b + 1)]
+                else:
+                    w = w2c[pair_of[g]][:, f, 2 * P * b : 2 * P * (b + 1)].bitcast(FP4X4)
+                    plane = s2c[:, 2 * pair_of[g] + f, P * b : P * (b + 1)]
+                hq, hs = codes[g, f]
+                nc.tensor.matmul_mx(out=bank[:, k * C : (k + 1) * C], lhsT=w, lhsT_scale=plane, rhs=hq, rhs_scale=hs, start=True, stop=True)
+            slot = first_slot[g] + experts[0] * C
+            copy(y[b][:, slot : slot + len(experts) * C], bank[:, 0 : len(experts) * C])
 
+        quantise("a", [0, 1], "sig_h2")
+        quantise("h", [0, 1], "hq_h")
+        quantise("b", [0, 1], "hq_b")
+        quantise("c", [0], "hq_c0")
+        quantise("c", [1], "hq_c1")
+        second_layer(high[0], 0, "a", [0, 1], nc.scalar.copy)
+        second_layer(high[1], 0, "h", [0, 1], nc.scalar.copy)
+        second_layer(high[2], 0, "b", [0, 1], nc.vector.tensor_copy)
+        second_layer(high[3], 0, "c", [0], nc.scalar.copy)
+        second_layer(low[0], 0, "c", [1], nc.scalar.copy)
+        for bank, g in zip((high[0], high[1], high[3], low[0]), "ahbc"):
+            second_layer(bank, 1, g, [0, 1], nc.scalar.copy)
 
-        for bank, first in zip((high[3], high[2], high[3], high[2]), (0, 8, 4, 12)):
-            second_layer(bank, 1, first, first + 4, nc.scalar.copy)
+        def chunk(c):
+            return slice(c * P, (c + 1) * P)
 
-        chunks = T // P
+        def turn_add(dst, src, start, stop):
+            nc.tensor.matmul(dst, src, ident[:], start=start, stop=stop, is_transpose=True)
 
-        def pick(dst, b, r, cols):
-            entries = pos_t[r][:, cols.start // 16 : cols.stop // 16]
-            nc.vector.tensor_tensor(dst[:, cols], y[b][:].indirect(entries), gate_t[:, r, cols], MULT)
+        def pick(b, r, parts=1):
+            picked = sbuf([P, T], F32, f"picked{b}{r}")
 
-        def turned_sum(b, lists, last_parts):
-            for r in range(lists):
-                picked = keep.tile([P, T], F32, name=f"picked{b}{r}")
-                parts = last_parts if r == lists - 1 else 1
-                for k in range(parts):
-                    pick(picked, b, r, slice(k * T // parts, (k + 1) * T // parts))
-                for c in range(chunks):
-                    nc.tensor.matmul(low[c][:, 0:P], picked[:, c * P : (c + 1) * P], ident[:], start=(r == 0), stop=(r == lists - 1), is_transpose=True)
-            halves = [high[2 * b + k][:, 0:HALF] for k in range(2)]
-            for c in range(chunks):
-                summed = keep.tile([P, P], F32, name=f"summed{b}{c}")
-                nc.scalar.copy(summed[:], low[c][:, 0:P])
-                nc.tensor.transpose(halves[c // 2][:, (c % 2) * P : (c % 2 + 1) * P], summed[:], ident[:])
-            return halves
+            def part(k):
+                cols = slice(k * T // parts, (k + 1) * T // parts)
+                entries = pos_t[r][:, cols.start // 16 : cols.stop // 16]
+                nc.vector.tensor_tensor(picked[:, cols], y[b][:].indirect(entries), gate_t[r][:, cols], MULT)
 
-        sums = turned_sum(0, TOP, 1)
-        res0 = keep.tile([P, T], F32, name="res0")
-        for k in range(2):
-            nc.scalar.copy(res0[:, k * HALF : (k + 1) * HALF], sums[k])
+            return picked, part
+
+        def two_lists(b, bank):
+            for r in range(2):
+                picked, part = pick(b, r)
+                part(0)
+                for c in range(CHUNKS):
+                    turn_add(bank[:, chunk(c)], picked[:, chunk(c)], r == 0 and c == 0, r == 1 and c == CHUNKS - 1)
+
+        def scalar_list(b, bank):
+            picked = sbuf([P, T], F32, f"picked{b}3")
+            nc.scalar.activation(picked[:], y[b][:].indirect(pos_t[3][:]), COPY)
+            for c in range(CHUNKS):
+                nc.tensor.transpose(bank[:, chunk(c)], picked[:, chunk(c)], ident[:])
+
+        def way_back(b, summed_bank, plain_bank, targets):
+            summed = sbuf([P, T], F32, f"summed{b}")
+            nc.scalar.copy(summed[:], summed_bank[:])
+            per = CHUNKS // len(targets)
+            for c in range(CHUNKS):
+                turn_add(targets[c // per][:, chunk(c % per)], summed[:, chunk(c)], c % per == 0, False)
+            for c in range(CHUNKS):
+                scaled = sbuf([P, P], F32, f"scaled{b}{c}")
+                nc.scalar.activation(scaled[:], plain_bank[:, chunk(c)], COPY, scale=gate_col[:, c : c + 1])
+                turn_add(targets[c // per][:, chunk(c % per)], scaled[:], False, c % per == per - 1)
+
+        two_lists(0, low[1])
+        scalar_list(0, low[2])
+        way_back(0, low[1], low[2], [high[0]])
+        two_lists(1, low[3])
+        scalar_list(1, high[2])
+        way_back(1, low[3], high[2], [high[1], high[3]])
+        third0, part0 = pick(0, 2)
+        third1, part1 = pick(1, 2, 2)
+        part0(0)
+        part1(0)
+        res0 = sbuf([P, T], F32, "res0")
+        nc.vector.tensor_tensor(res0[:], high[0][:], third0[:], ADD)
         nc.sync.dma_start(out=out[0:P, :], in_=res0[:])
-
-        sums = turned_sum(1, TOP - 1, 2)
-        fourth = keep.tile([P, T], F32, name="fourth")
-        for k in range(2):
-            pick(fourth, 1, TOP - 1, slice(k * HALF, (k + 1) * HALF))
-        for k in range(2):
+        part1(1)
+        for k, bank in enumerate((high[1], high[3])):
             cols = slice(k * HALF, (k + 1) * HALF)
-            res1 = keep.tile([P, HALF], F32, name=f"res1{k}")
-            nc.vector.tensor_tensor(res1[:], sums[k], fourth[:, cols], ADD)
+            res1 = sbuf([P, HALF], F32, f"res1{k}")
+            nc.vector.tensor_tensor(res1[:], bank[:, 0:HALF], third1[:, cols], ADD)
             nc.sync.dma_start(out=out[P : 2 * P, cols], in_=res1[:])

@@ -66,11 +66,6 @@ def tile_moe_hot_glu_sigmoid_kernel(
             nc.sync.dma_start(tile[:], entries)
             return tile
 
-        def load_gate(r):
-            tile = sbuf([P, T], F32, f"gate{r}")
-            nc.sync.dma_start(out=tile[:], in_=gate[r])
-            return tile
-
         s1c = zeroed_plane("s1c", COLD, H, nc.vector)
         s3c = zeroed_plane("s3c", COLD, H, nc.gpsimd)
         hot_rows = zeroed_plane("hot_rows", 1, H, nc.vector)
@@ -107,22 +102,18 @@ def tile_moe_hot_glu_sigmoid_kernel(
         raw[3, 1] = load_hot("w3h", w3h_words, 1)
         w1c[2] = load_cold_pair("w1c", w1c_words, 2)
         w3c[2] = load_cold_pair("w3c", w3c_words, 2)
+        pos_t = {r: load_list(f"pos{r}", pos) for r, pos in enumerate((pos1, pos2, pos3, pos4))}
+        gate_col = sbuf([P, CHUNKS], F32, "gate_col")
+        with nc.allow_non_contiguous_dma(reason="one gate value a partition"):
+            nc.sync.dma_start(out=gate_col[:], in_=gate[3, 0].rearrange("(c p) -> p c", p=P))
+        gate_t = sbuf([P, TOP - 1, T], F32, "gate_t")
+        nc.sync.dma_start(out=gate_t[:], in_=gate[0 : TOP - 1].rearrange("r p t -> p r t"))
         load_plane(s2c, w2c_scales)
         load_plane(s2h, w2h_scales)
         w2c[0] = load_cold_pair("w2c", w2c_words, 0)
         w2h = load_words("w2h", w2h_words[:, 0].rearrange("f p n t -> p f (n t)"))
         w2c[1] = load_cold_pair("w2c", w2c_words, 1)
         w2c[2] = load_cold_pair("w2c", w2c_words, 2)
-        pos_t, gate_t = {}, {}
-        for r in range(2):
-            pos_t[r] = load_list(f"pos{r}", (pos1, pos2)[r])
-            gate_t[r] = load_gate(r)
-        pos_t[3] = load_list("pos3", pos4)
-        gate_col = sbuf([P, CHUNKS], F32, "gate_col")
-        with nc.allow_non_contiguous_dma(reason="one gate value a partition"):
-            nc.sync.dma_start(out=gate_col[:], in_=gate[3, 0].rearrange("(c p) -> p c", p=P))
-        pos_t[2] = load_list("pos2", pos3)
-        gate_t[2] = load_gate(2)
 
         banks = [psum.tile([P, H], F32, name=f"bank{k}") for k in range(8)]
         low, high = banks[:4], banks[4:]
@@ -291,8 +282,15 @@ def tile_moe_hot_glu_sigmoid_kernel(
         second_layer(high[2], 0, "b", [0, 1], nc.vector.tensor_copy)
         second_layer(high[3], 0, "c", [0], nc.scalar.copy)
         second_layer(low[0], 0, "c", [1], nc.scalar.copy)
-        for bank, g in zip((high[0], high[1], high[3], low[0]), "ahbc"):
-            second_layer(bank, 1, g, [0, 1], nc.scalar.copy)
+        plain = {}
+
+        def scalar_gather(b):
+            plain[b] = sbuf([P, T], F32, f"plain_pick{b}")
+            nc.scalar.activation(plain[b][:], y[b][:].indirect(pos_t[3][:]), COPY)
+
+        scalar_gather(0)
+        for bank, g in zip((high[3], low[0], high[3], high[1]), "ahbc"):
+            second_layer(bank, 1, g, [0, 1], nc.vector.tensor_copy if g == "c" else nc.scalar.copy)
 
         def chunk(c):
             return slice(c * P, (c + 1) * P)
@@ -306,43 +304,51 @@ def tile_moe_hot_glu_sigmoid_kernel(
             def part(k):
                 cols = slice(k * T // parts, (k + 1) * T // parts)
                 entries = pos_t[r][:, cols.start // 16 : cols.stop // 16]
-                nc.vector.tensor_tensor(picked[:, cols], y[b][:].indirect(entries), gate_t[r][:, cols], MULT)
+                nc.vector.tensor_tensor(picked[:, cols], y[b][:].indirect(entries), gate_t[:, r, cols], MULT)
 
             return picked, part
 
-        def two_lists(b, bank):
+        def two_lists(b, targets):
+            per = CHUNKS // len(targets)
             for r in range(2):
-                picked, part = pick(b, r)
-                part(0)
+                parts = len(targets) if r == 1 else 1
+                picked, part = pick(b, r, parts)
+                for k in range(parts):
+                    part(k)
                 for c in range(CHUNKS):
-                    turn_add(bank[:, chunk(c)], picked[:, chunk(c)], r == 0 and c == 0, r == 1 and c == CHUNKS - 1)
+                    turn_add(targets[c // per][:, chunk(c % per)], picked[:, chunk(c)], r == 0 and c % per == 0, r == 1 and c % per == per - 1)
 
         def scalar_list(b, bank):
-            picked = sbuf([P, T], F32, f"picked{b}3")
-            nc.scalar.activation(picked[:], y[b][:].indirect(pos_t[3][:]), COPY)
             for c in range(CHUNKS):
-                nc.tensor.transpose(bank[:, chunk(c)], picked[:, chunk(c)], ident[:])
+                nc.tensor.transpose(bank[:, chunk(c)], plain[b][:, chunk(c)], ident[:])
 
-        def way_back(b, summed_bank, plain_bank, targets):
-            summed = sbuf([P, T], F32, f"summed{b}")
-            nc.scalar.copy(summed[:], summed_bank[:])
-            per = CHUNKS // len(targets)
-            for c in range(CHUNKS):
-                turn_add(targets[c // per][:, chunk(c % per)], summed[:, chunk(c)], c % per == 0, False)
-            for c in range(CHUNKS):
-                scaled = sbuf([P, P], F32, f"scaled{b}{c}")
-                nc.scalar.activation(scaled[:], plain_bank[:, chunk(c)], COPY, scale=gate_col[:, c : c + 1])
-                turn_add(targets[c // per][:, chunk(c % per)], scaled[:], False, c % per == per - 1)
+        def scaled_back(b, c, bank, dst, start, stop):
+            scaled = sbuf([P, P], F32, f"scaled{b}{c}")
+            nc.scalar.activation(scaled[:], bank[:, chunk(c)], COPY, scale=gate_col[:, c : c + 1])
+            turn_add(dst, scaled[:], start, stop)
 
-        two_lists(0, low[1])
         scalar_list(0, low[2])
-        way_back(0, low[1], low[2], [high[0]])
-        two_lists(1, low[3])
-        scalar_list(1, high[2])
-        way_back(1, low[3], high[2], [high[1], high[3]])
+        two_lists(0, [low[1]])
+        summed = sbuf([P, T], F32, "summed0")
+        nc.scalar.copy(summed[:], low[1][:])
+        for c in range(CHUNKS):
+            turn_add(high[0][:, chunk(c)], summed[:, chunk(c)], c == 0, False)
+        for c in range(CHUNKS):
+            scaled_back(0, c, low[2], high[0][:, chunk(c)], False, c == CHUNKS - 1)
         third0, part0 = pick(0, 2)
-        third1, part1 = pick(1, 2, 2)
         part0(0)
+        scalar_gather(1)
+        two_lists(1, [low[1], low[2]])
+        scalar_list(1, high[2])
+        halves = (high[1], high[3])
+        for k in range(2):
+            summed = sbuf([P, HALF], F32, f"summed1{k}")
+            nc.scalar.copy(summed[:], low[1 + k][:, 0:HALF])
+            for c in range(2):
+                turn_add(halves[k][:, chunk(c)], summed[:, chunk(c)], c == 0, False)
+        for c in range(CHUNKS):
+            scaled_back(1, c, high[2], halves[c // 2][:, chunk(c % 2)], False, c % 2 == 1)
+        third1, part1 = pick(1, 2, 2)
         part1(0)
         res0 = sbuf([P, T], F32, "res0")
         nc.vector.tensor_tensor(res0[:], high[0][:], third0[:], ADD)

@@ -112,8 +112,8 @@ def tile_moe_hot_glu_sigmoid_kernel(
         load_plane(s2h, w2h_scales)
         w2c[0] = load_cold_pair("w2c", w2c_words, 0)
         w2h = load_words("w2h", w2h_words[:, 0].rearrange("f p n t -> p f (n t)"))
-        w2c[1] = load_cold_pair("w2c", w2c_words, 1)
-        w2c[2] = load_cold_pair("w2c", w2c_words, 2)
+        rest = load_words("w2c_rest", w2c_words[2:COLD, 0].rearrange("f p c -> p f c"))
+        w2c[1], w2c[2] = rest[:, 0:2, :], rest[:, 2:4, :]
 
         banks = [psum.tile([P, H], F32, name=f"bank{k}") for k in range(8)]
         low, high = banks[:4], banks[4:]
@@ -284,13 +284,15 @@ def tile_moe_hot_glu_sigmoid_kernel(
         second_layer(low[0], 0, "c", [1], nc.scalar.copy)
         plain = {}
 
-        def scalar_gather(b):
-            plain[b] = sbuf([P, T], F32, f"plain_pick{b}")
+        def scalar_gather(b, tile):
+            plain[b] = tile
             nc.scalar.activation(plain[b][:], y[b][:].indirect(pos_t[3][:]), COPY)
 
-        scalar_gather(0)
-        for bank, g in zip((high[3], low[0], high[3], high[1]), "ahbc"):
-            second_layer(bank, 1, g, [0, 1], nc.vector.tensor_copy if g == "c" else nc.scalar.copy)
+        scalar_gather(0, sbuf([P, T], F32, "plain_pick"))
+        for bank, g in zip((high[2], high[3], low[0], high[2]), "ahbc"):
+            second_layer(bank, 1, g, [0, 1], nc.scalar.copy)
+
+        first_half, second_half, whole = slice(0, HALF), slice(HALF, T), slice(0, T)
 
         def chunk(c):
             return slice(c * P, (c + 1) * P)
@@ -298,25 +300,13 @@ def tile_moe_hot_glu_sigmoid_kernel(
         def turn_add(dst, src, start, stop):
             nc.tensor.matmul(dst, src, ident[:], start=start, stop=stop, is_transpose=True)
 
-        def pick(b, r, parts=1):
-            picked = sbuf([P, T], F32, f"picked{b}{r}")
+        def pick(dst, b, r, cols):
+            entries = pos_t[r][:, cols.start // 16 : cols.stop // 16]
+            nc.vector.tensor_tensor(dst, y[b][:].indirect(entries), gate_t[:, r, cols], MULT)
 
-            def part(k):
-                cols = slice(k * T // parts, (k + 1) * T // parts)
-                entries = pos_t[r][:, cols.start // 16 : cols.stop // 16]
-                nc.vector.tensor_tensor(picked[:, cols], y[b][:].indirect(entries), gate_t[:, r, cols], MULT)
-
-            return picked, part
-
-        def two_lists(b, targets):
-            per = CHUNKS // len(targets)
-            for r in range(2):
-                parts = len(targets) if r == 1 else 1
-                picked, part = pick(b, r, parts)
-                for k in range(parts):
-                    part(k)
-                for c in range(CHUNKS):
-                    turn_add(targets[c // per][:, chunk(c % per)], picked[:, chunk(c)], r == 0 and c % per == 0, r == 1 and c % per == per - 1)
+        def turn_chunks(bank, src, n, start, stop):
+            for c in range(n):
+                turn_add(bank[:, chunk(c)], src[:, chunk(c)], start and c == 0, stop and c == n - 1)
 
         def scalar_list(b, bank):
             for c in range(CHUNKS):
@@ -327,35 +317,47 @@ def tile_moe_hot_glu_sigmoid_kernel(
             nc.scalar.activation(scaled[:], bank[:, chunk(c)], COPY, scale=gate_col[:, c : c + 1])
             turn_add(dst, scaled[:], start, stop)
 
+        def summed_back(name, bank, n, dst, start, stop):
+            summed = sbuf([P, n * P], F32, name)
+            nc.scalar.copy(summed[:], bank[:, 0 : n * P])
+            turn_chunks(dst, summed, n, start, stop)
+            return summed
+
+        for r in range(2):
+            picked = sbuf([P, T], F32, f"picked0{r}")
+            pick(picked[:], 0, r, whole)
+            turn_chunks(low[1], picked, CHUNKS, r == 0, r == 1)
         scalar_list(0, low[2])
-        two_lists(0, [low[1]])
-        summed = sbuf([P, T], F32, "summed0")
-        nc.scalar.copy(summed[:], low[1][:])
-        for c in range(CHUNKS):
-            turn_add(high[0][:, chunk(c)], summed[:, chunk(c)], c == 0, False)
+        spent = summed_back("summed0", low[1], CHUNKS, high[0], True, False)
         for c in range(CHUNKS):
             scaled_back(0, c, low[2], high[0][:, chunk(c)], False, c == CHUNKS - 1)
-        third0, part0 = pick(0, 2)
-        part0(0)
-        scalar_gather(1)
-        two_lists(1, [low[1], low[2]])
-        scalar_list(1, high[2])
-        halves = (high[1], high[3])
-        for k in range(2):
-            summed = sbuf([P, HALF], F32, f"summed1{k}")
-            nc.scalar.copy(summed[:], low[1 + k][:, 0:HALF])
-            for c in range(2):
-                turn_add(halves[k][:, chunk(c)], summed[:, chunk(c)], c == 0, False)
-        for c in range(CHUNKS):
-            scaled_back(1, c, high[2], halves[c // 2][:, chunk(c % 2)], False, c % 2 == 1)
-        third1, part1 = pick(1, 2, 2)
-        part1(0)
+        shared = sbuf([P, 3 * HALF], F32, "shared")
+        third0 = shared[:, P : P + T]
+        pick(third0, 0, 2, whole)
+
+        scalar_gather(1, spent)
+        picked = sbuf([P, T], F32, "picked10")
+        pick(picked[:], 1, 0, whole)
+        turn_chunks(low[2], picked[:, first_half], 2, True, False)
+        turn_chunks(low[1], picked[:, second_half], 2, True, False)
+        picked = sbuf([P, HALF], F32, "picked11")
+        pick(picked[:], 1, 1, first_half)
+        turn_chunks(low[2], picked, 2, False, True)
         res0 = sbuf([P, T], F32, "res0")
-        nc.vector.tensor_tensor(res0[:], high[0][:], third0[:], ADD)
+        nc.vector.tensor_tensor(res0[:], high[0][:], third0, ADD)
         nc.sync.dma_start(out=out[0:P, :], in_=res0[:])
-        part1(1)
-        for k, bank in enumerate((high[1], high[3])):
-            cols = slice(k * HALF, (k + 1) * HALF)
+        scalar_list(1, high[2])
+        pick(shared[:, HALF:T], 1, 1, second_half)
+        turn_chunks(low[1], shared[:, HALF:T], 2, False, True)
+        halves = (high[1], high[3])
+        summed_back("summed10", low[2], 2, halves[0], True, False)
+        for c in range(CHUNKS):
+            scaled_back(1, c, high[2], halves[c // 2][:, chunk(c % 2)], c == 2, c == 1)
+        summed_back("summed11", low[1], 2, halves[1], False, True)
+        third1 = (shared[:, 0:HALF], shared[:, T : T + HALF])
+        for k, cols in enumerate((first_half, second_half)):
+            pick(third1[k], 1, 2, cols)
+        for k, cols in enumerate((first_half, second_half)):
             res1 = sbuf([P, HALF], F32, f"res1{k}")
-            nc.vector.tensor_tensor(res1[:], bank[:, 0:HALF], third1[:, cols], ADD)
+            nc.vector.tensor_tensor(res1[:], halves[k][:, 0:HALF], third1[k], ADD)
             nc.sync.dma_start(out=out[P : 2 * P, cols], in_=res1[:])

@@ -335,29 +335,39 @@ def tile_moe_hot_glu_sigmoid_kernel(
         third0 = shared[:, P : P + T]
         pick(third0, 0, 2, whole)
 
+        parts = (slice(0, HALF), slice(HALF, HALF + P), slice(HALF + P, T))
+        sums, backs = (low[2], low[1], low[3]), (high[1], high[3], low[0])
+
+        def width(cols):
+            return (cols.stop - cols.start) // P
+
         scalar_gather(1, spent)
         picked = sbuf([P, T], F32, "picked10")
         pick(picked[:], 1, 0, whole)
-        turn_chunks(low[2], picked[:, first_half], 2, True, False)
-        turn_chunks(low[1], picked[:, second_half], 2, True, False)
+        for bank, cols in zip(sums, parts):
+            turn_chunks(bank, picked[:, cols], width(cols), True, False)
         picked = sbuf([P, HALF], F32, "picked11")
         pick(picked[:], 1, 1, first_half)
-        turn_chunks(low[2], picked, 2, False, True)
+        turn_chunks(sums[0], picked, 2, False, True)
         res0 = sbuf([P, T], F32, "res0")
-        nc.vector.tensor_tensor(res0[:], high[0][:], third0, ADD)
+        for cols in (first_half, second_half):
+            nc.vector.tensor_tensor(res0[:, cols], high[0][:, cols], third0[:, cols], ADD)
         nc.sync.dma_start(out=out[0:P, :], in_=res0[:])
         scalar_list(1, high[2])
-        pick(shared[:, HALF:T], 1, 1, second_half)
-        turn_chunks(low[1], shared[:, HALF:T], 2, False, True)
-        halves = (high[1], high[3])
-        summed_back("summed10", low[2], 2, halves[0], True, False)
-        for c in range(CHUNKS):
-            scaled_back(1, c, high[2], halves[c // 2][:, chunk(c % 2)], c == 2, c == 1)
-        summed_back("summed11", low[1], 2, halves[1], False, True)
-        third1 = (shared[:, 0:HALF], shared[:, T : T + HALF])
-        for k, cols in enumerate((first_half, second_half)):
-            pick(third1[k], 1, 2, cols)
-        for k, cols in enumerate((first_half, second_half)):
-            res1 = sbuf([P, HALF], F32, f"res1{k}")
-            nc.vector.tensor_tensor(res1[:], halves[k][:, 0:HALF], third1[k], ADD)
+        pick(shared[:, 0:HALF], 1, 1, second_half)
+        for c in range(2):
+            turn_chunks(sums[1 + c], shared[:, chunk(c)], 1, False, True)
+        summed_back("summed10", sums[0], 2, backs[0], True, False)
+        for c in range(2):
+            scaled_back(1, c, high[2], backs[0][:, chunk(c)], False, c == 1)
+        for c in range(2):
+            scaled_back(1, 2 + c, high[2], backs[1 + c][:, chunk(0)], True, False)
+        for c in range(2):
+            summed_back(f"summed1{1 + c}", sums[1 + c], 1, backs[1 + c], False, True)
+        third1 = shared[:, HALF : HALF + T]
+        for cols in (first_half, second_half):
+            pick(third1[:, cols], 1, 2, cols)
+        for k, cols in enumerate(parts):
+            res1 = sbuf([P, width(cols) * P], F32, f"res1{k}")
+            nc.vector.tensor_tensor(res1[:], backs[k][:, 0 : width(cols) * P], third1[:, cols], ADD)
             nc.sync.dma_start(out=out[P : 2 * P, cols], in_=res1[:])

@@ -321,14 +321,17 @@ def tile_moe_hot_glu_sigmoid_kernel(
             summed = sbuf([P, n * P], F32, name)
             nc.scalar.copy(summed[:], bank[:, 0 : n * P])
             turn_chunks(dst, summed, n, start, stop)
-            return summed
 
         for r in range(2):
             picked = sbuf([P, T], F32, f"picked0{r}")
             pick(picked[:], 0, r, whole)
-            turn_chunks(low[1], picked, CHUNKS, r == 0, r == 1)
+            for bank, cols in ((low[1], first_half), (low[3], second_half)):
+                turn_chunks(bank, picked[:, cols], 2, r == 0, r == 1)
         scalar_list(0, low[2])
-        spent = summed_back("summed0", low[1], CHUNKS, high[0], True, False)
+        spent = sbuf([P, T], F32, "summed0")
+        for bank, cols in ((low[1], first_half), (low[3], second_half)):
+            nc.scalar.copy(spent[:, cols], bank[:, 0:HALF])
+        turn_chunks(high[0], spent, CHUNKS, True, False)
         for c in range(CHUNKS):
             scaled_back(0, c, low[2], high[0][:, chunk(c)], False, c == CHUNKS - 1)
         shared = sbuf([P, 3 * HALF], F32, "shared")

from contextlib import ExitStack

import concourse.mybir as mybir
from concourse.masks import make_identity

K, T, E, C, H, N, HOT, TOP = 512, 512, 8, 256, 512, 256, 2, 4
COLD = E - HOT
S = E * C
FLOPS = 2 * S * (2 * K * H + H * N)

F32 = mybir.dt.float32
BF16 = mybir.dt.bfloat16
I32 = mybir.dt.int32
U32 = mybir.dt.uint32
U16 = mybir.dt.uint16
U8 = mybir.dt.uint8
FP8X4 = mybir.dt.float8_e4m3fn_x4
FP4X4 = mybir.dt.float4_e2m1fn_x4
MULT = mybir.AluOpType.mult
ADD = mybir.AluOpType.add
SIGMOID = mybir.ActivationFunctionType.Sigmoid
COPY = mybir.ActivationFunctionType.Copy

P = 128
HALF = T // 2
CHUNKS = T // P
COLD_PIECE = 3
HOT_PIECE = 2


def tile_moe_hot_glu_sigmoid_kernel(
    tc, x_words, x_scales, w1h_words, w1h_scales, w3h_words, w3h_scales, w2h_words, w2h_scales,
    w1c_words, w1c_scales, w3c_words, w3c_scales, w2c_words, w2c_scales, gate, offs, pos1, pos2, pos3, pos4, out,
):
    nc = tc.nc
    with ExitStack() as ctx:
        keep = ctx.enter_context(tc.tile_pool(name="keep", bufs=1))
        psum = ctx.enter_context(tc.psum_pool(name="psum", bufs=1))

        def sbuf(shape, dtype, name):
            return keep.tile(shape, dtype, name=name, align_bytes=64)

        def zeroed_plane(name, experts, width, engine):
            plane = sbuf([P, experts, width], U8, name)
            engine.memset(plane[:].bitcast(I32), 0)
            return plane

        def load_plane(plane, scales):
            rows = scales[:, 0].rearrange("f (q r) c -> r q f c", r=4)
            for r in range(4):
                nc.sync.dma_start(out=plane[r:P:32, :, :].bitcast(I32), in_=rows[r].bitcast(I32))

        def load_words(name, words):
            tile = sbuf(list(words.shape), U8, name)
            nc.sync.dma_start(out=tile[:].bitcast(I32), in_=words.bitcast(I32))
            return tile

        def load_cold_pair(name, words, pair):
            return load_words(f"{name}{pair}", words[2 * pair : 2 * pair + 2, 0].rearrange("f p c -> p f c"))

        def load_hot(name, words, f):
            return load_words(f"{name}{f}", words[f, 0].rearrange("p n t -> p (n t)"))

        def load_list(name, entries):
            tile = keep.tile(list(entries.shape), U16, name=name)
            nc.sync.dma_start(tile[:], entries)
            return tile

        s1c = zeroed_plane("s1c", COLD, H, nc.vector)
        s3c = zeroed_plane("s3c", COLD, H, nc.gpsimd)
        hot_rows = zeroed_plane("hot_rows", 1, H, nc.vector)
        s2c = zeroed_plane("s2c", COLD, N, nc.vector)
        s2h = zeroed_plane("s2h", HOT, N, nc.vector)
        ident = sbuf([P, P], F32, "ident")
        make_identity(nc, ident[:])

        xw = sbuf([P, T], I32, "xw")
        xs = sbuf([P, T], U8, "xs")
        nc.sync.dma_start(out=xw[:], in_=x_words[0].rearrange("p t d -> p (t d)").bitcast(I32))
        for q in range(4):
            rows = x_scales[0, 4 * q : 4 * q + 4].bitcast(I32)
            queue = nc.scalar if q < 2 else nc.sync
            queue.dma_start(out=xs[32 * q : 32 * q + 32, :].bitcast(I32), in_=rows.unsqueeze(0).to_broadcast([8, 4, T // 4]))
        offs_t = load_list("offs_t", offs)

        w1c, w3c, w2c, raw = {}, {}, {}, {}
        w1c[0] = load_cold_pair("w1c", w1c_words, 0)
        load_plane(s1c, w1c_scales)
        w3c[0] = load_cold_pair("w3c", w3c_words, 0)
        load_plane(s3c, w3c_scales)
        raw[1, 0] = load_hot("w1h", w1h_words, 0)
        w1c[1] = load_cold_pair("w1c", w1c_words, 1)
        w3c[1] = load_cold_pair("w3c", w3c_words, 1)
        for first, scales in ((0, w1h_scales), (8, w3h_scales)):
            for q in range(4):
                nc.sync.dma_start(
                    out=hot_rows[32 * q + first : 32 * q + first + 8, 0, :].bitcast(I32),
                    in_=scales[:, 0, 4 * q : 4 * q + 4, :].bitcast(I32),
                )
        raw[3, 0] = load_hot("w3h", w3h_words, 0)
        raw[1, 1] = load_hot("w1h", w1h_words, 1)
        raw[3, 1] = load_hot("w3h", w3h_words, 1)
        w1c[2] = load_cold_pair("w1c", w1c_words, 2)
        w3c[2] = load_cold_pair("w3c", w3c_words, 2)
        pos_t = {r: load_list(f"pos{r}", pos) for r, pos in enumerate((pos1, pos2, pos3, pos4))}
        gate_col = sbuf([P, CHUNKS], F32, "gate_col")
        with nc.allow_non_contiguous_dma(reason="one gate value a partition"):
            nc.sync.dma_start(out=gate_col[:], in_=gate[3, 0].rearrange("(c p) -> p c", p=P))
        gate_t = sbuf([P, TOP - 1, T], F32, "gate_t")
        nc.sync.dma_start(out=gate_t[:], in_=gate[0 : TOP - 1].rearrange("r p t -> p r t"))
        load_plane(s2c, w2c_scales)
        load_plane(s2h, w2h_scales)
        w2c[0] = load_cold_pair("w2c", w2c_words, 0)
        w2h = load_words("w2h", w2h_words[:, 0].rearrange("f p n t -> p f (n t)"))
        rest = load_words("w2c_rest", w2c_words[2:COLD, 0].rearrange("f p c -> p f c"))
        w2c[1], w2c[2] = rest[:, 0:2, :], rest[:, 2:4, :]

        banks = [psum.tile([P, H], F32, name=f"bank{k}") for k in range(8)]
        low, high = banks[:4], banks[4:]

        first_slot = {"h": 0, "a": 2 * C, "b": 4 * C, "c": 6 * C}
        pair_of = {"a": 0, "b": 1, "c": 2}

        tokens = {}
        cold_tiles = [(g, k) for g in "abc" for k in range(4)]
        hot_tiles = [("h", k) for k in range(4)]
        pieces = [cold_tiles[k : k + COLD_PIECE] for k in range(0, 12, COLD_PIECE)]
        pieces = pieces + [hot_tiles[k : k + HOT_PIECE] for k in range(0, 4, HOT_PIECE)]
        for n, piece in enumerate(pieces):
            slot = first_slot[piece[0][0]] + piece[0][1] * P
            entries = offs_t[:, slot // 16 : (slot + len(piece) * P) // 16]
            gw = sbuf([P, len(piece) * P], U32, f"gw{n}")
            gs = sbuf([P, len(piece) * P], U8, f"gs{n}")
            nc.vector.tensor_copy(gw[:], xw[:].bitcast(U32).indirect(entries))
            nc.vector.tensor_copy(gs[:], xs[:].indirect(entries))
            for k, tile in enumerate(piece):
                tokens[tile] = (gw[:, k * P : (k + 1) * P].bitcast(FP8X4), gs[:, k * P : (k + 1) * P])

        by_t = {}
        hot_plane = sbuf([P, H], U8, "hot_plane")

        def permute(which, f):
            tile = sbuf([P, H], I32, f"w{which}h{f}_by_t")
            nc.gpsimd.tensor_copy(
                tile[:].rearrange("p (t c i) -> p c t i", t=4, i=4),
                raw[which, f][:].bitcast(I32).rearrange("p (c i t) -> p c t i", t=4, i=4),
            )
            by_t[which, f] = tile

        def uqd(ap):
            return ap.rearrange("s (u q d) -> s u q d", u=2, d=2)

        def first_layer(bank, tile, which):
            words, scales = tokens[tile]
            g, f = tile[0], tile[1] // 2
            if g == "h":
                row = 4 * f + (8 if which == 3 else 0)
                for t in range(4):
                    cols = slice(t * P, (t + 1) * P)
                    nc.tensor.matmul_mx(out=bank[:, cols], lhsT=by_t[which, f][:, cols].bitcast(FP8X4), lhsT_scale=hot_plane[row:P, cols],
                                        rhs=words, rhs_scale=scales, start=True, stop=True)
                return bank[:].rearrange("q (t s) -> q s t", t=4)
            w = (w1c if which == 1 else w3c)[pair_of[g]][:, f, :].bitcast(FP4X4)
            plane = (s1c if which == 1 else s3c)[:, 2 * pair_of[g] + f, :]
            nc.tensor.matmul_mx(out=bank[:], lhsT=words, lhsT_scale=scales, rhs=w, rhs_scale=plane, start=True, stop=True)
            return bank[:].rearrange("s (q u d) -> s u q d", u=2, d=2)

        def like_sums(ap, tile):
            return ap.rearrange("q (s t) -> q s t", t=4) if tile[0] == "h" else uqd(ap)

        sigs, plains, a3, hidden = {}, {}, {}, {}
        ready = {g: sbuf([P, 4 * H], BF16, f"ready_{g}") for g in "abch"}

        def sigmoid(tile, bank):
            a1 = first_layer(bank, tile, 1)
            sigs[tile] = sbuf([P, H], F32, f"sig_{tile[0]}{tile[1]}")
            nc.scalar.activation(like_sums(sigs[tile][:], tile), a1, SIGMOID)

        def lend(tile, bank):
            sums = first_layer(bank, tile, 3)
            plains[tile] = sbuf([P, H], F32, f"plain{tile[1]}")
            nc.scalar.copy(uqd(plains[tile][:]), sums)

        def lent_product(tile):
            hidden[tile] = sbuf([P, H], BF16, f"hb_{tile[0]}{tile[1]}")
            nc.gpsimd.tensor_tensor(hidden[tile][:], plains[tile][:], sigs[tile][:], MULT)

        def other_half(tile):
            a3[tile] = first_layer(high[tile[1]], tile, 3)

        def product(tile):
            if tile[0] == "h":
                hb = ready["h"][:, tile[1] * H : (tile[1] + 1) * H]
            else:
                hidden[tile] = sbuf([P, H], BF16, f"hb_{tile[0]}{tile[1]}")
                hb = hidden[tile][:]
            nc.vector.tensor_tensor(like_sums(hb, tile), a3[tile], like_sums(sigs[tile][:], tile), MULT)

        def turn(g, f, bank):
            across = bank[:].rearrange("q (j u s) -> q j u s", j=2, u=2)
            for j in (1, 0):
                pairs = hidden[g, 2 * f + j][:].bitcast(F32)
                for u in range(2):
                    nc.tensor.transpose(across[:, j, u, :], pairs[:, u * P : (u + 1) * P], ident[:])
            dst = ready[g][:, 2 * f * H : (2 * f + 2) * H].bitcast(F32).rearrange("q (j s u) -> q j s u", j=2, u=2)
            nc.scalar.copy(dst, across.rearrange("q j u s -> q j s u"))

        permute(1, 0)
        sigmoid(("a", 0), low[0])
        sigmoid(("a", 1), low[1])
        lend(("a", 0), low[2])
        lend(("a", 1), low[3])
        sigmoid(("a", 2), low[2])
        sigmoid(("a", 3), low[3])
        lend(("a", 2), low[0])
        lend(("a", 3), low[1])
        for k in range(4):
            lent_product(("a", k))
        nc.gpsimd.tensor_copy(hot_plane[:].rearrange("p (t q) -> p t q", t=4), hot_rows[:, 0, :].rearrange("p (q t) -> p t q", t=4))
        permute(3, 0)
        permute(1, 1)
        permute(3, 1)
        for k in range(4):
            sigmoid(("b", k), low[(k + 2) % 4])
        for k in range(4):
            other_half(("b", k))
            product(("b", k))
        for k in range(4):
            sigmoid(("c", k), low[(k + 2) % 4])
        turn("a", 0, low[2])
        turn("a", 1, low[3])
        for k in range(4):
            other_half(("c", k))
            product(("c", k))
        sigmoid(("h", 0), low[0])
        sigmoid(("h", 1), low[1])
        other_half(("h", 0))
        sigmoid(("h", 2), low[2])
        other_half(("h", 1))
        sigmoid(("h", 3), low[3])
        other_half(("h", 2))
        other_half(("h", 3))
        for k in range(4):
            product(("h", k))
        turn("b", 0, low[0])
        turn("b", 1, low[1])
        turn("c", 0, low[2])
        turn("c", 1, low[3])

        codes = {}

        def quantise(g, experts, name):
            first, n = experts[0], len(experts)
            hq = sbuf([P, n * C], U32, name)
            hs = sbuf([P, n * C], U8, f"hs_{g}{first}")
            nc.vector.quantize_mx(out=hq[:].bitcast(FP8X4), scales=hs[:], in_=ready[g][:, 2 * first * H : 2 * (first + n) * H])
            for f in experts:
                cols = slice((f - first) * C, (f - first + 1) * C)
                codes[g, f] = (hq[:, cols].bitcast(FP8X4), hs[:, cols])

        y = [sbuf([P, S], F32, f"y{b}") for b in range(2)]

        def second_layer(bank, b, g, experts, copy):
            for k, f in enumerate(experts):
                if g == "h":
                    w, plane = w2h[:, f, 4 * P * b : 4 * P * (b + 1)].bitcast(FP8X4), s2h[:, f, P * b : P * (b + 1)]
                else:
                    w = w2c[pair_of[g]][:, f, 2 * P * b : 2 * P * (b + 1)].bitcast(FP4X4)
                    plane = s2c[:, 2 * pair_of[g] + f, P * b : P * (b + 1)]
                hq, hs = codes[g, f]
                nc.tensor.matmul_mx(out=bank[:, k * C : (k + 1) * C], lhsT=w, lhsT_scale=plane, rhs=hq, rhs_scale=hs, start=True, stop=True)
            slot = first_slot[g] + experts[0] * C
            copy(y[b][:, slot : slot + len(experts) * C], bank[:, 0 : len(experts) * C])

        quantise("a", [0, 1], "sig_h2")
        quantise("h", [0, 1], "hq_h")
        quantise("b", [0, 1], "hq_b")
        quantise("c", [0], "hq_c0")
        quantise("c", [1], "hq_c1")
        second_layer(high[0], 0, "a", [0, 1], nc.scalar.copy)
        second_layer(high[1], 0, "h", [0, 1], nc.scalar.copy)
        second_layer(high[2], 0, "b", [0, 1], nc.vector.tensor_copy)
        second_layer(high[3], 0, "c", [0], nc.scalar.copy)
        second_layer(low[0], 0, "c", [1], nc.scalar.copy)
        plain = {}

        def scalar_gather(b, tile):
            plain[b] = tile
            nc.scalar.activation(plain[b][:], y[b][:].indirect(pos_t[3][:]), COPY)

        scalar_gather(0, sbuf([P, T], F32, "plain_pick"))
        for bank, g in zip((high[2], high[3], low[0], high[2]), "ahbc"):
            second_layer(bank, 1, g, [0, 1], nc.scalar.copy)

        first_half, second_half, whole = slice(0, HALF), slice(HALF, T), slice(0, T)

        def chunk(c):
            return slice(c * P, (c + 1) * P)

        def turn_add(dst, src, start, stop):
            nc.tensor.matmul(dst, src, ident[:], start=start, stop=stop, is_transpose=True)

        def pick(dst, b, r, cols):
            entries = pos_t[r][:, cols.start // 16 : cols.stop // 16]
            nc.vector.tensor_tensor(dst, y[b][:].indirect(entries), gate_t[:, r, cols], MULT)

        def turn_chunks(bank, src, n, start, stop):
            for c in range(n):
                turn_add(bank[:, chunk(c)], src[:, chunk(c)], start and c == 0, stop and c == n - 1)

        def scalar_list(b, bank):
            for c in range(CHUNKS):
                nc.tensor.transpose(bank[:, chunk(c)], plain[b][:, chunk(c)], ident[:])

        def scaled_back(b, c, bank, dst, start, stop):
            scaled = sbuf([P, P], F32, f"scaled{b}{c}")
            nc.scalar.activation(scaled[:], bank[:, chunk(c)], COPY, scale=gate_col[:, c : c + 1])
            turn_add(dst, scaled[:], start, stop)

        def summed_back(name, bank, n, dst, start, stop):
            summed = sbuf([P, n * P], F32, name)
            nc.scalar.copy(summed[:], bank[:, 0 : n * P])
            turn_chunks(dst, summed, n, start, stop)

        for r in range(2):
            picked = sbuf([P, T], F32, f"picked0{r}")
            pick(picked[:], 0, r, whole)
            for bank, cols in ((low[1], first_half), (low[3], second_half)):
                turn_chunks(bank, picked[:, cols], 2, r == 0, r == 1)
        scalar_list(0, low[2])
        spent = sbuf([P, T], F32, "summed0")
        for bank, cols in ((low[1], first_half), (low[3], second_half)):
            nc.scalar.copy(spent[:, cols], bank[:, 0:HALF])
        turn_chunks(high[0], spent, CHUNKS, True, False)
        for c in range(CHUNKS):
            scaled_back(0, c, low[2], high[0][:, chunk(c)], False, c == CHUNKS - 1)
        shared = sbuf([P, 3 * HALF], F32, "shared")
        third0 = shared[:, P : P + T]
        pick(third0, 0, 2, whole)

        parts = (slice(0, HALF), slice(HALF, HALF + P), slice(HALF + P, T))
        sums, backs = (low[2], low[1], low[3]), (high[1], high[3], low[0])

        def width(cols):
            return (cols.stop - cols.start) // P

        scalar_gather(1, spent)
        picked = sbuf([P, T], F32, "picked10")
        pick(picked[:], 1, 0, whole)
        for bank, cols in zip(sums, parts):
            turn_chunks(bank, picked[:, cols], width(cols), True, False)
        picked = sbuf([P, HALF], F32, "picked11")
        pick(picked[:], 1, 1, first_half)
        turn_chunks(sums[0], picked, 2, False, True)
        res0 = sbuf([P, T], F32, "res0")
        for cols in (first_half, second_half):
            nc.vector.tensor_tensor(res0[:, cols], high[0][:, cols], third0[:, cols], ADD)
        nc.sync.dma_start(out=out[0:P, :], in_=res0[:])
        scalar_list(1, high[2])
        pick(shared[:, 0:HALF], 1, 1, second_half)
        for c in range(2):
            turn_chunks(sums[1 + c], shared[:, chunk(c)], 1, False, True)
        summed_back("summed10", sums[0], 2, backs[0], True, False)
        for c in range(2):
            scaled_back(1, c, high[2], backs[0][:, chunk(c)], False, c == 1)
        for c in range(2):
            scaled_back(1, 2 + c, high[2], backs[1 + c][:, chunk(0)], True, False)
        for c in range(2):
            summed_back(f"summed1{1 + c}", sums[1 + c], 1, backs[1 + c], False, True)
        third1 = shared[:, HALF : HALF + T]
        for cols in (first_half, second_half):
            pick(third1[:, cols], 1, 2, cols)
        for k, cols in enumerate(parts):
            res1 = sbuf([P, width(cols) * P], F32, f"res1{k}")
            nc.vector.tensor_tensor(res1[:], backs[k][:, 0 : width(cols) * P], third1[:, cols], ADD)
            nc.sync.dma_start(out=out[P : 2 * P, cols], in_=res1[:])
